import numpy as np, ml_dtypes
CORES = [2,6,10,14,18,22,26,30]
N = 8
BF = ml_dtypes.bfloat16
def gentries(a):
    return np.ascontiguousarray(a.reshape(8, 16, -1).transpose(0, 2, 1)).reshape(8, -1)
def gtable(e):
    e = np.asarray(e); return np.ascontiguousarray(e.reshape(8, -1, 16).transpose(0, 2, 1)).reshape(128, -1).astype(np.int32)
V, G, B, L, RO = 2048, 128, 3, 128, 2
W = V + B * G
def numbers(rng, ghost):
    s = (N, 8, V, 16)
    return np.where(rng.random(s) < ghost, rng.integers(V, W, s), rng.integers(0, V, s))
def image(t, nb):
    tw = np.concatenate([t, np.broadcast_to(np.arange(V, W), (N, 8, W - V))], axis=2)
    e = np.take_along_axis(tw, nb.reshape(N, 8, -1), 2).reshape(nb.shape)
    return np.take_along_axis(e, np.argsort(t, axis=-1)[..., None], 2)
def parts(rng, z, wild, mix):
    t = np.argsort(rng.random((N, 8, V)), axis=-1); nb = numbers(rng, 0.125)
    nz = np.where(rng.random(nb.shape) < wild, numbers(rng, 0.125), image(t, nb))
    x = np.clip(np.take_along_axis(z, t[:, :, None, :], 3) + rng.integers(-2, 3, z.shape), 0, 255)
    x = np.where(rng.random(z.shape) < 0.1, rng.integers(0, 256, z.shape), x)
    o = np.argsort(rng.random((N, 8, V)), axis=-1); m = t.copy()
    for r in range(N):
        for g in range(8):
            j = o[r, g, :int(V * mix[r, g])]; m[r, g, j] = t[r, g, np.roll(j, 1)]
    bx = np.ascontiguousarray(np.argsort(rng.random((N, 8, V)), axis=-1)[..., :G]); bz = np.take_along_axis(t, bx, 2)
    return {"x": x, "z": z, "nb": nb, "nz": nz, "m": m, "bx": bx, "bz": bz}
def pack(d):
    return {"x": np.ascontiguousarray(d["x"].reshape(N, 128, V)).astype(np.float32).astype(BF), "z": np.ascontiguousarray(d["z"].reshape(N, 128, V)).astype(np.float32).astype(BF),
            "nb": np.stack([gtable(a.reshape(8, -1)) for a in d["nb"]]), "nz": np.stack([gtable(a.reshape(8, -1)) for a in d["nz"]]),
            "m": d["m"].astype(np.int32), "im": np.argsort(d["m"], axis=-1).astype(np.int32),
            "bx": np.stack([gtable(a) for a in d["bx"]]), "bz": np.stack([gtable(a) for a in d["bz"]])}
def setup_inputs(rng):
    size = rng.permuted(np.tile(np.array([1, 1, 3, 3, 15, 63, 255, 255]), (N, 1)), axis=1)[:, :, None, None]
    z = rng.integers(0, size + 1, (N, 8, 16, V))
    wild = rng.choice(np.array([0.05, 0.2, 0.5, 1.0]), (N, 8, 1, 1)); mix = rng.choice(np.array([0.1, 0.3, 0.6, 1.0]), (N, 8))
    h = int(rng.integers(0, 8)); wild[:, h] = 0.0; mix[:, h] = 0.05
    return pack(parts(rng, z, wild, mix))
def setup_inputs_ties(rng):
    z = rng.integers(0, 2, (N, 8, 16, V)) * (rng.random((N, 8, 1, V)) < 0.5); z[:, 1, 1:] = 0
    d = parts(rng, z, rng.choice(np.array([0.2, 1.0]), (N, 8, 1, 1)), np.full((N, 8), 0.8))
    u = (np.arange(L) * (V // L))[1::2]
    for r in range(N):
        for g in (0, 2, 4, 6):
            s0 = np.flatnonzero(np.all(z[r, g] == 0, axis=0)); im = np.argsort(d["m"][r, g])
            d["nb"][r, g, u] = im[rng.choice(s0, (len(u), 16))]; d["nz"][r, g, d["m"][r, g, u]] = rng.choice(s0, (len(u), 16))
    d["nb"][:, 5] = rng.integers(0, V, (N, 1, 16))
    return pack(d)
def setup_inputs_crowd(rng):
    z = rng.integers(0, rng.choice(np.array([3, 15, 255]), (N, 8, 1, 1)) + 1, (N, 8, 16, V))
    d = parts(rng, z, np.ones((N, 8, 1, 1)), np.ones((N, 8)))
    for r in range(N):
        for g in range(8):
            n = (24, 160)[g % 2]
            s = np.concatenate([np.array([0, V - 1]), 1 + rng.permutation(V - 2)[:n - 2]]); e = np.concatenate([np.array([0, V - 1]), 1 + rng.permutation(V - 2)[:n - 2]])
            if g < 4: e = d["m"][r, g, s]
            ends = np.array([V, W - 1])
            d["nb"][r, g] = np.where(rng.random((V, 16)) < 0.05, rng.choice(ends, (V, 16)), rng.choice(s, (V, 16)))
            d["nz"][r, g] = np.where(rng.random((V, 16)) < 0.05, rng.choice(ends, (V, 16)), rng.choice(e, (V, 16)))
            d["bx"][r, g] = rng.choice(s, G); d["bz"][r, g] = rng.choice(e, G)
    return pack(d)
def setup_inputs_border(rng):
    z = rng.integers(0, rng.choice(np.array([3, 15, 255]), (N, 8, 1, 1)) + 1, (N, 8, 16, V))
    d = parts(rng, z, np.ones((N, 8, 1, 1)), np.ones((N, 8)))
    for r in range(N):
        for g in range(8):
            s = rng.permutation(V)[:160]; e = d["m"][r, g, s]
            d["nb"][r, g] = np.where(rng.random((V, 16)) < 0.3, rng.integers(V, W, (V, 16)), rng.choice(s, (V, 16)))
            d["nz"][r, g] = np.where(rng.random((V, 16)) < 0.3, rng.integers(V, W, (V, 16)), rng.choice(e, (V, 16)))
            d["bx"][r, g] = rng.choice(s, G); d["bz"][r, g] = rng.choice(e, G)
    d["bx"][:, :, 0] = 0; d["bx"][:, :, G - 1] = V - 1; d["bz"][:, :, 0] = V - 1; d["bz"][:, :, G - 1] = 0
    q = rng.permutation(8); d["nb"][:, q[0]] = rng.integers(V, W, (N, V, 16)); d["nz"][:, q[1]] = rng.integers(V, W, (N, V, 16))
    d["nb"][:, :, 0, :2] = np.array([V, W - 1])
    return pack(d)
def agree(d, r, g):
    t = np.concatenate([d["m"][r, g], np.arange(V, W)]); d["nz"][r, g, t[:V]] = t[d["nb"][r, g]]
def early(rng, d, r, g, n):
    st = np.arange(L) * (V // L); o = rng.permutation(np.setdiff1d(np.arange(V), np.concatenate([st, d["bx"][r, g]])))
    p = o[:2 * n]; a = d["nb"][r, g][st]; a[np.isin(a, p)] = o[2 * n]
    a[rng.permutation(L)[:n], rng.integers(0, 16, n)] = p[:n]; d["nb"][r, g, st] = a
    agree(d, r, g); t = d["m"][r, g].copy(); d["m"][r, g, p] = t[np.roll(p, n)]
def late(rng, d, r, g):
    st = np.arange(L) * (V // L); o = rng.permutation(np.setdiff1d(np.arange(V), np.concatenate([st, d["bx"][r, g], np.array([819, V - 1])])))
    p = o[:6].copy(); s = p[:3]; f = int(o[6]); b = o[7:7 + L].copy(); c = o[7 + L:7 + 2 * L].copy(); rest = o[7 + 2 * L:]
    j = 1 + rng.permutation(L - 1)[:3]; b[j[0]] = 819
    nb = d["nb"][r, g]; nb[np.isin(nb, p)] = f
    nb[p] = rng.choice(rest, (6, 16)); nb[s, rng.integers(0, 16, 3)] = f
    nb[st, 0] = b; nb[b, 0] = c; nb[819, 0] = rng.integers(V, W)
    nb[np.array([b[j[1]], c[j[2]], V - 1]), rng.integers(1, 16, 3)] = s
    agree(d, r, g); t = d["m"][r, g].copy(); z = d["z"][r, g]
    z[:] = rng.integers(0, 200, (16, 1)); z[:, t[s]] += rng.integers(1, 5, (16, 3)); z[int(rng.integers(0, 16)), t[f]] += rng.integers(1, 16)
    d["m"][r, g, p] = t[np.roll(p, 3)]
def setup_inputs_still(rng):
    z = rng.integers(0, 256, (N, 8, 16, V)); d = parts(rng, z, np.zeros((N, 8, 1, 1)), np.zeros((N, 8)))
    q, q2, q3 = [int(i) for i in rng.permutation(N)[:3]]; h, h2 = [int(i) for i in rng.permutation(8)[:2]]; st = np.arange(L) * (V // L)
    room = [L] + [(287 - L + i) // 5 for i in range(5)]
    for r in range(N):
        for g in range(8):
            if r == q or g == h: continue
            if r in (q2, q3):
                if g == h2: late(rng, d, r, g)
                elif r == q3: early(rng, d, r, g, room.pop())
                continue
            c = np.unique(d["nb"][r, g, st]); c = np.setdiff1d(c[c < V], np.concatenate([st, d["bx"][r, g]]))
            p = rng.permutation(c)[:2 * int(rng.integers(1, 4))]
            d["m"][r, g, p] = d["m"][r, g, p.reshape(-1, 2)[:, ::-1].reshape(-1)]
    return pack(d)
def setup_inputs_spread(rng):
    z = (np.exp2(8 * rng.random((N, 8, 1, V))) * rng.random((N, 8, 16, V)) * (rng.random((N, 8, 1, V)) > 0.0625)).astype(np.int64)
    wild = rng.choice(np.array([0.05, 0.3, 1.0]), (N, 8, 1, 1)); mix = rng.choice(np.array([0.2, 0.5, 1.0]), (N, 8))
    for h in rng.permutation(8)[:2]:
        u = rng.integers(0, 4, (N, 16, V)); z[:, h] = np.where(rng.random((N, 1, V)) < 0.5, u, 255 - u); wild[:, h] = 1.0; mix[:, h] = 1.0
    return pack(parts(rng, z, wild, mix))
def check_inputs(d):
    bad = []
    for k in ("x", "z"):
        a = np.asarray(d[k]).astype(np.float32)
        if not np.all((a >= 0) & (a <= 255) & (a == np.floor(a))): bad.append("whole numbers 0 to 255 in " + k)
    for k, hi in (("nb", W - 1), ("nz", W - 1), ("m", V - 1), ("im", V - 1), ("bx", V - 1), ("bz", V - 1)):
        if np.min(d[k]) < 0 or np.max(d[k]) > hi: bad.append("range of " + k)
    if not np.all(np.sort(d["m"], axis=-1) == np.arange(V)): bad.append("m is a bijection")
    elif not np.all(np.argsort(d["m"], axis=-1) == d["im"]): bad.append("im is the inverse of m")
    return bad
def reference(x, z, nb, nz, m, im, bx, bz):
    X = x.astype(np.float32).astype(np.int64).reshape(N, 8, 16, V); Z = z.astype(np.float32).astype(np.int64).reshape(N, 8, 16, V)
    nv = np.stack([gentries(a) for a in nb]).astype(np.int64).reshape(N, 8, V, 16); ns = np.stack([gentries(a) for a in nz]).astype(np.int64).reshape(N, 8, V, 16)
    M = m.astype(np.int64); I = im.astype(np.int64)
    b1 = np.stack([gentries(a) for a in bx]).astype(np.int64); b2 = np.stack([gentries(a) for a in bz]).astype(np.int64)
    lane = np.arange(L); v = np.tile(lane * (V // L), (N, 8, 1)); last = np.zeros(N, np.int64)
    for rnd in range(RO):
        Y = np.take_along_axis(Z, M[:, :, None, :], 3)
        ey = np.take_along_axis(Y, b1[:, :, None, :], 3); ez = np.take_along_axis(Z, b2[:, :, None, :], 3)
        YW = np.concatenate([Y] + [np.roll(ey, -d, axis=0) for d in range(1, B + 1)], axis=3)
        ZW = np.concatenate([Z] + [np.roll(ez, -d, axis=0) for d in range(1, B + 1)], axis=3)
        th = last & 31; last = np.zeros(N, np.int64)
        for r in range(N):
            for g in range(8):
                Yg, Zg, n1, n2, at = YW[r, g], ZW[r, g], nv[r, g], ns[r, g], v[r, g].copy()
                na = n1[at]; nq = n2[M[r, g, at]]
                D = np.add.reduce(np.abs(Yg[:, na] - Zg[:, nq]), axis=0); k = np.argmax(D, axis=1)
                a = na[lane, k]; q = nq[lane, k]; live = (D[lane, k] > 0) & (a < V) & (q < V)
                ac = np.minimum(a, V - 1); qc = np.minimum(q, V - 1); w = I[r, g, qc]; p = M[r, g, ac]
                Aa = Yg[:, n1[ac]]; Aw = Yg[:, n1[w]]; Ba = Zg[:, n2[p]]; Bw = Zg[:, n2[qc]]
                gain = np.add.reduce(np.abs(Aa - Ba) + np.abs(Aw - Bw) - np.abs(Aa - Bw) - np.abs(Aw - Ba), axis=(0, 2))
                prop = live & (gain > th[r])
                first = np.full(V, L); np.minimum.at(first, ac[prop], lane[prop]); np.minimum.at(first, w[prop], lane[prop])
                com = prop & (first[ac] >= lane) & (first[w] >= lane)
                last[r] += np.count_nonzero(com)
                v[r, g] = np.where(com, a, np.where(q < V, w, (5 * at + 1) & (V - 1)))
                a, w, p, q = a[com], w[com], p[com], q[com]
                M[r, g, a] = q; M[r, g, w] = p; I[r, g, q] = a; I[r, g, p] = w
                for vert, site in ((a, q), (w, p)):
                    old = Z[r, g][:, site]; Z[r, g][:, site] = old + np.clip(X[r, g][:, vert] - old, -1, 1)
    return {"mo": M.astype(np.float32), "zo": Z.reshape(N, 128, V).astype(np.float32).astype(BF)}

@@ -1,0 +1,444 @@
+from concourse.bass import DstId, RemoteDMATransfer
+from concourse.mybir import AluOpType as A, AxisListType, ActivationFunctionType as F
+
+N, NV, NW, DUMP = 8, 2048, 2432, 2944
+ROUNDS = 2
+
+
+def _buffers():
+    s = {}
+    def add(names, cols, ty):
+        for n in names.split():
+            s[n] = ("sbuf", [128, cols], ty)
+    add("Z Y", DUMP, "bfloat16"); add("X", NW, "bfloat16")
+    add("mrep imrep", DUMP, "float32"); add("nbt nzt", NW, "int32")
+    add("mS mc imc", 128, "int32"); add("bxi bzi bci", 8, "int32"); add("l15i", 16, "int32"); add("ip32 pmi pgi tha thb", 1, "int32")
+    add("ipf pm pg dc1 dc2 pm16 thh cn", 1, "float32")
+    add("rowI rowG If mSf KEY MX OH ones cK", 128, "float32"); add("rowT diag segm PAQ SC E WPm WPs E2", 256, "float32")
+    add("rowc", 40, "float32"); add("RD", 40, "float16"); add("rowGG", 1024, "float32"); add("BOg", 1024, "float16")
+    add("Ih BOh mch imch EC", 128, "float16"); add("tri RH", 256, "float16"); add("LT RR", 2048, "float16")
+    add("Ib prop8 bi16 bip bim", 128, "bfloat16")
+    add("ind ind16 vl nv5 own ea WS bad thr thr2 nc tv", 8, "float32"); add("bad2", 16, "float32"); add("nvi", 8, "int32"); add("LST", 32, "float32")
+    add("ML nal nql LA LBp LAp LB", 128, "uint16"); add("BXL BZL bc VU MVL", 8, "uint16"); add("L15", 16, "uint16"); add("UL OF", 32, "uint16")
+    add("naf nqf", 128, "float32"); add("ZQ DF AD Bp Bb Ap M1 M2 M3 M4", 2048, "bfloat16"); add("EQ", 4096, "bfloat16")
+    add("RP", 512, "float32"); add("XD CL ZQP sb0 sb1", 256, "bfloat16")
+    for n in ("st0", "st1"):
+        s[n] = ("sbuf", [128, 3, 256], "bfloat16")
+    for n in range(8):
+        s["k%d" % n] = ("psum", [128, 512], "float32")
+    return s
+
+
+SCRATCH = _buffers()
+SEMAPHORES = ["qV", "qS", "qP", "qG", "sent", "arr0", "arr1", "dms", "dz", "dmc", "dim", "dbx", "dbz", "dnz", "dnb", "dx", "dzo", "dmo"]
+
+
+def rank_program(g, core, T, topo):
+    rank = T.rank_of(core)
+    if rank is None:
+        return
+    eng = {"V": g.vector, "S": g.scalar, "P": g.tensor, "G": g, "Y": g.sync}
+    due = {n: 0 for n in SEMAPHORES}
+    know = {q: {} for q in eng}
+    acc = {}
+
+    def order(q, reads, writes):
+        toks = {}
+        for w, specs in ((False, reads), (True, writes)):
+            for (n, lo, hi) in specs:
+                ps = SCRATCH[n][0] == "psum"
+                for (l2, h2, w2, q2, sem, val, kn) in acc.get(n, []):
+                    if ps:
+                        if q2 == q and (q == "P" or not (w or w2)): continue
+                    elif not (w or w2) or lo >= h2 or l2 >= hi:
+                        continue
+                    if toks.get(sem, (0,))[0] < val: toks[sem] = (val, kn)
+        for sem, (val, kn) in sorted(toks.items(), key=lambda t: -sum(t[1][1].values())):
+            if know[q].get(sem, 0) < val:
+                eng[q].wait_ge(T.sem[sem], val)
+                for s2, v2 in list(kn.items()) + [(sem, val)]:
+                    if know[q].get(s2, 0) < v2: know[q][s2] = v2
+
+    def note(q, reads, writes, sem, val, kn):
+        for w, specs in ((False, reads), (True, writes)):
+            for (n, lo, hi) in specs:
+                a = acc.setdefault(n, [])
+                if SCRATCH[n][0] == "psum":
+                    a[:] = [e for e in a if not (e[3] == q and e[2] <= w)]
+                else:
+                    a[:] = [e for e in a if not (lo <= e[0] and e[1] <= hi and (w or (e[3] == q and e[4] == sem and not e[2])))]
+                a.append((lo, hi, w, q, sem, val, kn))
+
+    def op(q, fn, reads, writes):
+        order(q, reads, writes)
+        fn().then_inc(T.sem["q" + q], 1)
+        due["q" + q] += 1
+        note(q, reads, writes, "q" + q, due["q" + q], dict(know[q]))
+
+    def dma(q, sem, out, in_, total=16):
+        order(q, in_[1], out[1])
+        eng[q].dma_start(out[0], in_[0]).then_inc(T.sem[sem], 16)
+        due[sem] += 16
+        note(q, in_[1], out[1], sem, total, dict(know[q]))
+
+    def b(n, lo=0, hi=None, step=1):
+        hi = SCRATCH[n][1][1] if hi is None else hi
+        return (T[n][:, lo:hi:step] if step != 1 else T[n][:, lo:hi], [(n, lo, hi)])
+
+    def ext(ap):
+        return (ap, [])
+
+    def ind(win, off):
+        return (win[0].indirect(off[0]), win[1] + off[1])
+
+    def num(s):
+        return (s[0], s[1]) if isinstance(s, tuple) else (s, [])
+
+    def tt(out, in0, in1, o):
+        op("V", lambda: g.vector.tensor_tensor(out[0], in0[0], in1[0], o), in0[1] + in1[1] + out[1][1:], out[1][:1])
+
+    def ts(out, in0, s1, s2, o0, o1=None):
+        a1, r1 = num(s1)
+        a2, r2 = num(s2)
+        if o1 is None:
+            op("V", lambda: g.vector.tensor_scalar(out[0], in0[0], a1, None, o0), in0[1] + r1, out[1])
+        else:
+            op("V", lambda: g.vector.tensor_scalar(out[0], in0[0], a1, a2, o0, o1), in0[1] + r1 + r2, out[1])
+
+    def cp(out, in_):
+        op("V", lambda: g.vector.tensor_copy(out[0], in_[0]), in_[1] + out[1][1:], out[1][:1])
+
+    def fill(out, c):
+        op("V", lambda: g.vector.memset(out[0], c), [], out[1])
+
+    def scan(out, d0, d1, o0, o1):
+        op("V", lambda: g.vector.tensor_tensor_scan(out[0], d0[0], d1[0], 0.0, o0, o1), d0[1] + d1[1], out[1])
+
+    def act(out, in_, f=F.Copy, scale=1.0):
+        op("S", lambda: g.scalar.activation(out[0], in_[0], f, scale=scale), in_[1], out[1])
+
+    def mm(out, l, r, start=True, stop=True):
+        op("P", lambda: g.tensor.matmul(out[0], l[0], r[0], start, stop), l[1] + r[1], out[1])
+
+    def iota(out, pat, base, cm, f=True):
+        if f:
+            op("G", lambda: g.iota(out[0], pat, base, cm, allow_small_or_imprecise_dtypes=True), [], out[1])
+        else:
+            op("G", lambda: g.iota(out[0], pat, base, cm), [], out[1])
+
+    for k in range(8):
+        dma("SY"[k % 2], "dms", b("mS", 16 * k, 16 * k + 16), ext(T.m[k, :]), 128)
+    dma("S", "dmc", b("mc"), ext(T.m[:, :]))
+    dma("Y", "dbx", b("bxi"), ext(T.bx[:, :]))
+    dma("S", "dim", b("imc"), ext(T.im[:, :]))
+    dma("Y", "dbz", b("bzi"), ext(T.bz[:, :]))
+    dma("Y", "dz", b("Z", 0, NV), ext(T.z[:, :]))
+    dma("Y", "dnz", b("nzt", 0, NV), ext(T.nz[:, :]))
+    dma("Y", "dnb", b("nbt", 0, NV), ext(T.nb[:, :]))
+    dma("Y", "dx", b("X", 0, NV), ext(T.x[:, :]))
+
+    iota(b("ip32"), [[0, 1]], 0, 1, False)
+    iota(b("ipf"), [[0, 1]], 0, 1)
+    iota(b("rowI"), [[1, 128]], 0, 0)
+    iota(b("rowG"), [[1, 8], [0, 16]], 0, 0)
+    iota(b("rowT"), [[0, 16], [1, 16]], 0, 0)
+    iota(b("rowc"), [[0, 5], [1, 8]], 0, 0)
+    iota(b("l15i"), [[16, 16]], 15, 0, False)
+    iota(b("bci"), [[1, 8]], 0, 0, False)
+    iota(b("vl"), [[256, 8]], 0, 0)
+    iota(b("rowGG"), [[1, 8], [0, 128]], 0, 0)
+    for n in ("mrep", "imrep", "nbt", "nzt", "X"):
+        iota(b(n, NV, NW), [[0, NW - NV]], 0, 0, n[0] != "n")
+    ts(b("If"), b("rowI"), b("ipf"), None, A.is_equal)
+    ts(b("pmi"), b("ip32"), 15, None, A.bitwise_and)
+    ts(b("pgi"), b("ip32"), 4, None, A.arith_shift_right)
+    cp(b("pm"), b("pmi"))
+    cp(b("pg"), b("pgi"))
+    ts(b("BOh"), b("rowG"), b("pg"), None, A.is_equal)
+    ts(b("diag"), b("rowT"), b("pm"), None, A.is_equal)
+    cp(b("mSf"), b("mS"))
+    mm(b("k0", 0, 128), b("mSf"), b("If"))
+    cp(b("ML"), b("k0", 0, 128))
+    cp(b("BXL"), b("bxi"))
+    cp(b("BZL"), b("bzi"))
+    for t in range(16):
+        ts(b("LT", 128 * t, 128 * t + 128), b("BOh"), b("diag", t, t + 1), None, A.mult)
+    cp(b("mch"), b("mc"))
+    cp(b("imch"), b("imc"))
+    for t in range(16):
+        mm(b("k%d" % (4 + t // 4), t % 4 * 128, t % 4 * 128 + 128), b("LT", 128 * t, 128 * t + 128), b("mch"))
+    for t in range(16):
+        mm(b("k%d" % (t // 4), t % 4 * 128, t % 4 * 128 + 128), b("LT", 128 * t, 128 * t + 128), b("imch"))
+    cp(b("Y", 0, 1024), ind(b("Z", 0, NV), b("ML", 0, 64)))
+    act(b("Y", 1024, 2048), ind(b("Z", 0, NV), b("ML", 64, 128)))
+
+    def engines_to(src, dst):
+        e = topo.engines(src, dst)
+        if topo.chip(src) != topo.chip(dst):
+            return e
+        far = [c for c in T.cores if topo.chip(c) != topo.chip(src) and topo.may_write(src, c)]
+        used = topo.engines(src, far[0])
+        return [k for k in e if k not in used]
+
+    def send(rd):
+        cp(b("sb%d" % rd, 0, 128), ind(b("Y", 0, NV), b("BXL")))
+        act(b("sb%d" % rd, 128, 256), ind(b("Z", 0, NV), b("BZL")))
+        groups = {}
+        for d in (1, 2, 3):
+            dst = T.cores[(rank - d) % N]
+            groups.setdefault(tuple(engines_to(core, dst)), []).append((d, dst))
+        order("G", b("sb%d" % rd)[1], [])
+        tr = []
+        for e, ds in groups.items():
+            ids = []
+            for d, dst in ds:
+                rid, pid, _ = topo.addr(dst)
+                ids.append(DstId(rid=rid, pnc=pid))
+            tr.append(RemoteDMATransfer(dst_ids=ids, dma_engine_mask=sum(1 << k for k in e), remote_sem=T.sem["arr%d" % rd],
+                                        srcs=[T["sb%d" % rd][:, :]], dsts=[T["st%d" % rd][:, d - 1, :] for d, _ in ds]))
+            due["sent"] += len(e)
+        g.remote_dma_fused(tr, local_sem=T.sem["sent"])
+        due["arr%d" % rd] = sum(len(engines_to(T.cores[(rank + d) % N], core)) for d in (1, 2, 3))
+        note("G", [], [("st%d" % rd, 0, 768)], "arr%d" % rd, due["arr%d" % rd], {})
+
+    send(0)
+    ts(b("ind"), b("rowc", 0, 8), b("pg"), None, A.is_equal)
+    for k in range(4):
+        act(b("mrep", 512 * k, 512 * k + 512), b("k%d" % (4 + k)))
+    for k in range(4):
+        cp(b("imrep", 512 * k, 512 * k + 512), b("k%d" % k))
+    ts(b("segm"), b("rowT"), 0.0, None, A.is_gt)
+    ts(b("cK"), b("rowT", 0, 128), -1.0, 15.0, A.mult, A.add)
+    act(b("bi16", 0, 8), b("ind"), F.Copy, 16.0)
+    act(b("bip", 0, 8), b("ind"))
+    act(b("bim", 0, 8), b("ind"), F.Copy, -1.0)
+    act(b("ind16"), b("ind"), F.Copy, 0.0625)
+    cp(b("L15"), b("l15i"))
+    cp(b("bc"), b("bci"))
+    act(b("Ih"), b("If"))
+    act(b("Ib"), b("If"))
+    ts(b("BOg"), b("rowGG"), b("pg"), 0.0625, A.is_equal, A.mult)
+    for k in (0, 128):
+        ts(b("tri", k, k + 128), b("rowI"), b("ipf"), 4096.0, A.is_le, A.mult)
+    ts(b("dc1"), b("ipf"), 2.0, float(NW), A.mult, A.add)
+    ts(b("dc2"), b("dc1"), 256.0, None, A.add)
+    for k in range(4):
+        ts(b("RD", 8 * k, 8 * k + 8), b("rowc", 8 * k, 8 * k + 8), b("pg"), b("dc%d" % (1 + k % 2)), A.is_equal, A.mult)
+    cp(b("RD", 32, 40), b("ind"))
+    ts(b("pm16"), b("pm"), 16.0, None, A.mult)
+    ts(b("vl"), b("vl"), b("pm16"), None, A.add)
+    fill(b("ones"), 1.0)
+    fill(b("thh"), 0.0)
+
+    def half(n, k):
+        return b(n, 128 * k, 128 * k + 128)
+
+    def ch(n, c):
+        return b(n, 512 * c, 512 * c + 512)
+
+    def lst(n, c):
+        return b(n, 32 * c, 32 * c + 32)
+
+    def every16(n, base=15, cnt=8):
+        return b(n, base, base + 16 * cnt - 15, 16)
+
+    Yw, Zw, Xw = b("Y", 0, NW), b("Z", 0, NW), b("X", 0, NW)
+    Mw, Iw, NBw, NZw = b("mrep", 0, NW), b("imrep", 0, NW), b("nbt"), b("nzt")
+
+    def names(rd):
+        if rd == 0:
+            tt(half("WPm", 0), b("mrep", 0, NV, 16), half("diag", 0), A.mult)
+            cp(b("nal"), b("nbt", 0, NV, 16))
+        else:
+            tt(half("WPm", 0), ind(Mw, b("VU")), half("diag", 0), A.mult)
+            cp(b("nal"), ind(NBw, b("VU")))
+        scan(half("WPs", 0), half("segm", 0), half("WPm", 0), A.mult, A.add)
+        cp(b("naf"), b("nal"))
+        cp(b("MVL"), every16("WPs"))
+        cp(b("nql"), ind(NZw, b("MVL")))
+        cp(b("nqf"), b("nql"))
+
+    names(0)
+    for rd in range(ROUNDS):
+        last = rd == ROUNDS - 1
+        cp((T["Y"][:, NV:NW], [("Y", NV, NW)]), (T["st%d" % rd][:, :, 0:128], [("st%d" % rd, 0, 768)]))
+        act((T["Z"][:, NV:NW], [("Z", NV, NW)]), (T["st%d" % rd][:, :, 128:256], [("st%d" % rd, 0, 768)]))
+        def dsum(c):
+            for k in range(16):
+                mm((T["k0"][32 * c:32 * c + 32, k:128:16], [("k0", 0, 128)]), b("AD", 512 * c + k, 512 * c + 512, 16), b("bi16", 0, 8))
+        act(ch("ZQ", 0), ind(Zw, lst("nql", 0)))
+        cp(ch("ZQ", 1), ind(Zw, lst("nql", 1)))
+        tt(ch("DF", 0), ind(Yw, lst("nal", 0)), ch("ZQ", 0), A.subtract)
+        act(ch("ZQ", 2), ind(Zw, lst("nql", 2)))
+        act(ch("AD", 0), ch("DF", 0), F.Abs)
+        dsum(0)
+        tt(ch("DF", 1), ind(Yw, lst("nal", 1)), ch("ZQ", 1), A.subtract)
+        act(ch("ZQ", 3), ind(Zw, lst("nql", 3)))
+        act(ch("AD", 1), ch("DF", 1), F.Abs)
+        mm(b("k1", 0, 128), b("naf"), b("If"))
+        mm(b("k1", 128, 256), b("nqf"), b("If"))
+        dsum(1)
+        for c in (2, 3):
+            tt(ch("DF", c), ind(Yw, lst("nal", c)), ch("ZQ", c), A.subtract)
+            act(ch("AD", c), ch("DF", c), F.Abs)
+            dsum(c)
+        tt(b("KEY"), b("k0", 0, 128), b("cK"), A.add)
+        scan(b("MX"), half("segm", 0), b("KEY"), A.mult, A.max)
+        tt(b("OH"), ind(b("MX"), b("L15", 0, 8)), b("KEY"), A.is_equal)
+        tt(half("PAQ", 0), b("OH"), b("k1", 0, 128), A.mult)
+        tt(half("PAQ", 1), b("OH"), b("k1", 128, 256), A.mult)
+        scan(b("SC"), b("segm"), b("PAQ"), A.mult, A.add)
+        tt(b("E"), ind(b("SC"), b("L15")), b("diag"), A.mult)
+        act(b("E2"), ind(b("SC"), b("L15")))
+        mm(b("k2", 8, 16), half("E", 1), b("ind"))
+        mm(b("k2", 0, 8), half("E", 0), b("ind"))
+        cp(b("UL", 16, 24), b("k2", 8, 16))
+        cp(b("UL", 0, 8), b("k2", 0, 8))
+        cp(b("LBp"), ind(NZw, b("UL", 16, 24)))
+        cp(b("LA"), ind(NBw, b("UL", 0, 8)))
+        tt(half("WPm", 0), ind(Iw, b("UL", 16, 24)), half("diag", 0), A.mult)
+        tt(half("WPm", 1), ind(Mw, b("UL", 0, 8)), half("diag", 1), A.mult)
+        scan(b("WPs"), b("segm"), b("WPm"), A.mult, A.add)
+        act(ch("Bp", 0), ind(Zw, lst("LBp", 0)))
+        cp(b("UL", 8, 16), every16("WPs"))
+        cp(b("UL", 24, 32), every16("WPs", 143))
+        act(b("LST", 0, 8), b("k2", 0, 8))
+        act(b("LST", 16, 24), b("k2", 8, 16))
+        for c in (1, 2, 3):
+            act(ch("Bp", c), ind(Zw, lst("LBp", c)))
+        mm(b("k3", 0, 128), half("E2", 0), b("If"))
+        mm(b("k3", 128, 256), half("E2", 1), b("If"))
+
+        def gsum(n, c, sgn, start, stop):
+            for k in range(16):
+                mm((T["k1"][32 * c:32 * c + 32, 0:8], [("k1", 0, 8)]), b(n, 512 * c + k, 512 * c + 512, 16), b(sgn, 0, 8), start and k == 0, stop and k == 15)
+
+        def gall(n, sgn, start, stop):
+            for k in range(16):
+                mm(b("k0", 0, 8), b(n, k, 2048, 16), b(sgn, 0, 8), start and k == 0, stop and k == 15)
+
+        def rows(h):
+            kb = "k%d" % (2 + h % 2)
+            for e in (0, 1):
+                gg = 2 * h + e
+                mm(b(kb, 256 * e, 256 * e + 256), b("BOg", 128 * gg, 128 * gg + 128), b("RH"), True, False)
+                mm(b(kb, 256 * e, 256 * e + 256), b("Ih"), b("tri"), False, True)
+            act(ch("RR", h), b(kb))
+
+        def compare(h):
+            for gg in (2 * h, 2 * h + 1):
+                for s in (0, 1):
+                    col = b("SC", 16 * gg + 15, 16 * gg + 16) if s == 0 else b("WS", gg, gg + 1)
+                    ts(b("EQ", (2 * gg + s) * 256, (2 * gg + s) * 256 + 256), b("RR", 256 * gg, 256 * gg + 256), col, None, A.is_equal)
+
+        def topb(c):
+            mm(b("k%d" % (4 + 2 * (c % 2))), b("Ib"), ch("Bp", c))
+
+        def tops(c):
+            mm(b("k%d" % (5 + 2 * (c % 2))), b("Ib"), ch("Bb", c))
+
+        topb(0)
+        topb(1)
+        for c in range(4):
+            tt(ch("M1", c), ind(Yw, lst("LA", c)), ch("Bp", c), A.max)
+            if c == 0:
+                cp(b("LB"), ind(NZw, b("UL", 24, 32)))
+            if c == 1:
+                cp(b("LAp"), ind(NBw, b("UL", 8, 16)))
+        act(ch("Bb", 0), ind(Zw, lst("LB", 0)))
+        act(ch("Bb", 1), ind(Zw, lst("LB", 1)))
+        act(half("RP", 1), ind(Iw, b("UL", 16, 24)))
+        act(half("RP", 0), b("k3", 0, 128))
+        act(b("RH"), b("RP", 0, 256))
+        mm(b("k2", 0, 8), half("RP", 1), b("ind16"))
+        act(ch("Bb", 2), ind(Zw, lst("LB", 2)))
+        act(b("WS"), b("k2", 0, 8))
+        act(half("RP", 2), b("k3", 128, 256))
+        act(ch("Bb", 3), ind(Zw, lst("LB", 3)))
+        act(half("RP", 3), ind(Mw, b("UL", 0, 8)))
+        act(b("LST", 8, 16), every16("WPs"))
+        act(b("LST", 24, 32), every16("WPs", 143))
+        act(b("ZQP"), ind(Zw, b("UL", 16, 32)))
+        for c in range(4):
+            tt(ch("M2", c), ind(Yw, lst("LA", c)), ch("Bb", c), A.max)
+        tops(0)
+        tops(1)
+        rows(0)
+        rows(1)
+        gall("M1", "bim", True, False)
+        act(ch("Ap", 0), ind(Yw, lst("LAp", 0)))
+        act(ch("Ap", 1), ind(Yw, lst("LAp", 1)))
+        rows(2)
+        rows(3)
+        gall("M2", "bip", False, True)
+        act(ch("Ap", 2), ind(Yw, lst("LAp", 2)))
+        act(ch("Ap", 3), ind(Yw, lst("LAp", 3)))
+        ts(b("bad"), every16("MX"), 16.0, None, A.is_lt)
+        ts(b("bad2"), every16("SC", 15, 16), float(NV), None, A.is_ge)
+        tt(b("bad"), b("bad"), b("bad2", 0, 8), A.add)
+        tt(b("bad"), b("bad"), b("bad2", 8, 16), A.add)
+        ts(b("thr"), b("bad"), 1.0e6, b("thh"), A.mult, A.add)
+        tt(b("XD"), ind(Xw, b("UL", 0, 16)), b("ZQP"), A.subtract)
+        compare(0)
+        compare(1)
+        ts(b("CL"), b("XD"), 1.0, -1.0, A.min, A.max)
+
+        def late(c):
+            tt(ch("M3", c), ch("Ap", c), b("k%d" % (4 + 2 * (c % 2))), A.max)
+            tt(ch("M4", c), ch("Ap", c), b("k%d" % (5 + 2 * (c % 2))), A.max)
+            if c < 2:
+                topb(c + 2)
+                tops(c + 2)
+            gsum("M3", c, "bip", True, False)
+            gsum("M4", c, "bim", False, True)
+
+        late(0)
+        compare(2)
+        late(1)
+        compare(3)
+        tt(b("thr2"), b("thr"), b("k0", 0, 8), A.subtract)
+        late(2)
+        late(3)
+        tt(b("prop8", 0, 8), b("k1", 0, 8), b("thr2"), A.is_gt)
+        for gg in range(8):
+            for i in range(4):
+                o = (2 * gg + i // 2) * 256 + i % 2 * 128
+                mm(b("k2", gg, gg + 1), b("EQ", o, o + 128), b("prop8", gg, gg + 1), i == 0, i == 3)
+        if not last:
+            ts(b("nvi"), b("vl"), 5.0, 1.0, A.mult, A.add)
+            ts(b("nvi"), b("nvi"), 2047, None, A.bitwise_and)
+            cp(b("nv5"), b("nvi"))
+            ts(b("own"), b("LST", 16, 24), float(NV), None, A.is_lt)
+            tt(b("ea"), b("LST", 8, 16), b("nv5"), A.subtract)
+            tt(b("ea"), b("ea"), b("own"), A.mult)
+            tt(b("ea"), b("ea"), b("nv5"), A.add)
+            tt(b("ea"), b("ea"), b("LST", 0, 8), A.subtract)
+        tt(b("nc"), b("k2", 0, 8), b("prop8", 0, 8), A.is_ge)
+        tt(b("EC"), ind(b("nc"), b("bc")), half("diag", 0), A.mult)
+        mm(b("k3", 0, 40), b("EC"), b("RD"))
+        tt(b("OF"), b("LST"), b("k3", 0, 32), A.max)
+
+        def scat(n, o):
+            return (T[n][:, 0:DUMP].indirect(T["OF"][:, o:o + 16]), [(n, 0, DUMP), ("OF", o, o + 16)])
+
+        tt(scat("Z", 16), b("CL"), b("ZQP"), A.add)
+        if last:
+            dma("Y", "dzo", ext(T.zo[:, :]), b("Z", 0, NV))
+            cp(scat("mrep", 0), b("RP", 256, 512))
+            dma("S", "dmo", ext(T.mo[:, :]), (T["mrep"][0:128:16, 0:NV], [("mrep", 0, NV)]))
+            break
+        tt(scat("Y", 0), b("CL"), b("ZQP"), A.add)
+        send(rd + 1)
+        tt(b("tv"), b("k3", 32, 40), b("ea"), A.mult)
+        tt(b("VU"), b("tv"), b("LST", 0, 8), A.add)
+        mm(b("k2", 0, 8), b("ones"), b("nc"))
+        cp(scat("mrep", 0), b("RP", 256, 512))
+        names(1)
+        op("V", lambda: g.vector.tensor_reduce(T["cn"][:, :], T["k2"][:, 0:8], AxisListType.X, A.add), [("k2", 0, 8)], [("cn", 0, 1)])
+        ts(b("tha"), b("cn"), -1.0, None, A.mult)
+        ts(b("thb"), b("tha"), 31, None, A.bitwise_and)
+        ts(b("thh"), b("thb"), 0.5, None, A.mult)
+        cp(scat("imrep", 16), b("RP", 0, 256))
+    for s in SEMAPHORES:
+        if know["G"].get(s, 0) < due[s] and due[s]:
+            g.wait_ge(T.sem[s], due[s])

@@ -1,8 +1,11 @@
+import math
 from concourse.bass import DstId, RemoteDMATransfer
 from concourse.mybir import AluOpType as A, AxisListType, ActivationFunctionType as F
 
 N, NV, NW, DUMP = 8, 2048, 2432, 2944
 ROUNDS = 2
+BIG = float(2 ** 20)
+RATIO = 3.5
 
 
 def _buffers():
@@ -12,16 +15,18 @@ def _buffers():
             s[n] = ("sbuf", [128, cols], ty)
     add("Z Y", DUMP, "bfloat16"); add("X", NW, "bfloat16")
     add("mrep imrep", DUMP, "float32"); add("nbt nzt", NW, "int32")
-    add("mS mc imc", 128, "int32"); add("bxi bzi bci", 8, "int32"); add("l15i", 16, "int32"); add("ip32 pmi pgi tha thb", 1, "int32")
-    add("ipf pm pg dc1 dc2 pm16 thh cn", 1, "float32")
-    add("rowI rowG If mSf KEY MX OH ones cK", 128, "float32"); add("rowT diag segm PAQ SC E WPm WPs E2", 256, "float32")
-    add("rowc", 40, "float32"); add("RD", 40, "float16"); add("rowGG", 1024, "float32"); add("BOg", 1024, "float16")
-    add("Ih BOh mch imch EC", 128, "float16"); add("tri RH", 256, "float16"); add("LT RR", 2048, "float16")
-    add("Ib prop8 bi16 bip bim", 128, "bfloat16")
-    add("ind ind16 vl nv5 own ea WS bad thr thr2 nc tv", 8, "float32"); add("bad2", 16, "float32"); add("nvi", 8, "int32"); add("LST", 32, "float32")
+    add("mc imc", 128, "int32"); add("bxi bzi bci", 8, "int32"); add("l15i", 16, "int32"); add("ip32 pmi pgi odi tha thb", 1, "int32")
+    add("ipf pm pg od ev dc1 dc2 pm16 thh cn wj wt", 1, "float32")
+    add("rowI rowG If MX FL NF ones segm", 128, "float32"); add("rowT diag FP SC E E2", 256, "float32")
+    add("WPm WPs segh", 256, "float16")
+    add("rowc", 40, "float32"); add("RD", 40, "float16"); add("BOg", 512, "float16"); add("dgh", 16, "float16"); add("ind16", 8, "float16")
+    add("BOh mch imch EC onesh", 128, "float16"); add("RW", 512, "float16"); add("LT RR", 2048, "float16")
+    add("Ib nIb cK prop8 bi16 bi32 bn16 bip bim bpen cbig", 128, "bfloat16"); add("GF", 256, "bfloat16")
+    add("ind vl nv5 own ea eb WS thr pt nc tv", 8, "float32"); add("nvi", 8, "int32"); add("LST", 32, "float32")
     add("ML nal nql LA LBp LAp LB", 128, "uint16"); add("BXL BZL bc VU MVL", 8, "uint16"); add("L15", 16, "uint16"); add("UL OF", 32, "uint16")
-    add("naf nqf", 128, "float32"); add("ZQ DF AD Bp Bb Ap M1 M2 M3 M4", 2048, "bfloat16"); add("EQ", 4096, "bfloat16")
-    add("RP", 512, "float32"); add("XD CL ZQP sb0 sb1", 256, "bfloat16")
+    add("naf nqf", 128, "float32"); add("Bp Bb D1 D2 R1 R2 R3 R4", 2048, "bfloat16"); add("EQ", 4096, "bfloat16")
+    add("XD CL ZQP sb0 sb1", 256, "bfloat16")
+    s["Lm"] = ("sbuf", [128, 8, 32], "float16")
     for n in ("st0", "st1"):
         s[n] = ("sbuf", [128, 3, 256], "bfloat16")
     for n in range(8):
@@ -30,7 +35,7 @@ def _buffers():
 
 
 SCRATCH = _buffers()
-SEMAPHORES = ["qV", "qS", "qP", "qG", "sent", "arr0", "arr1", "dms", "dz", "dmc", "dim", "dbx", "dbz", "dnz", "dnb", "dx", "dzo", "dmo"]
+SEMAPHORES = ["qV", "qS", "qP", "qG", "sent0", "sent1", "arr0", "arr1", "dz", "dmc", "dim", "dbx", "dbz", "dnz", "dnb", "dx", "dzo", "dmo"]
 
 
 def rank_program(g, core, T, topo):
@@ -75,15 +80,18 @@ def rank_program(g, core, T, topo):
         due["q" + q] += 1
         note(q, reads, writes, "q" + q, due["q" + q], dict(know[q]))
 
-    def dma(q, sem, out, in_, total=16):
+    def dma(q, sem, out, in_):
         order(q, in_[1], out[1])
         eng[q].dma_start(out[0], in_[0]).then_inc(T.sem[sem], 16)
         due[sem] += 16
-        note(q, in_[1], out[1], sem, total, dict(know[q]))
+        note(q, in_[1], out[1], sem, 16, dict(know[q]))
 
     def b(n, lo=0, hi=None, step=1):
         hi = SCRATCH[n][1][1] if hi is None else hi
         return (T[n][:, lo:hi:step] if step != 1 else T[n][:, lo:hi], [(n, lo, hi)])
+
+    def part(n, p0, p1, lo, hi, step=1):
+        return (T[n][p0:p1, lo:hi:step] if step != 1 else T[n][p0:p1, lo:hi], [(n, lo, hi)])
 
     def ext(ap):
         return (ap, [])
@@ -114,8 +122,12 @@ def rank_program(g, core, T, topo):
     def scan(out, d0, d1, o0, o1):
         op("V", lambda: g.vector.tensor_tensor_scan(out[0], d0[0], d1[0], 0.0, o0, o1), d0[1] + d1[1], out[1])
 
-    def act(out, in_, f=F.Copy, scale=1.0):
-        op("S", lambda: g.scalar.activation(out[0], in_[0], f, scale=scale), in_[1], out[1])
+    def act(out, in_, f=F.Copy, scale=1.0, bias=None):
+        sc, r = num(scale)
+        if bias is None:
+            op("S", lambda: g.scalar.activation(out[0], in_[0], f, scale=sc), in_[1] + r, out[1])
+        else:
+            op("S", lambda: g.scalar.activation(out[0], in_[0], f, bias=bias, scale=sc), in_[1] + r, out[1])
 
     def mm(out, l, r, start=True, stop=True):
         op("P", lambda: g.tensor.matmul(out[0], l[0], r[0], start, stop), l[1] + r[1], out[1])
@@ -126,51 +138,61 @@ def rank_program(g, core, T, topo):
         else:
             op("G", lambda: g.iota(out[0], pat, base, cm), [], out[1])
 
-    for k in range(8):
-        dma("SY"[k % 2], "dms", b("mS", 16 * k, 16 * k + 16), ext(T.m[k, :]), 128)
     dma("S", "dmc", b("mc"), ext(T.m[:, :]))
-    dma("Y", "dbx", b("bxi"), ext(T.bx[:, :]))
-    dma("S", "dim", b("imc"), ext(T.im[:, :]))
-    dma("Y", "dbz", b("bzi"), ext(T.bz[:, :]))
     dma("Y", "dz", b("Z", 0, NV), ext(T.z[:, :]))
+    dma("S", "dbz", b("bzi"), ext(T.bz[:, :]))
+    dma("Y", "dbx", b("bxi"), ext(T.bx[:, :]))
+    dma("Y", "dim", b("imc"), ext(T.im[:, :]))
     dma("Y", "dnz", b("nzt", 0, NV), ext(T.nz[:, :]))
     dma("Y", "dnb", b("nbt", 0, NV), ext(T.nb[:, :]))
-    dma("Y", "dx", b("X", 0, NV), ext(T.x[:, :]))
 
     iota(b("ip32"), [[0, 1]], 0, 1, False)
-    iota(b("ipf"), [[0, 1]], 0, 1)
-    iota(b("rowI"), [[1, 128]], 0, 0)
-    iota(b("rowG"), [[1, 8], [0, 16]], 0, 0)
     iota(b("rowT"), [[0, 16], [1, 16]], 0, 0)
+    iota(b("rowG"), [[1, 8], [0, 16]], 0, 0)
+    iota(b("rowI"), [[1, 128]], 0, 0)
     iota(b("rowc"), [[0, 5], [1, 8]], 0, 0)
     iota(b("l15i"), [[16, 16]], 15, 0, False)
     iota(b("bci"), [[1, 8]], 0, 0, False)
     iota(b("vl"), [[256, 8]], 0, 0)
-    iota(b("rowGG"), [[1, 8], [0, 128]], 0, 0)
-    for n in ("mrep", "imrep", "nbt", "nzt", "X"):
-        iota(b(n, NV, NW), [[0, NW - NV]], 0, 0, n[0] != "n")
-    ts(b("If"), b("rowI"), b("ipf"), None, A.is_equal)
     ts(b("pmi"), b("ip32"), 15, None, A.bitwise_and)
     ts(b("pgi"), b("ip32"), 4, None, A.arith_shift_right)
+    ts(b("odi"), b("ip32"), 4, 1, A.arith_shift_right, A.bitwise_and)
+    cp(b("ipf"), b("ip32"))
     cp(b("pm"), b("pmi"))
     cp(b("pg"), b("pgi"))
-    ts(b("BOh"), b("rowG"), b("pg"), None, A.is_equal)
+    cp(b("od"), b("odi"))
+    act(b("wj"), b("ipf"), F.Exp, -math.log(RATIO), 63.5 * math.log(RATIO))
+    ts(b("ev"), b("od"), -1.0, 1.0, A.mult, A.add)
+    ts(b("dgh"), b("rowT", 0, 16), b("pm"), None, A.is_equal)
     ts(b("diag"), b("rowT"), b("pm"), None, A.is_equal)
-    cp(b("mSf"), b("mS"))
-    mm(b("k0", 0, 128), b("mSf"), b("If"))
-    cp(b("ML"), b("k0", 0, 128))
-    cp(b("BXL"), b("bxi"))
-    cp(b("BZL"), b("bzi"))
-    for t in range(16):
+    ts(b("BOh"), b("rowG"), b("pg"), None, A.is_equal)
+    ts(b("If"), b("rowI"), b("ipf"), None, A.is_equal)
+    ts(b("ind"), b("rowc", 0, 8), b("pg"), None, A.is_equal)
+    act(b("wt"), b("wj"), F.Copy, 0.9 * RATIO)
+    act(b("cK"), b("rowT", 0, 128), F.Copy, -0.5)
+    act(b("Ib"), b("If"))
+    act(b("nIb"), b("If"), F.Copy, -1.0)
+    for n, c in (("bi16", 16.0), ("bi32", 32.0), ("bn16", -16.0), ("bip", 1.0), ("bim", -1.0), ("bpen", -BIG / 16), ("ind16", 0.0625)):
+        act(b(n, 0, 8), b("ind"), F.Copy, c)
+    for t in range(4):
         ts(b("LT", 128 * t, 128 * t + 128), b("BOh"), b("diag", t, t + 1), None, A.mult)
+    for e, n in enumerate(("ev", "od")):
+        ts((T["Lm"][:, :, 16 * e:16 * e + 16], [("Lm", 0, 256)]), b("mc"), b(n), None, A.mult)
+    for a in range(4):
+        for u in range(8):
+            mm(part("k0", 32 * a, 32 * a + 32, u, 128, 8), (T["Lm"][32 * a:32 * a + 32, u, :], [("Lm", 0, 256)]), part("dgh", 32 * a, 32 * a + 32, 0, 16))
     cp(b("mch"), b("mc"))
-    cp(b("imch"), b("imc"))
+    for t in range(4, 10):
+        ts(b("LT", 128 * t, 128 * t + 128), b("BOh"), b("diag", t, t + 1), None, A.mult)
+    cp(b("ML"), b("k0", 0, 128))
+    for t in range(10, 16):
+        ts(b("LT", 128 * t, 128 * t + 128), b("BOh"), b("diag", t, t + 1), None, A.mult)
     for t in range(16):
         mm(b("k%d" % (4 + t // 4), t % 4 * 128, t % 4 * 128 + 128), b("LT", 128 * t, 128 * t + 128), b("mch"))
-    for t in range(16):
-        mm(b("k%d" % (t // 4), t % 4 * 128, t % 4 * 128 + 128), b("LT", 128 * t, 128 * t + 128), b("imch"))
+    cp(b("BZL"), b("bzi"))
     cp(b("Y", 0, 1024), ind(b("Z", 0, NV), b("ML", 0, 64)))
     act(b("Y", 1024, 2048), ind(b("Z", 0, NV), b("ML", 64, 128)))
+    cp(b("BXL"), b("bxi"))
 
     def engines_to(src, dst):
         e = topo.engines(src, dst)
@@ -196,48 +218,50 @@ def rank_program(g, core, T, topo):
                 ids.append(DstId(rid=rid, pnc=pid))
             tr.append(RemoteDMATransfer(dst_ids=ids, dma_engine_mask=sum(1 << k for k in e), remote_sem=T.sem["arr%d" % rd],
                                         srcs=[T["sb%d" % rd][:, :]], dsts=[T["st%d" % rd][:, d - 1, :] for d, _ in ds]))
-            due["sent"] += len(e)
-        g.remote_dma_fused(tr, local_sem=T.sem["sent"])
+            due["sent%d" % rd] += len(e)
+        g.remote_dma_fused(tr, local_sem=T.sem["sent%d" % rd])
         due["arr%d" % rd] = sum(len(engines_to(T.cores[(rank + d) % N], core)) for d in (1, 2, 3))
         note("G", [], [("st%d" % rd, 0, 768)], "arr%d" % rd, due["arr%d" % rd], {})
 
     send(0)
-    ts(b("ind"), b("rowc", 0, 8), b("pg"), None, A.is_equal)
+    g.sync.wait_ge(T.sem["sent0"], due["sent0"])
+    dma("Y", "dx", b("X", 0, NV), ext(T.x[:, :]))
+    for n in ("nzt", "nbt", "mrep", "imrep", "X"):
+        iota(b(n, NV, NW), [[0, NW - NV]], 0, 0, n[0] != "n")
+    cp(b("imch"), b("imc"))
     for k in range(4):
         act(b("mrep", 512 * k, 512 * k + 512), b("k%d" % (4 + k)))
-    for k in range(4):
-        cp(b("imrep", 512 * k, 512 * k + 512), b("k%d" % k))
-    ts(b("segm"), b("rowT"), 0.0, None, A.is_gt)
-    ts(b("cK"), b("rowT", 0, 128), -1.0, 15.0, A.mult, A.add)
-    act(b("bi16", 0, 8), b("ind"), F.Copy, 16.0)
-    act(b("bip", 0, 8), b("ind"))
-    act(b("bim", 0, 8), b("ind"), F.Copy, -1.0)
-    act(b("ind16"), b("ind"), F.Copy, 0.0625)
+    for t in range(16):
+        mm(b("k%d" % (t // 4), t % 4 * 128, t % 4 * 128 + 128), b("LT", 128 * t, 128 * t + 128), b("imch"))
+    ts(b("segh"), b("rowT"), 0.0, None, A.is_gt)
+    ts(b("segm"), b("rowT", 0, 128), 0.0, None, A.is_gt)
     cp(b("L15"), b("l15i"))
     cp(b("bc"), b("bci"))
-    act(b("Ih"), b("If"))
-    act(b("Ib"), b("If"))
-    ts(b("BOg"), b("rowGG"), b("pg"), 0.0625, A.is_equal, A.mult)
-    for k in (0, 128):
-        ts(b("tri", k, k + 128), b("rowI"), b("ipf"), 4096.0, A.is_le, A.mult)
+    fill(b("cbig", 0, 8), -BIG)
+    fill(b("ones"), 1.0)
+    fill(b("onesh"), 0.0625)
+    for h in range(4):
+        ts(b("BOg", 128 * h, 128 * h + 128), b("onesh"), b("ind", 2 * h + 1, 2 * h + 2), None, A.mult)
     ts(b("dc1"), b("ipf"), 2.0, float(NW), A.mult, A.add)
-    ts(b("dc2"), b("dc1"), 256.0, None, A.add)
+    ts(b("dc2"), b("ipf"), 2.0, float(NW + 256), A.mult, A.add)
     for k in range(4):
         ts(b("RD", 8 * k, 8 * k + 8), b("rowc", 8 * k, 8 * k + 8), b("pg"), b("dc%d" % (1 + k % 2)), A.is_equal, A.mult)
     cp(b("RD", 32, 40), b("ind"))
     ts(b("pm16"), b("pm"), 16.0, None, A.mult)
     ts(b("vl"), b("vl"), b("pm16"), None, A.add)
-    fill(b("ones"), 1.0)
-    fill(b("thh"), 0.0)
+    ts(b("nvi"), b("vl"), 5.0, 1.0, A.mult, A.add)
+    ts(b("nvi"), b("nvi"), 2047, None, A.bitwise_and)
+    cp(b("nv5"), b("nvi"))
+    fill(b("thh"), -BIG)
 
     def half(n, k):
         return b(n, 128 * k, 128 * k + 128)
 
-    def ch(n, c):
-        return b(n, 512 * c, 512 * c + 512)
+    def ch(n, c, m=1):
+        return b(n, 512 * c, 512 * (c + m))
 
-    def lst(n, c):
-        return b(n, 32 * c, 32 * c + 32)
+    def lst(n, c, m=1):
+        return b(n, 32 * c, 32 * (c + m))
 
     def every16(n, base=15, cnt=8):
         return b(n, base, base + 16 * cnt - 15, 16)
@@ -248,172 +272,166 @@ def rank_program(g, core, T, topo):
     def names(rd):
         if rd == 0:
             tt(half("WPm", 0), b("mrep", 0, NV, 16), half("diag", 0), A.mult)
-            cp(b("nal"), b("nbt", 0, NV, 16))
         else:
-            tt(half("WPm", 0), ind(Mw, b("VU")), half("diag", 0), A.mult)
-            cp(b("nal"), ind(NBw, b("VU")))
-        scan(half("WPs", 0), half("segm", 0), half("WPm", 0), A.mult, A.add)
-        cp(b("naf"), b("nal"))
+            tt(half("WPm", 0), ind(b("mrep", 0, NV), b("VU")), half("diag", 0), A.mult)
+        scan(half("WPs", 0), half("segh", 0), half("WPm", 0), A.mult, A.add)
+        if rd == 1:
+            cp(b("nal"), ind(b("nbt", 0, NV), b("VU")))
         cp(b("MVL"), every16("WPs"))
-        cp(b("nql"), ind(NZw, b("MVL")))
+        cp(b("nql"), ind(b("nzt", 0, NV), b("MVL")))
+        if rd == 0:
+            cp(b("nal"), b("nbt", 0, NV, 16))
         cp(b("nqf"), b("nql"))
+        cp(b("naf"), b("nal"))
 
+    for k in range(4):
+        act(b("imrep", 512 * k, 512 * k + 512), b("k%d" % k))
     names(0)
     for rd in range(ROUNDS):
         last = rd == ROUNDS - 1
-        cp((T["Y"][:, NV:NW], [("Y", NV, NW)]), (T["st%d" % rd][:, :, 0:128], [("st%d" % rd, 0, 768)]))
-        act((T["Z"][:, NV:NW], [("Z", NV, NW)]), (T["st%d" % rd][:, :, 128:256], [("st%d" % rd, 0, 768)]))
-        def dsum(c):
+        st = "st%d" % rd
+        cp((T["Z"][:, NV:NW], [("Z", NV, NW)]), (T[st][:, :, 128:256], [(st, 0, 768)]))
+        cp((T["Y"][:, NV:NW], [("Y", NV, NW)]), (T[st][:, :, 0:128], [(st, 0, 768)]))
+        mm(b("k1", 0, 128), b("nqf"), b("If"))
+        mm(b("k1", 128, 256), b("naf"), b("If"))
+        mm(b("k0", 0, 128), b("Ib"), b("cK"), True, False)
+
+        def dsum(n, c, coef):
             for k in range(16):
-                mm((T["k0"][32 * c:32 * c + 32, k:128:16], [("k0", 0, 128)]), b("AD", 512 * c + k, 512 * c + 512, 16), b("bi16", 0, 8))
-        act(ch("ZQ", 0), ind(Zw, lst("nql", 0)))
-        cp(ch("ZQ", 1), ind(Zw, lst("nql", 1)))
-        tt(ch("DF", 0), ind(Yw, lst("nal", 0)), ch("ZQ", 0), A.subtract)
-        act(ch("ZQ", 2), ind(Zw, lst("nql", 2)))
-        act(ch("AD", 0), ch("DF", 0), F.Abs)
-        dsum(0)
-        tt(ch("DF", 1), ind(Yw, lst("nal", 1)), ch("ZQ", 1), A.subtract)
-        act(ch("ZQ", 3), ind(Zw, lst("nql", 3)))
-        act(ch("AD", 1), ch("DF", 1), F.Abs)
-        mm(b("k1", 0, 128), b("naf"), b("If"))
-        mm(b("k1", 128, 256), b("nqf"), b("If"))
-        dsum(1)
-        for c in (2, 3):
-            tt(ch("DF", c), ind(Yw, lst("nal", c)), ch("ZQ", c), A.subtract)
-            act(ch("AD", c), ch("DF", c), F.Abs)
-            dsum(c)
-        tt(b("KEY"), b("k0", 0, 128), b("cK"), A.add)
-        scan(b("MX"), half("segm", 0), b("KEY"), A.mult, A.max)
-        tt(b("OH"), ind(b("MX"), b("L15", 0, 8)), b("KEY"), A.is_equal)
-        tt(half("PAQ", 0), b("OH"), b("k1", 0, 128), A.mult)
-        tt(half("PAQ", 1), b("OH"), b("k1", 128, 256), A.mult)
-        scan(b("SC"), b("segm"), b("PAQ"), A.mult, A.add)
-        tt(b("E"), ind(b("SC"), b("L15")), b("diag"), A.mult)
+                mm(part("k0", 32 * c, 32 * c + 32, k, 128, 16), b(n, 512 * c + k, 512 * c + 512, 16), b(coef, 0, 8), False, False)
+
+        ZQ, DF, AD = "R3", "R4", "R2"
+        act(b(ZQ, 0, 320), ind(Zw, b("nql", 0, 20)))
+        cp(b(ZQ, 320, 512), ind(Zw, b("nql", 20, 32)))
+        for c in range(4):
+            if c < 3:
+                act(ch(ZQ, c + 1), ind(Zw, lst("nql", c + 1)))
+            tt(ch(DF, c), ind(Yw, lst("nal", c)), ch(ZQ, c), A.subtract)
+        for c in (0, 1):
+            act(ch(AD, c), ch(DF, c), F.Abs)
+        dsum(DF, 2, "bn16")
+        dsum(AD, 0, "bi16")
+        dsum(DF, 3, "bn16")
+        for c in (3, 2):
+            ts(ch(AD, c), ch(DF, c), 0.0, None, A.max)
+        dsum(AD, 3, "bi32")
+        dsum(AD, 1, "bi16")
+        dsum(AD, 2, "bi32")
+        mm(b("k0", 0, 128), b("Ib"), b("cK"), False, True)
+        scan(b("MX"), half("segm", 0), b("k0", 0, 128), A.mult, A.max)
+        tt(b("FL"), b("k0", 0, 128), b("MX"), A.is_equal)
+        act(b("NF"), b("FL"), F.Identity, -1.0, 1.0)
+        for e in (0, 1):
+            tt(half("FP", e), b("FL"), b("k1", 128 * e, 128 * e + 128), A.mult)
+        for e, kb in ((0, "k2"), (1, "k4")):
+            scan(half("SC", e), b("NF"), half("FP", e), A.mult, A.add)
+            tt(half("E", e), ind(half("SC", e), b("L15", 0, 8)), half("diag", 0), A.mult)
+            mm(b(kb, 0, 8), half("E", e), b("ind"))
         act(b("E2"), ind(b("SC"), b("L15")))
-        mm(b("k2", 8, 16), half("E", 1), b("ind"))
-        mm(b("k2", 0, 8), half("E", 0), b("ind"))
-        cp(b("UL", 16, 24), b("k2", 8, 16))
-        cp(b("UL", 0, 8), b("k2", 0, 8))
+        cp(b("UL", 16, 24), b("k2", 0, 8))
         cp(b("LBp"), ind(NZw, b("UL", 16, 24)))
-        cp(b("LA"), ind(NBw, b("UL", 0, 8)))
-        tt(half("WPm", 0), ind(Iw, b("UL", 16, 24)), half("diag", 0), A.mult)
-        tt(half("WPm", 1), ind(Mw, b("UL", 0, 8)), half("diag", 1), A.mult)
-        scan(b("WPs"), b("segm"), b("WPm"), A.mult, A.add)
+        cp(b("UL", 0, 8), b("k4", 0, 8))
+        mm(b("k3", 0, 128), half("E2", 1), b("If"))
+        mm(b("k3", 128, 256), half("E2", 0), b("If"))
         act(ch("Bp", 0), ind(Zw, lst("LBp", 0)))
-        cp(b("UL", 8, 16), every16("WPs"))
+        cp(b("LA"), ind(NBw, b("UL", 0, 8)))
+        tt(half("WPm", 1), ind(Mw, b("UL", 0, 8)), half("diag", 1), A.mult)
+        tt(half("WPm", 0), ind(Iw, b("UL", 16, 24)), half("diag", 0), A.mult)
+        scan(b("WPs"), b("segh"), b("WPm"), A.mult, A.add)
+        act(half("RW", 1), ind(Iw, b("UL", 16, 24)))
+        act(half("RW", 0), b("k3", 0, 128))
         cp(b("UL", 24, 32), every16("WPs", 143))
-        act(b("LST", 0, 8), b("k2", 0, 8))
-        act(b("LST", 16, 24), b("k2", 8, 16))
-        for c in (1, 2, 3):
-            act(ch("Bp", c), ind(Zw, lst("LBp", c)))
-        mm(b("k3", 0, 128), half("E2", 0), b("If"))
-        mm(b("k3", 128, 256), half("E2", 1), b("If"))
+        cp(b("UL", 8, 16), every16("WPs"))
 
-        def gsum(n, c, sgn, start, stop):
+        def gsum(n, c, sgn, stop=False):
             for k in range(16):
-                mm((T["k1"][32 * c:32 * c + 32, 0:8], [("k1", 0, 8)]), b(n, 512 * c + k, 512 * c + 512, 16), b(sgn, 0, 8), start and k == 0, stop and k == 15)
+                mm(part("k0", 32 * c, 32 * c + 32, 0, 8), b(n, 512 * c + k, 512 * c + 512, 16), b(sgn, 0, 8), False, stop and k == 15)
 
-        def gall(n, sgn, start, stop):
+        def gall(n, sgn):
             for k in range(16):
-                mm(b("k0", 0, 8), b(n, k, 2048, 16), b(sgn, 0, 8), start and k == 0, stop and k == 15)
+                mm(b("k0", 0, 8), b(n, k, 2048, 16), b(sgn, 0, 8), False, False)
+
+        def shifted(n, c, kb):
+            mm(b(kb), b("Ib"), ch("Bp", c), True, False)
+            mm(b(kb), b("Ib"), ch(n, c), False, False)
+            mm(b(kb), b("nIb"), ch("Bb", c), False, True)
 
         def rows(h):
-            kb = "k%d" % (2 + h % 2)
+            kb = "k%d" % (1 + 2 * h)
             for e in (0, 1):
-                gg = 2 * h + e
-                mm(b(kb, 256 * e, 256 * e + 256), b("BOg", 128 * gg, 128 * gg + 128), b("RH"), True, False)
-                mm(b(kb, 256 * e, 256 * e + 256), b("Ih"), b("tri"), False, True)
-            act(ch("RR", h), b(kb))
+                mm(b(kb, 256 * e, 256 * e + 256), b("BOg", 128 * (2 * h + e), 128 * (2 * h + e + 1)), b("RW", 0, 256))
 
-        def compare(h):
-            for gg in (2 * h, 2 * h + 1):
-                for s in (0, 1):
-                    col = b("SC", 16 * gg + 15, 16 * gg + 16) if s == 0 else b("WS", gg, gg + 1)
-                    ts(b("EQ", (2 * gg + s) * 256, (2 * gg + s) * 256 + 256), b("RR", 256 * gg, 256 * gg + 256), col, None, A.is_equal)
+        def place(gg):
+            return 256 * (gg // 2 + 4 * (gg % 2))
 
-        def topb(c):
-            mm(b("k%d" % (4 + 2 * (c % 2))), b("Ib"), ch("Bp", c))
+        def compare(gg):
+            for s in (0, 1):
+                col = b("SC", 128 + 16 * gg + 15, 128 + 16 * gg + 16) if s == 0 else b("WS", gg, gg + 1)
+                ts(b("EQ", (2 * gg + s) * 256, (2 * gg + s) * 256 + 256), b("RR", place(gg), place(gg) + 256), col, b("wj"), A.is_equal, A.mult)
 
-        def tops(c):
-            mm(b("k%d" % (5 + 2 * (c % 2))), b("Ib"), ch("Bb", c))
-
-        topb(0)
-        topb(1)
-        for c in range(4):
-            tt(ch("M1", c), ind(Yw, lst("LA", c)), ch("Bp", c), A.max)
-            if c == 0:
-                cp(b("LB"), ind(NZw, b("UL", 24, 32)))
-            if c == 1:
-                cp(b("LAp"), ind(NBw, b("UL", 8, 16)))
-        act(ch("Bb", 0), ind(Zw, lst("LB", 0)))
-        act(ch("Bb", 1), ind(Zw, lst("LB", 1)))
-        act(half("RP", 1), ind(Iw, b("UL", 16, 24)))
-        act(half("RP", 0), b("k3", 0, 128))
-        act(b("RH"), b("RP", 0, 256))
-        mm(b("k2", 0, 8), half("RP", 1), b("ind16"))
-        act(ch("Bb", 2), ind(Zw, lst("LB", 2)))
+        for h in range(4):
+            o, i = b("RR", 256 * h, 256 * h + 256), part("RW", 32 * h, 32 * h + 1, 0, 256)
+            op("G", lambda: g.partition_broadcast(o[0], i[0], 128), i[1], o[1])
+        mm(b("k2", 0, 8), half("RW", 1), b("ind16"))
+        act(ch("Bp", 1), ind(Zw, lst("LBp", 1)))
+        act(half("RW", 2), b("k3", 128, 256))
+        act(ch("Bp", 2), ind(Zw, lst("LBp", 2)))
         act(b("WS"), b("k2", 0, 8))
-        act(half("RP", 2), b("k3", 128, 256))
-        act(ch("Bb", 3), ind(Zw, lst("LB", 3)))
-        act(half("RP", 3), ind(Mw, b("UL", 0, 8)))
-        act(b("LST", 8, 16), every16("WPs"))
-        act(b("LST", 24, 32), every16("WPs", 143))
-        act(b("ZQP"), ind(Zw, b("UL", 16, 32)))
-        for c in range(4):
-            tt(ch("M2", c), ind(Yw, lst("LA", c)), ch("Bb", c), A.max)
-        tops(0)
-        tops(1)
+        act(ch("Bp", 3), ind(Zw, lst("LBp", 3)))
         rows(0)
         rows(1)
-        gall("M1", "bim", True, False)
-        act(ch("Ap", 0), ind(Yw, lst("LAp", 0)))
-        act(ch("Ap", 1), ind(Yw, lst("LAp", 1)))
-        rows(2)
-        rows(3)
-        gall("M2", "bip", False, True)
-        act(ch("Ap", 2), ind(Yw, lst("LAp", 2)))
-        act(ch("Ap", 3), ind(Yw, lst("LAp", 3)))
-        ts(b("bad"), every16("MX"), 16.0, None, A.is_lt)
-        ts(b("bad2"), every16("SC", 15, 16), float(NV), None, A.is_ge)
-        tt(b("bad"), b("bad"), b("bad2", 0, 8), A.add)
-        tt(b("bad"), b("bad"), b("bad2", 8, 16), A.add)
-        ts(b("thr"), b("bad"), 1.0e6, b("thh"), A.mult, A.add)
+        tt(ch("D1", 0), ind(Yw, lst("LA", 0)), ch("Bp", 0), A.subtract)
+        cp(b("LB"), ind(NZw, b("UL", 24, 32)))
+        tt(ch("D1", 1), ind(Yw, lst("LA", 1)), ch("Bp", 1), A.subtract)
+        cp(b("LAp"), ind(NBw, b("UL", 8, 16)))
+        ts(half("GF", 0), half("RW", 0), float(NV), None, A.is_ge)
+        tt(ch("D1", 2), ind(Yw, lst("LA", 2)), ch("Bp", 2), A.subtract)
+        ts(half("GF", 1), half("RW", 2), float(NV), None, A.is_ge)
+        ts(b("thr"), every16("MX"), 0.5, b("thh"), A.is_ge, A.mult)
+        cp(b("LST"), b("UL"))
+        tt(ch("D1", 3), ind(Yw, lst("LA", 3)), ch("Bp", 3), A.subtract)
+        mm(b("k0", 0, 8), b("Ib"), b("cbig", 0, 8), True, False)
+        mm(b("k0", 0, 8), half("GF", 0), b("bpen", 0, 8), False, False)
+        for c in range(4):
+            act(ch("Bb", c), ind(Zw, lst("LB", c)))
+            shifted("D1", c, "k%d" % (4 + c))
+        ts(b("R1"), b("D1"), 0.0, None, A.max)
+        gall("R1", "bim")
+        for c in range(4):
+            tt(ch("D2", c), ind(Yw, lst("LAp", c)), ch("Bp", c), A.subtract)
+        act(ch("RR", 2), b("k1"))
+        for c in range(4):
+            act(ch("R3", c), b("k%d" % (4 + c)), F.Relu)
+            shifted("D2", c, "k%d" % (4 + c))
+            if c == 0:
+                act(ch("RR", 3), b("k3"))
+            if c == 1:
+                act(half("RW", 3), ind(Mw, b("UL", 0, 8)))
+            if c == 2:
+                act(b("ZQP"), ind(Zw, b("UL", 16, 32)))
+        ts(b("R2"), b("D2"), 0.0, None, A.max)
+        gall("R3", "bip")
+        gall("R2", "bip")
+        for gg in (0, 2, 4, 6, 1, 3, 5, 7):
+            compare(gg)
         tt(b("XD"), ind(Xw, b("UL", 0, 16)), b("ZQP"), A.subtract)
-        compare(0)
-        compare(1)
         ts(b("CL"), b("XD"), 1.0, -1.0, A.min, A.max)
-
-        def late(c):
-            tt(ch("M3", c), ch("Ap", c), b("k%d" % (4 + 2 * (c % 2))), A.max)
-            tt(ch("M4", c), ch("Ap", c), b("k%d" % (5 + 2 * (c % 2))), A.max)
-            if c < 2:
-                topb(c + 2)
-                tops(c + 2)
-            gsum("M3", c, "bip", True, False)
-            gsum("M4", c, "bim", False, True)
-
-        late(0)
-        compare(2)
-        late(1)
-        compare(3)
-        tt(b("thr2"), b("thr"), b("k0", 0, 8), A.subtract)
-        late(2)
-        late(3)
-        tt(b("prop8", 0, 8), b("k1", 0, 8), b("thr2"), A.is_gt)
+        for c in range(4):
+            act(ch("R4", c), b("k%d" % (4 + c)), F.Relu)
+            gsum("R4", c, "bim")
+        mm(b("k0", 0, 8), half("GF", 1), b("bpen", 0, 8), False, True)
+        if not last:
+            ts(b("own"), b("LST", 16, 24), float(NV), None, A.is_ge)
+            tt(b("ea"), b("LST", 8, 16), b("LST", 0, 8), A.subtract)
+            tt(b("eb"), b("own"), b("nv5"), A.mult)
+            tt(b("ea"), b("ea"), b("eb"), A.add)
+        tt(b("prop8", 0, 8), b("k0", 0, 8), b("thr"), A.is_gt)
+        act(b("pt"), b("prop8", 0, 8), F.Copy, b("wt"))
         for gg in range(8):
             for i in range(4):
                 o = (2 * gg + i // 2) * 256 + i % 2 * 128
                 mm(b("k2", gg, gg + 1), b("EQ", o, o + 128), b("prop8", gg, gg + 1), i == 0, i == 3)
-        if not last:
-            ts(b("nvi"), b("vl"), 5.0, 1.0, A.mult, A.add)
-            ts(b("nvi"), b("nvi"), 2047, None, A.bitwise_and)
-            cp(b("nv5"), b("nvi"))
-            ts(b("own"), b("LST", 16, 24), float(NV), None, A.is_lt)
-            tt(b("ea"), b("LST", 8, 16), b("nv5"), A.subtract)
-            tt(b("ea"), b("ea"), b("own"), A.mult)
-            tt(b("ea"), b("ea"), b("nv5"), A.add)
-            tt(b("ea"), b("ea"), b("LST", 0, 8), A.subtract)
-        tt(b("nc"), b("k2", 0, 8), b("prop8", 0, 8), A.is_ge)
+        tt(b("nc"), b("k2", 0, 8), b("pt"), A.is_ge)
         tt(b("EC"), ind(b("nc"), b("bc")), half("diag", 0), A.mult)
         mm(b("k3", 0, 40), b("EC"), b("RD"))
         tt(b("OF"), b("LST"), b("k3", 0, 32), A.max)
@@ -424,7 +442,7 @@ def rank_program(g, core, T, topo):
         tt(scat("Z", 16), b("CL"), b("ZQP"), A.add)
         if last:
             dma("Y", "dzo", ext(T.zo[:, :]), b("Z", 0, NV))
-            cp(scat("mrep", 0), b("RP", 256, 512))
+            cp(scat("mrep", 0), b("RW", 256, 512))
             dma("S", "dmo", ext(T.mo[:, :]), (T["mrep"][0:128:16, 0:NV], [("mrep", 0, NV)]))
             break
         tt(scat("Y", 0), b("CL"), b("ZQP"), A.add)
@@ -432,13 +450,13 @@ def rank_program(g, core, T, topo):
         tt(b("tv"), b("k3", 32, 40), b("ea"), A.mult)
         tt(b("VU"), b("tv"), b("LST", 0, 8), A.add)
         mm(b("k2", 0, 8), b("ones"), b("nc"))
-        cp(scat("mrep", 0), b("RP", 256, 512))
+        cp(scat("mrep", 0), b("RW", 256, 512))
         names(1)
         op("V", lambda: g.vector.tensor_reduce(T["cn"][:, :], T["k2"][:, 0:8], AxisListType.X, A.add), [("k2", 0, 8)], [("cn", 0, 1)])
         ts(b("tha"), b("cn"), -1.0, None, A.mult)
         ts(b("thb"), b("tha"), 31, None, A.bitwise_and)
-        ts(b("thh"), b("thb"), 0.5, None, A.mult)
-        cp(scat("imrep", 16), b("RP", 0, 256))
+        ts(b("thh"), b("thb"), 0.5, -BIG, A.mult, A.add)
+        cp(scat("imrep", 16), b("RW", 0, 256))
     for s in SEMAPHORES:
         if know["G"].get(s, 0) < due[s] and due[s]:
             g.wait_ge(T.sem[s], due[s])

@@ -6,6 +6,7 @@ N, NV, NW, DUMP = 8, 2048, 2432, 2944
 ROUNDS = 2
 BIG = float(2 ** 20)
 RATIO = 3.5
+FL = {}
 
 
 def _buffers():
@@ -16,13 +17,13 @@ def _buffers():
     add("Z Y", DUMP, "bfloat16"); add("X", NW, "bfloat16")
     add("mrep imrep", DUMP, "float32"); add("nbt nzt", NW, "int32")
     add("mc imc", 128, "int32"); add("bxi bzi bci", 8, "int32"); add("l15i", 16, "int32"); add("ip32 pmi pgi odi tha thb", 1, "int32")
-    add("ipf pm pg od ev dc1 dc2 pm16 thh cn wj wt", 1, "float32")
-    add("rowI rowG If MX FL NF ones segm", 128, "float32"); add("rowT diag FP SC E E2", 256, "float32")
+    add("ipf pm pg od ev pm16 thh cn wj wt", 1, "float32")
+    add("rowI rowG rowT diag If MX FG NF ones segm", 128, "float32"); add("FP SC E E2", 256, "float32")
     add("WPm WPs segh", 256, "float16")
-    add("rowc", 40, "float32"); add("RD", 40, "float16"); add("BOg", 512, "float16"); add("dgh", 16, "float16"); add("ind16", 8, "float16")
-    add("BOh mch imch EC onesh", 128, "float16"); add("RW", 512, "float16"); add("LT RR", 2048, "float16")
+    add("rowc dcv ind", 32, "float32"); add("RD", 40, "float16"); add("BOg", 512, "float16"); add("dgh", 16, "float16"); add("ind16", 8, "float16")
+    add("BOh mch imch EC", 128, "float16"); add("RW", 512, "float16"); add("LT RR", 2048, "float16")
     add("Ib nIb cK prop8 bi16 bi32 bn16 bip bim bpen cbig", 128, "bfloat16"); add("GF", 256, "bfloat16")
-    add("ind vl nv5 own ea eb WS thr pt nc tv", 8, "float32"); add("nvi", 8, "int32"); add("LST", 32, "float32")
+    add("vl nv5 own ea WS thr pt nc tv i16", 8, "float32"); add("nvi", 8, "int32"); add("LST", 32, "float32")
     add("ML nal nql LA LBp LAp LB", 128, "uint16"); add("BXL BZL bc VU MVL", 8, "uint16"); add("L15", 16, "uint16"); add("UL OF", 32, "uint16")
     add("naf nqf", 128, "float32"); add("Bp Bb D1 D2 R1 R2 R3 R4", 2048, "bfloat16"); add("EQ", 4096, "bfloat16")
     add("XD CL ZQP sb0 sb1", 256, "bfloat16")
@@ -93,6 +94,18 @@ def rank_program(g, core, T, topo):
     def part(n, p0, p1, lo, hi, step=1):
         return (T[n][p0:p1, lo:hi:step] if step != 1 else T[n][p0:p1, lo:hi], [(n, lo, hi)])
 
+    def half(n, k):
+        return b(n, 128 * k, 128 * k + 128)
+
+    def ch(n, c, m=1):
+        return b(n, 512 * c, 512 * (c + m))
+
+    def lst(n, c, m=1):
+        return b(n, 32 * c, 32 * (c + m))
+
+    def every16(n, base=15, cnt=8):
+        return b(n, base, base + 16 * cnt - 15, 16)
+
     def ext(ap):
         return (ap, [])
 
@@ -116,9 +129,6 @@ def rank_program(g, core, T, topo):
     def cp(out, in_):
         op("V", lambda: g.vector.tensor_copy(out[0], in_[0]), in_[1] + out[1][1:], out[1][:1])
 
-    def fill(out, c):
-        op("V", lambda: g.vector.memset(out[0], c), [], out[1])
-
     def scan(out, d0, d1, o0, o1):
         op("V", lambda: g.vector.tensor_tensor_scan(out[0], d0[0], d1[0], 0.0, o0, o1), d0[1] + d1[1], out[1])
 
@@ -140,59 +150,65 @@ def rank_program(g, core, T, topo):
 
     dma("S", "dmc", b("mc"), ext(T.m[:, :]))
     dma("Y", "dz", b("Z", 0, NV), ext(T.z[:, :]))
+    dma("S", "dbx", b("bxi"), ext(T.bx[:, :]))
     dma("S", "dbz", b("bzi"), ext(T.bz[:, :]))
-    dma("Y", "dbx", b("bxi"), ext(T.bx[:, :]))
     dma("Y", "dim", b("imc"), ext(T.im[:, :]))
     dma("Y", "dnz", b("nzt", 0, NV), ext(T.nz[:, :]))
     dma("Y", "dnb", b("nbt", 0, NV), ext(T.nb[:, :]))
 
     iota(b("ip32"), [[0, 1]], 0, 1, False)
-    iota(b("rowT"), [[0, 16], [1, 16]], 0, 0)
+    iota(b("rowT"), [[0, 8], [1, 16]], 0, 0)
     iota(b("rowG"), [[1, 8], [0, 16]], 0, 0)
     iota(b("rowI"), [[1, 128]], 0, 0)
-    iota(b("rowc"), [[0, 5], [1, 8]], 0, 0)
+    iota(b("rowc"), [[0, 4], [1, 8]], 0, 0)
+    iota(b("vl"), [[256, 8]], 0, 0)
+    iota(b("ones"), [[0, 128]], 1, 0)
     iota(b("l15i"), [[16, 16]], 15, 0, False)
     iota(b("bci"), [[1, 8]], 0, 0, False)
-    iota(b("vl"), [[256, 8]], 0, 0)
-    ts(b("pmi"), b("ip32"), 15, None, A.bitwise_and)
-    ts(b("pgi"), b("ip32"), 4, None, A.arith_shift_right)
-    ts(b("odi"), b("ip32"), 4, 1, A.arith_shift_right, A.bitwise_and)
+    iota(b("dcv"), [[0, 2], [256, 2], [0, 8]], NW, 2)
     cp(b("ipf"), b("ip32"))
-    cp(b("pm"), b("pmi"))
-    cp(b("pg"), b("pgi"))
-    cp(b("od"), b("odi"))
+    ts(b("pmi"), b("ip32"), 15, None, A.bitwise_and)
+    ts(b("odi"), b("ip32"), 4, 1, A.arith_shift_right, A.bitwise_and)
+    ts(b("pgi"), b("ip32"), 4, None, A.arith_shift_right)
     act(b("wj"), b("ipf"), F.Exp, -math.log(RATIO), 63.5 * math.log(RATIO))
-    ts(b("ev"), b("od"), -1.0, 1.0, A.mult, A.add)
-    ts(b("dgh"), b("rowT", 0, 16), b("pm"), None, A.is_equal)
+    cp(b("pm"), b("pmi"))
+    cp(b("od"), b("odi"))
+    cp(b("pg"), b("pgi"))
     ts(b("diag"), b("rowT"), b("pm"), None, A.is_equal)
+    ts(b("ev"), b("od"), -1.0, 1.0, A.mult, A.add)
     ts(b("BOh"), b("rowG"), b("pg"), None, A.is_equal)
+    ts(b("dgh"), b("rowT", 0, 16), b("pm"), None, A.is_equal)
+    ts(b("pm16"), b("pm"), 16.0, None, A.mult)
     ts(b("If"), b("rowI"), b("ipf"), None, A.is_equal)
-    ts(b("ind"), b("rowc", 0, 8), b("pg"), None, A.is_equal)
-    act(b("wt"), b("wj"), F.Copy, 0.9 * RATIO)
-    act(b("cK"), b("rowT", 0, 128), F.Copy, -0.5)
-    act(b("Ib"), b("If"))
-    act(b("nIb"), b("If"), F.Copy, -1.0)
-    for n, c in (("bi16", 16.0), ("bi32", 32.0), ("bn16", -16.0), ("bip", 1.0), ("bim", -1.0), ("bpen", -BIG / 16), ("ind16", 0.0625)):
-        act(b(n, 0, 8), b("ind"), F.Copy, c)
-    for t in range(4):
-        ts(b("LT", 128 * t, 128 * t + 128), b("BOh"), b("diag", t, t + 1), None, A.mult)
-    for e, n in enumerate(("ev", "od")):
-        ts((T["Lm"][:, :, 16 * e:16 * e + 16], [("Lm", 0, 256)]), b("mc"), b(n), None, A.mult)
+    ts(b("ind"), b("rowc"), b("pg"), None, A.is_equal)
+    ts(b("vl"), b("vl"), b("pm16"), None, A.add)
+
+    def lt(t0, t1):
+        for t in range(t0, t1):
+            ts(half("LT", t), b("BOh"), b("diag", t, t + 1), None, A.mult)
+
+    def spread(n, k0):
+        for t in range(16):
+            mm(half("k%d" % (k0 + t // 4), t % 4), half("LT", t), b(n))
+
+    for t in range(8, 16):
+        act(half("LT", t), b("BOh"), F.Copy, b("diag", t, t + 1))
+    lt(0, 2)
+    for e, k in enumerate(("ev", "od")):
+        ts((T["Lm"][:, :, 16 * e:16 * e + 16], [("Lm", e, e + 1)]), b("mc"), b(k), None, A.mult)
     for a in range(4):
         for u in range(8):
-            mm(part("k0", 32 * a, 32 * a + 32, u, 128, 8), (T["Lm"][32 * a:32 * a + 32, u, :], [("Lm", 0, 256)]), part("dgh", 32 * a, 32 * a + 32, 0, 16))
+            mm(part("k0", 32 * a, 32 * a + 32, u, 128, 8), (T["Lm"][32 * a:32 * a + 32, u, :], [("Lm", 0, 2)]), part("dgh", 32 * a, 32 * a + 32, 0, 16))
     cp(b("mch"), b("mc"))
-    for t in range(4, 10):
-        ts(b("LT", 128 * t, 128 * t + 128), b("BOh"), b("diag", t, t + 1), None, A.mult)
+    lt(2, 6)
     cp(b("ML"), b("k0", 0, 128))
-    for t in range(10, 16):
-        ts(b("LT", 128 * t, 128 * t + 128), b("BOh"), b("diag", t, t + 1), None, A.mult)
-    for t in range(16):
-        mm(b("k%d" % (4 + t // 4), t % 4 * 128, t % 4 * 128 + 128), b("LT", 128 * t, 128 * t + 128), b("mch"))
-    cp(b("BZL"), b("bzi"))
+    lt(6, 8)
+    spread("mch", 4)
     cp(b("Y", 0, 1024), ind(b("Z", 0, NV), b("ML", 0, 64)))
     act(b("Y", 1024, 2048), ind(b("Z", 0, NV), b("ML", 64, 128)))
+    cp(b("BZL"), b("bzi"))
     cp(b("BXL"), b("bxi"))
+    cp(b("imch"), b("imc"))
 
     def engines_to(src, dst):
         e = topo.engines(src, dst)
@@ -202,9 +218,13 @@ def rank_program(g, core, T, topo):
         used = topo.engines(src, far[0])
         return [k for k in e if k not in used]
 
+    def border(rd, k):
+        if k:
+            act(half("sb%d" % rd, 1), ind(b("Z", 0, NV), b("BZL")))
+        else:
+            cp(half("sb%d" % rd, 0), ind(b("Y", 0, NV), b("BXL")))
+
     def send(rd):
-        cp(b("sb%d" % rd, 0, 128), ind(b("Y", 0, NV), b("BXL")))
-        act(b("sb%d" % rd, 128, 256), ind(b("Z", 0, NV), b("BZL")))
         groups = {}
         for d in (1, 2, 3):
             dst = T.cores[(rank - d) % N]
@@ -223,129 +243,127 @@ def rank_program(g, core, T, topo):
         due["arr%d" % rd] = sum(len(engines_to(T.cores[(rank + d) % N], core)) for d in (1, 2, 3))
         note("G", [], [("st%d" % rd, 0, 768)], "arr%d" % rd, due["arr%d" % rd], {})
 
+    border(0, 0)
+    border(0, 1)
     send(0)
-    g.sync.wait_ge(T.sem["sent0"], due["sent0"])
-    dma("Y", "dx", b("X", 0, NV), ext(T.x[:, :]))
     for n in ("nzt", "nbt", "mrep", "imrep", "X"):
         iota(b(n, NV, NW), [[0, NW - NV]], 0, 0, n[0] != "n")
-    cp(b("imch"), b("imc"))
+    g.sync.wait_ge(T.sem["sent0"], due["sent0"])
+    dma("Y", "dx", b("X", 0, NV), ext(T.x[:, :]))
+    spread("imch", 0)
     for k in range(4):
-        act(b("mrep", 512 * k, 512 * k + 512), b("k%d" % (4 + k)))
-    for t in range(16):
-        mm(b("k%d" % (t // 4), t % 4 * 128, t % 4 * 128 + 128), b("LT", 128 * t, 128 * t + 128), b("imch"))
-    ts(b("segh"), b("rowT"), 0.0, None, A.is_gt)
-    ts(b("segm"), b("rowT", 0, 128), 0.0, None, A.is_gt)
+        (act, cp)[k % 2](ch("mrep", k), b("k%d" % (4 + k)))
+    act(b("segh", 0, 128), b("rowT"), F.Sign)
+    cp(b("VU"), b("vl"))
     cp(b("L15"), b("l15i"))
-    cp(b("bc"), b("bci"))
-    fill(b("cbig", 0, 8), -BIG)
-    fill(b("ones"), 1.0)
-    fill(b("onesh"), 0.0625)
-    for h in range(4):
-        ts(b("BOg", 128 * h, 128 * h + 128), b("onesh"), b("ind", 2 * h + 1, 2 * h + 2), None, A.mult)
-    ts(b("dc1"), b("ipf"), 2.0, float(NW), A.mult, A.add)
-    ts(b("dc2"), b("ipf"), 2.0, float(NW + 256), A.mult, A.add)
-    for k in range(4):
-        ts(b("RD", 8 * k, 8 * k + 8), b("rowc", 8 * k, 8 * k + 8), b("pg"), b("dc%d" % (1 + k % 2)), A.is_equal, A.mult)
-    cp(b("RD", 32, 40), b("ind"))
-    ts(b("pm16"), b("pm"), 16.0, None, A.mult)
-    ts(b("vl"), b("vl"), b("pm16"), None, A.add)
-    ts(b("nvi"), b("vl"), 5.0, 1.0, A.mult, A.add)
-    ts(b("nvi"), b("nvi"), 2047, None, A.bitwise_and)
-    cp(b("nv5"), b("nvi"))
-    fill(b("thh"), -BIG)
-
-    def half(n, k):
-        return b(n, 128 * k, 128 * k + 128)
-
-    def ch(n, c, m=1):
-        return b(n, 512 * c, 512 * (c + m))
-
-    def lst(n, c, m=1):
-        return b(n, 32 * c, 32 * (c + m))
-
-    def every16(n, base=15, cnt=8):
-        return b(n, base, base + 16 * cnt - 15, 16)
+    for k in range(2):
+        act(ch("imrep", k), b("k%d" % k))
+    act(b("Ib"), b("If"))
+    act(b("cK"), b("rowT"), F.Copy, -0.5)
+    for n, c in (("bi16", 16.0), ("bi32", 32.0), ("bn16", -16.0)):
+        act(b(n, 0, 8), b("ind", 0, 8), F.Copy, c)
+    act(b("segm"), b("rowT"), F.Sign)
 
     Yw, Zw, Xw = b("Y", 0, NW), b("Z", 0, NW), b("X", 0, NW)
     Mw, Iw, NBw, NZw = b("mrep", 0, NW), b("imrep", 0, NW), b("nbt"), b("nzt")
 
-    def names(rd):
-        if rd == 0:
-            tt(half("WPm", 0), b("mrep", 0, NV, 16), half("diag", 0), A.mult)
-        else:
-            tt(half("WPm", 0), ind(b("mrep", 0, NV), b("VU")), half("diag", 0), A.mult)
+    def names(between):
+        tt(half("WPm", 0), ind(b("mrep", 0, NV), b("VU")), b("diag"), A.mult)
+        between[0]()
         scan(half("WPs", 0), half("segh", 0), half("WPm", 0), A.mult, A.add)
-        if rd == 1:
-            cp(b("nal"), ind(b("nbt", 0, NV), b("VU")))
+        between[1]()
         cp(b("MVL"), every16("WPs"))
+        between[2]()
         cp(b("nql"), ind(b("nzt", 0, NV), b("MVL")))
-        if rd == 0:
-            cp(b("nal"), b("nbt", 0, NV, 16))
-        cp(b("nqf"), b("nql"))
-        cp(b("naf"), b("nal"))
+        act(b("nqf"), ind(b("nzt", 0, NV), b("MVL")))
 
-    for k in range(4):
-        act(b("imrep", 512 * k, 512 * k + 512), b("k%d" % k))
-    names(0)
+    def own_list():
+        cp(b("nal"), ind(b("nbt", 0, NV), b("VU")))
+        act(b("naf"), ind(b("nbt", 0, NV), b("VU")))
+
+    names([lambda: (ts(b("nvi"), b("vl"), 5.0, 1.0, A.mult, A.add), cp(b("bc"), b("bci")), tt(b("RD", 0, 32), b("ind"), b("dcv"), A.mult)),
+           lambda: ts(b("nvi"), b("nvi"), 2047, None, A.bitwise_and),
+           lambda: cp(b("nv5"), b("nvi"))])
+    own_list()
+
+    def later_constants():
+        for k in (2, 3):
+            act(ch("imrep", k), b("k%d" % k))
+        act(b("segh", 128, 256), b("rowT"), F.Sign)
+        act(b("ind16"), b("ind", 0, 8), F.Copy, 0.0625)
+        act(b("i16"), b("ind", 0, 8), F.Copy, 0.0625)
+        act(b("thh"), b("ones", 0, 1), F.Copy, -BIG)
+        act(b("cbig", 0, 8), b("ones", 0, 8), F.Copy, -BIG)
+
+    def last_constants():
+        for h in range(4):
+            act(half("BOg", h), b("ones"), F.Copy, b("i16", 2 * h + 1, 2 * h + 2))
+        act(b("nIb"), b("If"), F.Copy, -1.0)
+        for n, c in (("bip", 1.0), ("bim", -1.0), ("bpen", -BIG / 16)):
+            act(b(n, 0, 8), b("ind", 0, 8), F.Copy, c)
+        act(b("RD", 32, 40), b("ind", 0, 8))
+        act(b("wt"), b("wj"), F.Copy, 0.9 * RATIO)
+
     for rd in range(ROUNDS):
         last = rd == ROUNDS - 1
         st = "st%d" % rd
         cp((T["Z"][:, NV:NW], [("Z", NV, NW)]), (T[st][:, :, 128:256], [(st, 0, 768)]))
         cp((T["Y"][:, NV:NW], [("Y", NV, NW)]), (T[st][:, :, 0:128], [(st, 0, 768)]))
+        mm(b("k0", 0, 128), b("Ib"), b("cK"), True, False)
         mm(b("k1", 0, 128), b("nqf"), b("If"))
         mm(b("k1", 128, 256), b("naf"), b("If"))
-        mm(b("k0", 0, 128), b("Ib"), b("cK"), True, False)
 
         def dsum(n, c, coef):
             for k in range(16):
                 mm(part("k0", 32 * c, 32 * c + 32, k, 128, 16), b(n, 512 * c + k, 512 * c + 512, 16), b(coef, 0, 8), False, False)
 
         ZQ, DF, AD = "R3", "R4", "R2"
-        act(b(ZQ, 0, 320), ind(Zw, b("nql", 0, 20)))
-        cp(b(ZQ, 320, 512), ind(Zw, b("nql", 20, 32)))
+        act(b(ZQ, 0, 256), ind(Zw, b("nql", 0, 16)))
+        cp(b(ZQ, 256, 512), ind(Zw, b("nql", 16, 32)))
         for c in range(4):
             if c < 3:
                 act(ch(ZQ, c + 1), ind(Zw, lst("nql", c + 1)))
             tt(ch(DF, c), ind(Yw, lst("nal", c)), ch(ZQ, c), A.subtract)
         for c in (0, 1):
             act(ch(AD, c), ch(DF, c), F.Abs)
-        dsum(DF, 2, "bn16")
-        dsum(AD, 0, "bi16")
-        dsum(DF, 3, "bn16")
-        for c in (3, 2):
+        for c in (2, 3):
             ts(ch(AD, c), ch(DF, c), 0.0, None, A.max)
-        dsum(AD, 3, "bi32")
-        dsum(AD, 1, "bi16")
-        dsum(AD, 2, "bi32")
+        for n, c, coef in ((DF, 2, "bn16"), (AD, 0, "bi16"), (DF, 3, "bn16"), (AD, 1, "bi16"), (AD, 2, "bi32"), (AD, 3, "bi32")):
+            dsum(n, c, coef)
         mm(b("k0", 0, 128), b("Ib"), b("cK"), False, True)
-        scan(b("MX"), half("segm", 0), b("k0", 0, 128), A.mult, A.max)
-        tt(b("FL"), b("k0", 0, 128), b("MX"), A.is_equal)
-        act(b("NF"), b("FL"), F.Identity, -1.0, 1.0)
+        if rd == 0:
+            later_constants()
+            last_constants()
+        scan(b("MX"), b("segm"), b("k0", 0, 128), A.mult, A.max)
+        tt(b("FG"), b("k0", 0, 128), b("MX"), A.is_equal)
+        tt(b("NF"), b("k0", 0, 128), b("MX"), A.not_equal)
         for e in (0, 1):
-            tt(half("FP", e), b("FL"), b("k1", 128 * e, 128 * e + 128), A.mult)
-        for e, kb in ((0, "k2"), (1, "k4")):
+            tt(half("FP", e), b("FG"), half("k1", e), A.mult)
+        for e in (0, 1):
             scan(half("SC", e), b("NF"), half("FP", e), A.mult, A.add)
-            tt(half("E", e), ind(half("SC", e), b("L15", 0, 8)), half("diag", 0), A.mult)
-            mm(b(kb, 0, 8), half("E", e), b("ind"))
+        for e, kb in ((0, "k5"), (1, "k4")):
+            tt(half("E", e), ind(half("SC", e), b("L15", 0, 8)), b("diag"), A.mult)
+            mm(b(kb, 0, 8), half("E", e), b("ind", 0, 8))
         act(b("E2"), ind(b("SC"), b("L15")))
-        cp(b("UL", 16, 24), b("k2", 0, 8))
-        cp(b("LBp"), ind(NZw, b("UL", 16, 24)))
+        cp(b("UL", 16, 24), b("k5", 0, 8))
         cp(b("UL", 0, 8), b("k4", 0, 8))
+        cp(b("LBp"), ind(NZw, b("UL", 16, 24)))
         mm(b("k3", 0, 128), half("E2", 1), b("If"))
         mm(b("k3", 128, 256), half("E2", 0), b("If"))
         act(ch("Bp", 0), ind(Zw, lst("LBp", 0)))
+        tt(half("WPm", 1), ind(Mw, b("UL", 0, 8)), b("diag"), A.mult)
+        tt(half("WPm", 0), ind(Iw, b("UL", 16, 24)), b("diag"), A.mult)
         cp(b("LA"), ind(NBw, b("UL", 0, 8)))
-        tt(half("WPm", 1), ind(Mw, b("UL", 0, 8)), half("diag", 1), A.mult)
-        tt(half("WPm", 0), ind(Iw, b("UL", 16, 24)), half("diag", 0), A.mult)
         scan(b("WPs"), b("segh"), b("WPm"), A.mult, A.add)
-        act(half("RW", 1), ind(Iw, b("UL", 16, 24)))
-        act(half("RW", 0), b("k3", 0, 128))
+        ts(b("thr"), every16("MX"), 0.5, b("thh"), A.is_ge, A.mult)
         cp(b("UL", 24, 32), every16("WPs", 143))
         cp(b("UL", 8, 16), every16("WPs"))
+        act(half("RW", 1), ind(Iw, b("UL", 16, 24)))
+        act(half("RW", 0), b("k3", 0, 128))
 
-        def gsum(n, c, sgn, stop=False):
+        def gsum(n, c, sgn):
             for k in range(16):
-                mm(part("k0", 32 * c, 32 * c + 32, 0, 8), b(n, 512 * c + k, 512 * c + 512, 16), b(sgn, 0, 8), False, stop and k == 15)
+                mm(part("k0", 32 * c, 32 * c + 32, 0, 8), b(n, 512 * c + k, 512 * c + 512, 16), b(sgn, 0, 8), False, False)
 
         def gall(n, sgn):
             for k in range(16):
@@ -353,13 +371,13 @@ def rank_program(g, core, T, topo):
 
         def shifted(n, c, kb):
             mm(b(kb), b("Ib"), ch("Bp", c), True, False)
-            mm(b(kb), b("Ib"), ch(n, c), False, False)
-            mm(b(kb), b("nIb"), ch("Bb", c), False, True)
+            mm(b(kb), b("nIb"), ch("Bb", c), False, False)
+            mm(b(kb), b("Ib"), ch(n, c), False, True)
 
         def rows(h):
             kb = "k%d" % (1 + 2 * h)
             for e in (0, 1):
-                mm(b(kb, 256 * e, 256 * e + 256), b("BOg", 128 * (2 * h + e), 128 * (2 * h + e + 1)), b("RW", 0, 256))
+                mm(b(kb, 256 * e, 256 * e + 256), half("BOg", 2 * h + e), b("RW", 0, 256))
 
         def place(gg):
             return 256 * (gg // 2 + 4 * (gg % 2))
@@ -369,94 +387,109 @@ def rank_program(g, core, T, topo):
                 col = b("SC", 128 + 16 * gg + 15, 128 + 16 * gg + 16) if s == 0 else b("WS", gg, gg + 1)
                 ts(b("EQ", (2 * gg + s) * 256, (2 * gg + s) * 256 + 256), b("RR", place(gg), place(gg) + 256), col, b("wj"), A.is_equal, A.mult)
 
+        def first(c):
+            tt(ch("D1", c), ind(Yw, lst("LA", c)), ch("Bp", c), A.subtract)
+            mm(b("k%d" % (4 + c)), b("Ib"), ch("Bp", c), True, False)
+            mm(b("k%d" % (4 + c)), b("Ib"), ch("D1", c), False, False)
+
         for h in range(4):
             o, i = b("RR", 256 * h, 256 * h + 256), part("RW", 32 * h, 32 * h + 1, 0, 256)
             op("G", lambda: g.partition_broadcast(o[0], i[0], 128), i[1], o[1])
         mm(b("k2", 0, 8), half("RW", 1), b("ind16"))
+        mm(b("k0", 0, 8), b("Ib"), b("cbig", 0, 8), True, False)
         act(ch("Bp", 1), ind(Zw, lst("LBp", 1)))
         act(half("RW", 2), b("k3", 128, 256))
         act(ch("Bp", 2), ind(Zw, lst("LBp", 2)))
         act(b("WS"), b("k2", 0, 8))
         act(ch("Bp", 3), ind(Zw, lst("LBp", 3)))
+        first(0)
         rows(0)
         rows(1)
-        tt(ch("D1", 0), ind(Yw, lst("LA", 0)), ch("Bp", 0), A.subtract)
         cp(b("LB"), ind(NZw, b("UL", 24, 32)))
-        tt(ch("D1", 1), ind(Yw, lst("LA", 1)), ch("Bp", 1), A.subtract)
-        cp(b("LAp"), ind(NBw, b("UL", 8, 16)))
+        first(1)
         ts(half("GF", 0), half("RW", 0), float(NV), None, A.is_ge)
-        tt(ch("D1", 2), ind(Yw, lst("LA", 2)), ch("Bp", 2), A.subtract)
+        cp(b("LAp"), ind(NBw, b("UL", 8, 16)))
+        first(2)
         ts(half("GF", 1), half("RW", 2), float(NV), None, A.is_ge)
-        ts(b("thr"), every16("MX"), 0.5, b("thh"), A.is_ge, A.mult)
         cp(b("LST"), b("UL"))
-        tt(ch("D1", 3), ind(Yw, lst("LA", 3)), ch("Bp", 3), A.subtract)
-        mm(b("k0", 0, 8), b("Ib"), b("cbig", 0, 8), True, False)
+        first(3)
         mm(b("k0", 0, 8), half("GF", 0), b("bpen", 0, 8), False, False)
+        second = ("k1", "k3", "k4", "k5")
         for c in range(4):
             act(ch("Bb", c), ind(Zw, lst("LB", c)))
-            shifted("D1", c, "k%d" % (4 + c))
-        ts(b("R1"), b("D1"), 0.0, None, A.max)
-        gall("R1", "bim")
-        for c in range(4):
+            mm(b("k%d" % (4 + c)), b("nIb"), ch("Bb", c), False, True)
             tt(ch("D2", c), ind(Yw, lst("LAp", c)), ch("Bp", c), A.subtract)
-        act(ch("RR", 2), b("k1"))
-        for c in range(4):
-            act(ch("R3", c), b("k%d" % (4 + c)), F.Relu)
-            shifted("D2", c, "k%d" % (4 + c))
             if c == 0:
-                act(ch("RR", 3), b("k3"))
+                ts(b("R1"), b("D1"), 0.0, None, A.max)
+                act(ch("RR", 2), b("k1"))
             if c == 1:
-                act(half("RW", 3), ind(Mw, b("UL", 0, 8)))
+                act(ch("RR", 3), b("k3"))
+                gall("R1", "bim")
             if c == 2:
                 act(b("ZQP"), ind(Zw, b("UL", 16, 32)))
-        ts(b("R2"), b("D2"), 0.0, None, A.max)
-        gall("R3", "bip")
-        gall("R2", "bip")
-        for gg in (0, 2, 4, 6, 1, 3, 5, 7):
-            compare(gg)
+            if c in (2, 3):
+                shifted("D2", c - 2, second[c - 2])
         tt(b("XD"), ind(Xw, b("UL", 0, 16)), b("ZQP"), A.subtract)
-        ts(b("CL"), b("XD"), 1.0, -1.0, A.min, A.max)
+        ts(b("R2"), b("D2"), 0.0, None, A.max)
         for c in range(4):
-            act(ch("R4", c), b("k%d" % (4 + c)), F.Relu)
+            act(ch("R3", c), b("k%d" % (4 + c)), F.Relu)
+            if c < 2:
+                shifted("D2", c + 2, second[c + 2])
+            if c == 2:
+                gall("R2", "bip")
+        gall("R3", "bip")
+        for gg in (0, 2, 4, 6, 1, 3):
+            compare(gg)
+        for c in range(4):
+            act(ch("R4", c), b(second[c]), F.Relu)
             gsum("R4", c, "bim")
         mm(b("k0", 0, 8), half("GF", 1), b("bpen", 0, 8), False, True)
-        if not last:
-            ts(b("own"), b("LST", 16, 24), float(NV), None, A.is_ge)
-            tt(b("ea"), b("LST", 8, 16), b("LST", 0, 8), A.subtract)
-            tt(b("eb"), b("own"), b("nv5"), A.mult)
-            tt(b("ea"), b("ea"), b("eb"), A.add)
+        act(b("CL"), b("XD"), F.Sign)
         tt(b("prop8", 0, 8), b("k0", 0, 8), b("thr"), A.is_gt)
         act(b("pt"), b("prop8", 0, 8), F.Copy, b("wt"))
-        for gg in range(8):
+        act(half("RW", 3), ind(Mw, b("UL", 0, 8)))
+        compare(5)
+        compare(7)
+        for gg in (0, 2, 4, 6, 1, 3, 5, 7):
             for i in range(4):
                 o = (2 * gg + i // 2) * 256 + i % 2 * 128
                 mm(b("k2", gg, gg + 1), b("EQ", o, o + 128), b("prop8", gg, gg + 1), i == 0, i == 3)
+        if not last:
+            ts(b("own"), b("LST", 16, 24), float(NV), None, A.is_ge)
+            tt(b("ea"), b("LST", 8, 16), b("LST", 0, 8), A.subtract)
         tt(b("nc"), b("k2", 0, 8), b("pt"), A.is_ge)
-        tt(b("EC"), ind(b("nc"), b("bc")), half("diag", 0), A.mult)
+        if not last:
+            tt(b("tv"), b("own"), b("nv5"), A.mult)
+        tt(b("EC"), ind(b("nc"), b("bc")), b("diag"), A.mult)
         mm(b("k3", 0, 40), b("EC"), b("RD"))
+        if not last:
+            tt(b("ea"), b("ea"), b("tv"), A.add)
         tt(b("OF"), b("LST"), b("k3", 0, 32), A.max)
 
         def scat(n, o):
             return (T[n][:, 0:DUMP].indirect(T["OF"][:, o:o + 16]), [(n, 0, DUMP), ("OF", o, o + 16)])
 
-        tt(scat("Z", 16), b("CL"), b("ZQP"), A.add)
         if last:
+            tt(scat("Z", 16), b("CL"), b("ZQP"), A.add)
             dma("Y", "dzo", ext(T.zo[:, :]), b("Z", 0, NV))
             cp(scat("mrep", 0), b("RW", 256, 512))
             dma("S", "dmo", ext(T.mo[:, :]), (T["mrep"][0:128:16, 0:NV], [("mrep", 0, NV)]))
             break
-        tt(scat("Y", 0), b("CL"), b("ZQP"), A.add)
-        send(rd + 1)
         tt(b("tv"), b("k3", 32, 40), b("ea"), A.mult)
+        tt(scat("Z", 16), b("CL"), b("ZQP"), A.add)
         tt(b("VU"), b("tv"), b("LST", 0, 8), A.add)
+        tt(scat("Y", 0), b("CL"), b("ZQP"), A.add)
+        border(rd + 1, 1)
+        own_list()
+        border(rd + 1, 0)
+        send(rd + 1)
         mm(b("k2", 0, 8), b("ones"), b("nc"))
         cp(scat("mrep", 0), b("RW", 256, 512))
-        names(1)
         op("V", lambda: g.vector.tensor_reduce(T["cn"][:, :], T["k2"][:, 0:8], AxisListType.X, A.add), [("k2", 0, 8)], [("cn", 0, 1)])
-        ts(b("tha"), b("cn"), -1.0, None, A.mult)
-        ts(b("thb"), b("tha"), 31, None, A.bitwise_and)
+        names([lambda: cp(scat("imrep", 16), b("RW", 0, 256)),
+               lambda: ts(b("tha"), b("cn"), -1.0, None, A.mult),
+               lambda: ts(b("thb"), b("tha"), 31, None, A.bitwise_and)])
         ts(b("thh"), b("thb"), 0.5, -BIG, A.mult, A.add)
-        cp(scat("imrep", 16), b("RW", 0, 256))
     for s in SEMAPHORES:
         if know["G"].get(s, 0) < due[s] and due[s]:
             g.wait_ge(T.sem[s], due[s])

@@ -4,7 +4,6 @@ from concourse.mybir import AluOpType as A, AxisListType, ActivationFunctionType
 
 N, NV, NW, DUMP = 8, 2048, 2432, 2944
 ROUNDS = 2
-BIG = float(2 ** 20)
 RATIO = 3.5
 FL = {}
 
@@ -15,18 +14,18 @@ def _buffers():
         for n in names.split():
             s[n] = ("sbuf", [128, cols], ty)
     add("Z Y", DUMP, "bfloat16"); add("X", NW, "bfloat16")
-    add("mrep imrep", DUMP, "float32"); add("nbt nzt", NW, "int32")
-    add("mc imc", 128, "int32"); add("bxi bzi bci", 8, "int32"); add("l15i", 16, "int32"); add("ip32 pmi pgi odi tha thb", 1, "int32")
-    add("ipf pm pg od ev pm16 thh cn wj wt", 1, "float32")
-    add("rowI rowG rowT diag If MX FG NF ones segm", 128, "float32"); add("FP SC E E2", 256, "float32")
-    add("WPm WPs segh", 256, "float16")
-    add("rowc dcv ind", 32, "float32"); add("RD", 40, "float16"); add("BOg", 512, "float16"); add("dgh", 16, "float16"); add("ind16", 8, "float16")
-    add("BOh mch imch EC", 128, "float16"); add("RW", 512, "float16"); add("LT RR", 2048, "float16")
-    add("Ib nIb cK prop8 bi16 bi32 bn16 bip bim bpen cbig", 128, "bfloat16"); add("GF", 256, "bfloat16")
-    add("vl nv5 own ea WS thr pt nc tv i16", 8, "float32"); add("nvi", 8, "int32"); add("LST", 32, "float32")
-    add("ML nal nql LA LBp LAp LB", 128, "uint16"); add("BXL BZL bc VU MVL", 8, "uint16"); add("L15", 16, "uint16"); add("UL OF", 32, "uint16")
-    add("naf nqf", 128, "float32"); add("Bp Bb D1 D2 R1 R2 R3 R4", 2048, "bfloat16"); add("EQ", 4096, "bfloat16")
+    add("mrep", DUMP, "float32"); add("imrep", DUMP, "int32"); add("nbt nzt", NW, "int32"); add("idt", NW, "float32")
+    add("mc", 128, "int32"); add("mcf", 128, "float32"); add("bxi bzi bci nvi", 8, "int32"); add("ip32 pmi pgi odi lbi tha thb", 1, "int32")
+    add("ipf pm pg od ev pm16 pm640 thh cn", 1, "float32"); add("ln wj wt mid", 2, "float32")
+    add("rowI rowT diag MX FG NF ones segm", 128, "float32"); add("FP SC", 256, "float32"); add("rowc dcv ind LST", 32, "float32")
+    add("vl vn nv5 ea zf fa fq s1 pt nc tv", 8, "float32"); add("WS", 16, "float32")
+    add("naf nqf RW2", 256, "float16"); add("WPm WPs segh SH MLh EC", 128, "float16"); add("SL2", 144, "float16"); add("bxl bxh", 8, "int32"); add("MBL", 8, "uint16")
+    add("RD", 40, "float16"); add("dgh", 16, "float16"); add("ind16", 8, "float16"); add("RW", 512, "float16"); add("RR", 2048, "float16")
+    add("Ib nIb cK c512 prop8 bip bim o128 th8", 128, "bfloat16"); add("SL", 144, "bfloat16")
+    add("ML nal nql LA LBp LAp LB", 128, "uint16"); add("BXL BZL bc VU MVL", 8, "uint16"); add("UL OF", 32, "uint16")
+    add("Bp Bb D1 D2 R1 R2 R3 R4", 2048, "bfloat16"); add("EQ", 4096, "bfloat16")
     add("XD CL ZQP sb0 sb1", 256, "bfloat16")
+    s["md"] = ("dram", [8, NV], "float32")
     s["Lm"] = ("sbuf", [128, 8, 32], "float16")
     for n in ("st0", "st1"):
         s[n] = ("sbuf", [128, 3, 256], "bfloat16")
@@ -36,7 +35,7 @@ def _buffers():
 
 
 SCRATCH = _buffers()
-SEMAPHORES = ["qV", "qS", "qP", "qG", "sent0", "sent1", "arr0", "arr1", "dz", "dmc", "dim", "dbx", "dbz", "dnz", "dnb", "dx", "dzo", "dmo"]
+SEMAPHORES = ["qV", "qS", "qP", "qG", "sent0", "sent1", "arr0", "arr1", "dz", "dmc", "dim", "dmd", "dmr", "dbx", "dbz", "dnz", "dnb", "dx", "dzo", "dmo"]
 
 
 def rank_program(g, core, T, topo):
@@ -81,11 +80,11 @@ def rank_program(g, core, T, topo):
         due["q" + q] += 1
         note(q, reads, writes, "q" + q, due["q" + q], dict(know[q]))
 
-    def dma(q, sem, out, in_):
+    def dma(q, sem, out, in_, total=16):
         order(q, in_[1], out[1])
         eng[q].dma_start(out[0], in_[0]).then_inc(T.sem[sem], 16)
         due[sem] += 16
-        note(q, in_[1], out[1], sem, 16, dict(know[q]))
+        note(q, in_[1], out[1], sem, total, dict(know[q]))
 
     def b(n, lo=0, hi=None, step=1):
         hi = SCRATCH[n][1][1] if hi is None else hi
@@ -112,6 +111,9 @@ def rank_program(g, core, T, topo):
     def ind(win, off):
         return (win[0].indirect(off[0]), win[1] + off[1])
 
+    def scat(n, o):
+        return (T[n][:, 0:DUMP].indirect(T["OF"][:, o:o + 16]), [(n, 0, DUMP), ("OF", o, o + 16)])
+
     def num(s):
         return (s[0], s[1]) if isinstance(s, tuple) else (s, [])
 
@@ -129,6 +131,9 @@ def rank_program(g, core, T, topo):
     def cp(out, in_):
         op("V", lambda: g.vector.tensor_copy(out[0], in_[0]), in_[1] + out[1][1:], out[1][:1])
 
+    def fill(out, c):
+        op("V", lambda: g.vector.memset(out[0], c), [], out[1])
+
     def scan(out, d0, d1, o0, o1):
         op("V", lambda: g.vector.tensor_tensor_scan(out[0], d0[0], d1[0], 0.0, o0, o1), d0[1] + d1[1], out[1])
 
@@ -137,7 +142,8 @@ def rank_program(g, core, T, topo):
         if bias is None:
             op("S", lambda: g.scalar.activation(out[0], in_[0], f, scale=sc), in_[1] + r, out[1])
         else:
-            op("S", lambda: g.scalar.activation(out[0], in_[0], f, bias=bias, scale=sc), in_[1] + r, out[1])
+            bi, r2 = num(bias)
+            op("S", lambda: g.scalar.activation(out[0], in_[0], f, bias=bi, scale=sc), in_[1] + r + r2, out[1])
 
     def mm(out, l, r, start=True, stop=True):
         op("P", lambda: g.tensor.matmul(out[0], l[0], r[0], start, stop), l[1] + r[1], out[1])
@@ -149,66 +155,68 @@ def rank_program(g, core, T, topo):
             op("G", lambda: g.iota(out[0], pat, base, cm), [], out[1])
 
     dma("S", "dmc", b("mc"), ext(T.m[:, :]))
-    dma("Y", "dz", b("Z", 0, NV), ext(T.z[:, :]))
-    dma("S", "dbx", b("bxi"), ext(T.bx[:, :]))
+    dma("Y", "dbx", b("bxi"), ext(T.bx[:, :]))
     dma("S", "dbz", b("bzi"), ext(T.bz[:, :]))
-    dma("Y", "dim", b("imc"), ext(T.im[:, :]))
+    dma("Y", "dz", b("Z", 0, NV), ext(T.z[:, :]))
     dma("Y", "dnz", b("nzt", 0, NV), ext(T.nz[:, :]))
     dma("Y", "dnb", b("nbt", 0, NV), ext(T.nb[:, :]))
 
     iota(b("ip32"), [[0, 1]], 0, 1, False)
     iota(b("rowT"), [[0, 8], [1, 16]], 0, 0)
-    iota(b("rowG"), [[1, 8], [0, 16]], 0, 0)
     iota(b("rowI"), [[1, 128]], 0, 0)
     iota(b("rowc"), [[0, 4], [1, 8]], 0, 0)
     iota(b("vl"), [[256, 8]], 0, 0)
+    iota(b("vn"), [[80, 8]], 1, 0)
     iota(b("ones"), [[0, 128]], 1, 0)
-    iota(b("l15i"), [[16, 16]], 15, 0, False)
     iota(b("bci"), [[1, 8]], 0, 0, False)
     iota(b("dcv"), [[0, 2], [256, 2], [0, 8]], NW, 2)
-    cp(b("ipf"), b("ip32"))
+
+    def no_ghosts(n):
+        iota(b(n, NV, NW), [[0, NW - NV]], 0, 0, n in ("mrep", "X"))
+
+    no_ghosts("nzt")
+    no_ghosts("nbt")
     ts(b("pmi"), b("ip32"), 15, None, A.bitwise_and)
-    ts(b("odi"), b("ip32"), 4, 1, A.arith_shift_right, A.bitwise_and)
+    ts(b("lbi"), b("ip32"), 1, None, A.bitwise_and)
     ts(b("pgi"), b("ip32"), 4, None, A.arith_shift_right)
-    act(b("wj"), b("ipf"), F.Exp, -math.log(RATIO), 63.5 * math.log(RATIO))
+    cp(b("ipf"), b("ip32"))
+    ts(b("pm16"), b("pmi"), 16.0, None, A.mult)
+    ts(b("odi"), b("ip32"), 4, 1, A.arith_shift_right, A.bitwise_and)
+    ts(b("ln", 1, 2), b("lbi"), 127.0, b("ipf"), A.mult, A.add)
+    ts(b("ln", 0, 1), b("pgi"), 2.0, b("pm16"), A.mult, A.add)
+    act(b("wj"), b("ln"), F.Exp, -0.5 * math.log(RATIO), 63.5 * math.log(RATIO))
     cp(b("pm"), b("pmi"))
     cp(b("od"), b("odi"))
     cp(b("pg"), b("pgi"))
-    ts(b("diag"), b("rowT"), b("pm"), None, A.is_equal)
-    ts(b("ev"), b("od"), -1.0, 1.0, A.mult, A.add)
-    ts(b("BOh"), b("rowG"), b("pg"), None, A.is_equal)
     ts(b("dgh"), b("rowT", 0, 16), b("pm"), None, A.is_equal)
-    ts(b("pm16"), b("pm"), 16.0, None, A.mult)
-    ts(b("If"), b("rowI"), b("ipf"), None, A.is_equal)
+    ts(b("ev"), b("od"), -1.0, 1.0, A.mult, A.add)
     ts(b("ind"), b("rowc"), b("pg"), None, A.is_equal)
-    ts(b("vl"), b("vl"), b("pm16"), None, A.add)
-
-    def lt(t0, t1):
-        for t in range(t0, t1):
-            ts(half("LT", t), b("BOh"), b("diag", t, t + 1), None, A.mult)
-
-    def spread(n, k0):
-        for t in range(16):
-            mm(half("k%d" % (k0 + t // 4), t % 4), half("LT", t), b(n))
-
-    for t in range(8, 16):
-        act(half("LT", t), b("BOh"), F.Copy, b("diag", t, t + 1))
-    lt(0, 2)
+    fill(b("SL2"), 0.0)
     for e, k in enumerate(("ev", "od")):
         ts((T["Lm"][:, :, 16 * e:16 * e + 16], [("Lm", e, e + 1)]), b("mc"), b(k), None, A.mult)
     for a in range(4):
         for u in range(8):
             mm(part("k0", 32 * a, 32 * a + 32, u, 128, 8), (T["Lm"][32 * a:32 * a + 32, u, :], [("Lm", 0, 2)]), part("dgh", 32 * a, 32 * a + 32, 0, 16))
-    cp(b("mch"), b("mc"))
-    lt(2, 6)
-    cp(b("ML"), b("k0", 0, 128))
-    lt(6, 8)
-    spread("mch", 4)
-    cp(b("Y", 0, 1024), ind(b("Z", 0, NV), b("ML", 0, 64)))
-    act(b("Y", 1024, 2048), ind(b("Z", 0, NV), b("ML", 64, 128)))
+    act(every16("SL2"), b("ind", 0, 8), F.Copy, 0.0625)
+
+    def as_list(row, o, pick, out):
+        for r in range(16):
+            mm(out, b(pick, 15 - r, 143 - r), b(row, o + r, o + 128, 16), r == 0, r == 15)
+
+    ts(b("bxl"), b("bxi"), 15, None, A.bitwise_and)
+    ts(b("bxh"), b("bxi"), 4, None, A.arith_shift_right)
+    cp(b("VU"), b("bxl"))
+    cp(b("MVL"), b("bxh"))
+    act(b("MX"), b("k0", 0, 128))
+    ts(b("FG"), ind(b("rowI"), b("VU")), b("pm"), None, A.is_equal)
     cp(b("BZL"), b("bzi"))
-    cp(b("BXL"), b("bxi"))
-    cp(b("imch"), b("imc"))
+    tt(b("WPm"), ind(b("MX"), b("MVL")), b("FG"), A.mult)
+    as_list("WPm", 0, "SL2", b("k2", 0, 8))
+    cp(b("ML"), b("MX"))
+    cp(b("mcf"), b("mc"))
+    dma("Y", "dmd", (T["md"][:, :], [("md", 0, NV)]), b("mcf"))
+    ts(b("MBL"), b("k2", 0, 8), 16.0, None, A.mult)
+    ts(b("vl"), b("vl"), b("pm16"), None, A.add)
 
     def engines_to(src, dst):
         e = topo.engines(src, dst)
@@ -222,7 +230,7 @@ def rank_program(g, core, T, topo):
         if k:
             act(half("sb%d" % rd, 1), ind(b("Z", 0, NV), b("BZL")))
         else:
-            cp(half("sb%d" % rd, 0), ind(b("Y", 0, NV), b("BXL")))
+            cp(half("sb%d" % rd, 0), ind(b("Y", 0, NV), b("BXL")) if rd else ind(b("Z", 0, NV), b("MBL")))
 
     def send(rd):
         groups = {}
@@ -246,63 +254,70 @@ def rank_program(g, core, T, topo):
     border(0, 0)
     border(0, 1)
     send(0)
-    for n in ("nzt", "nbt", "mrep", "imrep", "X"):
-        iota(b(n, NV, NW), [[0, NW - NV]], 0, 0, n[0] != "n")
+    no_ghosts("mrep")
+    no_ghosts("imrep")
+    iota(b("idt"), [[1, NW]], 0, 0)
+    no_ghosts("X")
     g.sync.wait_ge(T.sem["sent0"], due["sent0"])
+    for t in range(16):
+        dma("Y", "dim", (T["imrep"][t:128:16, 0:NV], [("imrep", 0, NV)] if t == 15 else []), ext(T.im[:, :]), 256)
+    for t in range(16):
+        dma("Y", "dmr", (T["mrep"][t:128:16, 0:NV], [("mrep", 0, NV)] if t == 15 else []), (T["md"][:, :], [("md", 0, NV)]), 256)
     dma("Y", "dx", b("X", 0, NV), ext(T.x[:, :]))
-    spread("imch", 0)
-    for k in range(4):
-        (act, cp)[k % 2](ch("mrep", k), b("k%d" % (4 + k)))
-    act(b("segh", 0, 128), b("rowT"), F.Sign)
-    cp(b("VU"), b("vl"))
-    cp(b("L15"), b("l15i"))
-    for k in range(2):
-        act(ch("imrep", k), b("k%d" % k))
-    act(b("Ib"), b("If"))
-    act(b("cK"), b("rowT"), F.Copy, -0.5)
-    for n, c in (("bi16", 16.0), ("bi32", 32.0), ("bn16", -16.0)):
-        act(b(n, 0, 8), b("ind", 0, 8), F.Copy, c)
-    act(b("segm"), b("rowT"), F.Sign)
 
-    Yw, Zw, Xw = b("Y", 0, NW), b("Z", 0, NW), b("X", 0, NW)
-    Mw, Iw, NBw, NZw = b("mrep", 0, NW), b("imrep", 0, NW), b("nbt"), b("nzt")
-
-    def names(between):
-        tt(half("WPm", 0), ind(b("mrep", 0, NV), b("VU")), b("diag"), A.mult)
-        between[0]()
-        scan(half("WPs", 0), half("segh", 0), half("WPm", 0), A.mult, A.add)
-        between[1]()
-        cp(b("MVL"), every16("WPs"))
-        between[2]()
-        cp(b("nql"), ind(b("nzt", 0, NV), b("MVL")))
-        act(b("nqf"), ind(b("nzt", 0, NV), b("MVL")))
+    def turned(n, table, off, e):
+        for k, m in enumerate(("ev", "od")):
+            act(half(n, k), ind(b(table, 0, NV), b(off)), F.Identity, b(m), b("mid", k, k + 1))
+        mm(half("k1", e), b("Ib"), b("c512"), True, False)
+        for a in range(4):
+            for c in range(8):
+                o = 128 * e + 16 * c
+                mm(part("k1", 32 * a, 32 * a + 32, o, o + 16), part(n, 32 * a, 32 * a + 32, c, 256, 8), part("dgh", 32 * a, 32 * a + 32, 0, 16), False, False)
+        mm(half("k1", e), b("Ib"), b("c512"), False, True)
 
     def own_list():
         cp(b("nal"), ind(b("nbt", 0, NV), b("VU")))
-        act(b("naf"), ind(b("nbt", 0, NV), b("VU")))
+        turned("naf", "nbt", "VU", 1)
 
-    names([lambda: (ts(b("nvi"), b("vl"), 5.0, 1.0, A.mult, A.add), cp(b("bc"), b("bci")), tt(b("RD", 0, 32), b("ind"), b("dcv"), A.mult)),
-           lambda: ts(b("nvi"), b("nvi"), 2047, None, A.bitwise_and),
-           lambda: cp(b("nv5"), b("nvi"))])
+    def site_list():
+        cp(b("nql"), ind(b("nzt", 0, NV), b("MVL")))
+        turned("nqf", "nzt", "MVL", 0)
+
+    ts(b("diag"), b("rowT"), b("pm"), None, A.is_equal)
+    act(b("Y", 896, 2048), ind(b("Z", 0, NV), b("ML", 56, 128)))
+    cp(b("Y", 0, 896), ind(b("Z", 0, NV), b("ML", 0, 56)))
+    act(b("MLh"), b("MX"), F.Copy, b("diag", 0, 1))
+    as_list("MLh", 0, "SL2", b("k2", 0, 8))
+    cp(b("VU"), b("vl"))
+    ts(b("Ib"), b("rowI"), b("ipf"), None, A.is_equal)
+    fill(b("SL"), 0.0)
+    fill(b("c512"), 512.0)
+    ts(b("pm640"), b("pm"), 640.0, None, A.mult)
+    cp(b("BXL"), b("bxi"))
+    for k, m in enumerate(("ev", "od")):
+        act(b("mid", k, k + 1), b(m), F.Copy, -1024.0)
+    act(b("segh"), b("rowT"), F.Sign)
+    act(b("cK"), b("rowT"), F.Copy, -0.5)
+    act(every16("SL"), b("ind", 0, 8), F.Copy, 16.0)
+    ts(b("MVL"), b("k2", 0, 8), 16.0, None, A.mult)
+    ts(b("nvi"), b("vn"), b("pm640"), None, A.add)
     own_list()
+    site_list()
+    cp(b("bc"), b("bci"))
+    ts(b("nvi"), b("nvi"), 2047, None, A.bitwise_and)
+    tt(b("RD", 0, 32), b("ind"), b("dcv"), A.mult)
+    ts(b("SH"), b("rowI"), 16.0, b("ipf"), A.add, A.is_equal)
+    ts(b("nv5"), b("nvi"), 1.0 / NV, None, A.mult)
+    act(b("segm"), b("rowT"), F.Sign)
+    act(b("nIb"), b("Ib"), F.Copy, -1.0)
+    for n, c in (("ind16", 0.0625), ("bip", 1.0), ("bim", -1.0), ("th8", 0.0)):
+        act(b(n, 0, 8), b("ind", 0, 8), F.Copy, c)
+    act(b("o128"), b("ones"), F.Copy, 1.0 / 128)
+    act(b("RD", 32, 40), b("ind", 0, 8))
+    act(b("wt"), b("wj"), F.Copy, 0.9 * RATIO)
 
-    def later_constants():
-        for k in (2, 3):
-            act(ch("imrep", k), b("k%d" % k))
-        act(b("segh", 128, 256), b("rowT"), F.Sign)
-        act(b("ind16"), b("ind", 0, 8), F.Copy, 0.0625)
-        act(b("i16"), b("ind", 0, 8), F.Copy, 0.0625)
-        act(b("thh"), b("ones", 0, 1), F.Copy, -BIG)
-        act(b("cbig", 0, 8), b("ones", 0, 8), F.Copy, -BIG)
-
-    def last_constants():
-        for h in range(4):
-            act(half("BOg", h), b("ones"), F.Copy, b("i16", 2 * h + 1, 2 * h + 2))
-        act(b("nIb"), b("If"), F.Copy, -1.0)
-        for n, c in (("bip", 1.0), ("bim", -1.0), ("bpen", -BIG / 16)):
-            act(b(n, 0, 8), b("ind", 0, 8), F.Copy, c)
-        act(b("RD", 32, 40), b("ind", 0, 8))
-        act(b("wt"), b("wj"), F.Copy, 0.9 * RATIO)
+    Yw, Zw, Xw = b("Y", 0, NW), b("Z", 0, NW), b("X", 0, NW)
+    Mw, Iw, NBw, NZw = b("mrep", 0, NW), b("imrep", 0, NW), b("nbt"), b("nzt")
 
     for rd in range(ROUNDS):
         last = rd == ROUNDS - 1
@@ -310,12 +325,10 @@ def rank_program(g, core, T, topo):
         cp((T["Z"][:, NV:NW], [("Z", NV, NW)]), (T[st][:, :, 128:256], [(st, 0, 768)]))
         cp((T["Y"][:, NV:NW], [("Y", NV, NW)]), (T[st][:, :, 0:128], [(st, 0, 768)]))
         mm(b("k0", 0, 128), b("Ib"), b("cK"), True, False)
-        mm(b("k1", 0, 128), b("nqf"), b("If"))
-        mm(b("k1", 128, 256), b("naf"), b("If"))
 
-        def dsum(n, c, coef):
-            for k in range(16):
-                mm(part("k0", 32 * c, 32 * c + 32, k, 128, 16), b(n, 512 * c + k, 512 * c + 512, 16), b(coef, 0, 8), False, False)
+        def dsum(n, c):
+            for r in range(4 * c, 4 * c + 4):
+                mm(b("k0", 0, 128), b("SL", 15 - r, 143 - r), half(n, r), False, False)
 
         ZQ, DF, AD = "R3", "R4", "R2"
         act(b(ZQ, 0, 256), ind(Zw, b("nql", 0, 16)))
@@ -324,96 +337,93 @@ def rank_program(g, core, T, topo):
             if c < 3:
                 act(ch(ZQ, c + 1), ind(Zw, lst("nql", c + 1)))
             tt(ch(DF, c), ind(Yw, lst("nal", c)), ch(ZQ, c), A.subtract)
-        for c in (0, 1):
+        for c in (0, 1, 2):
             act(ch(AD, c), ch(DF, c), F.Abs)
-        for c in (2, 3):
-            ts(ch(AD, c), ch(DF, c), 0.0, None, A.max)
-        for n, c, coef in ((DF, 2, "bn16"), (AD, 0, "bi16"), (DF, 3, "bn16"), (AD, 1, "bi16"), (AD, 2, "bi32"), (AD, 3, "bi32")):
-            dsum(n, c, coef)
+        ts(ch(AD, 3), ch(DF, 3), 0.0, -2.0, A.min, A.mult)
+        for n, c in ((AD, 0), (AD, 1), (DF, 3), (AD, 3), (AD, 2)):
+            dsum(n, c)
         mm(b("k0", 0, 128), b("Ib"), b("cK"), False, True)
-        if rd == 0:
-            later_constants()
-            last_constants()
+
+        def ghost_if(out, tmp, val, scale, bias):
+            act(b(tmp), val, F.Sign, scale, bias)
+            act(b(out), b(tmp), F.Relu, float(NV))
+
         scan(b("MX"), b("segm"), b("k0", 0, 128), A.mult, A.max)
         tt(b("FG"), b("k0", 0, 128), b("MX"), A.is_equal)
-        tt(b("NF"), b("k0", 0, 128), b("MX"), A.not_equal)
+        act(b("NF"), b("FG"), F.Identity, -1.0, 1.0)
+        ghost_if("zf", "s1", every16("MX"), -1.0, 0.5)
         for e in (0, 1):
             tt(half("FP", e), b("FG"), half("k1", e), A.mult)
         for e in (0, 1):
             scan(half("SC", e), b("NF"), half("FP", e), A.mult, A.add)
-        for e, kb in ((0, "k5"), (1, "k4")):
-            tt(half("E", e), ind(half("SC", e), b("L15", 0, 8)), b("diag"), A.mult)
-            mm(b(kb, 0, 8), half("E", e), b("ind", 0, 8))
-        act(b("E2"), ind(b("SC"), b("L15")))
-        cp(b("UL", 16, 24), b("k5", 0, 8))
-        cp(b("UL", 0, 8), b("k4", 0, 8))
+        ghost_if("fq", "pt", every16("SC"), 1.0, 0.5 - NV)
+        cp(b("UL", 16, 24), every16("SC"))
+        tt(b("UL", 0, 8), every16("SC", 143), b("zf"), A.max)
         cp(b("LBp"), ind(NZw, b("UL", 16, 24)))
-        mm(b("k3", 0, 128), half("E2", 1), b("If"))
-        mm(b("k3", 128, 256), half("E2", 0), b("If"))
-        act(ch("Bp", 0), ind(Zw, lst("LBp", 0)))
-        tt(half("WPm", 1), ind(Mw, b("UL", 0, 8)), b("diag"), A.mult)
-        tt(half("WPm", 0), ind(Iw, b("UL", 16, 24)), b("diag"), A.mult)
-        cp(b("LA"), ind(NBw, b("UL", 0, 8)))
-        scan(b("WPs"), b("segh"), b("WPm"), A.mult, A.add)
-        ts(b("thr"), every16("MX"), 0.5, b("thh"), A.is_ge, A.mult)
-        cp(b("UL", 24, 32), every16("WPs", 143))
-        cp(b("UL", 8, 16), every16("WPs"))
         act(half("RW", 1), ind(Iw, b("UL", 16, 24)))
-        act(half("RW", 0), b("k3", 0, 128))
+        as_list("RW", 128, "SL2", b("k2", 16, 24))
+        act(ch("Bp", 0), ind(Zw, lst("LBp", 0)))
+        cp(b("LA"), ind(NBw, b("UL", 0, 8)))
+        ts(b("fa"), b("UL", 0, 8), float(NV), float(NV), A.is_ge, A.mult)
+        if not last:
+            tt(b("tv"), b("fq"), b("nv5"), A.mult)
+        tt(b("UL", 8, 16), b("k2", 16, 24), b("fa"), A.max)
+        if not last:
+            tt(b("ea"), b("k2", 16, 24), b("tv"), A.add)
+        cp(b("LAp"), ind(NBw, b("UL", 8, 16)))
+        act(half("RW", 3), ind(Mw, b("UL", 0, 8)))
+        as_list("RW", 384, "SL2", b("k2", 24, 32))
 
         def gsum(n, c, sgn):
             for k in range(16):
                 mm(part("k0", 32 * c, 32 * c + 32, 0, 8), b(n, 512 * c + k, 512 * c + 512, 16), b(sgn, 0, 8), False, False)
 
-        def gall(n, sgn):
+        def gall(n, sgn, start=False):
             for k in range(16):
-                mm(b("k0", 0, 8), b(n, k, 2048, 16), b(sgn, 0, 8), False, False)
+                mm(b("k0", 0, 8), b(n, k, 2048, 16), b(sgn, 0, 8), start and k == 0, False)
 
         def shifted(n, c, kb):
             mm(b(kb), b("Ib"), ch("Bp", c), True, False)
             mm(b(kb), b("nIb"), ch("Bb", c), False, False)
             mm(b(kb), b("Ib"), ch(n, c), False, True)
 
-        def rows(h):
-            kb = "k%d" % (1 + 2 * h)
-            for e in (0, 1):
-                mm(b(kb, 256 * e, 256 * e + 256), half("BOg", 2 * h + e), b("RW", 0, 256))
-
         def place(gg):
             return 256 * (gg // 2 + 4 * (gg % 2))
 
         def compare(gg):
             for s in (0, 1):
-                col = b("SC", 128 + 16 * gg + 15, 128 + 16 * gg + 16) if s == 0 else b("WS", gg, gg + 1)
-                ts(b("EQ", (2 * gg + s) * 256, (2 * gg + s) * 256 + 256), b("RR", place(gg), place(gg) + 256), col, b("wj"), A.is_equal, A.mult)
+                col = b("WS", 8 * s + gg, 8 * s + gg + 1)
+                ts(b("EQ", (2 * gg + s) * 256, (2 * gg + s) * 256 + 256), b("RR", place(gg), place(gg) + 256), col, b("wj", rd, rd + 1), A.is_equal, A.mult)
 
         def first(c):
-            tt(ch("D1", c), ind(Yw, lst("LA", c)), ch("Bp", c), A.subtract)
+            if c:
+                tt(ch("D1", c), ind(Yw, lst("LA", c)), ch("Bp", c), A.subtract)
             mm(b("k%d" % (4 + c)), b("Ib"), ch("Bp", c), True, False)
             mm(b("k%d" % (4 + c)), b("Ib"), ch("D1", c), False, False)
 
-        for h in range(4):
-            o, i = b("RR", 256 * h, 256 * h + 256), part("RW", 32 * h, 32 * h + 1, 0, 256)
-            op("G", lambda: g.partition_broadcast(o[0], i[0], 128), i[1], o[1])
-        mm(b("k2", 0, 8), half("RW", 1), b("ind16"))
-        mm(b("k0", 0, 8), b("Ib"), b("cbig", 0, 8), True, False)
+        def repeat(n, e):
+            for h in range(4):
+                o, i = b("RR", place(2 * h + e), place(2 * h + e) + 256), part(n, 32 * h, 32 * h + 1, 0, 256)
+                op("G", lambda: g.partition_broadcast(o[0], i[0], 128), i[1], o[1])
+
         act(ch("Bp", 1), ind(Zw, lst("LBp", 1)))
-        act(half("RW", 2), b("k3", 128, 256))
+        act(half("RW", 0), ind(b("idt"), b("UL", 0, 8)))
+        repeat("RW", 0)
+        tt(ch("D1", 0), ind(Yw, lst("LA", 0)), ch("Bp", 0), A.subtract)
+        tt(b("UL", 24, 32), b("k2", 24, 32), b("fq"), A.max)
+        mm(b("k1", 0, 256), b("SH"), b("RW", 0, 256))
+        for s in (0, 1):
+            mm(b("k2", 8 * s, 8 * s + 8), half("RW", s), b("ind16"))
         act(ch("Bp", 2), ind(Zw, lst("LBp", 2)))
-        act(b("WS"), b("k2", 0, 8))
         act(ch("Bp", 3), ind(Zw, lst("LBp", 3)))
+        act(b("RW2"), b("k1", 0, 256))
+        act(b("WS"), b("k2", 0, 16))
+        repeat("RW2", 1)
         first(0)
-        rows(0)
-        rows(1)
-        cp(b("LB"), ind(NZw, b("UL", 24, 32)))
         first(1)
-        ts(half("GF", 0), half("RW", 0), float(NV), None, A.is_ge)
-        cp(b("LAp"), ind(NBw, b("UL", 8, 16)))
+        cp(b("LB"), ind(NZw, b("UL", 24, 32)))
         first(2)
-        ts(half("GF", 1), half("RW", 2), float(NV), None, A.is_ge)
-        cp(b("LST"), b("UL"))
         first(3)
-        mm(b("k0", 0, 8), half("GF", 0), b("bpen", 0, 8), False, False)
         second = ("k1", "k3", "k4", "k5")
         for c in range(4):
             act(ch("Bb", c), ind(Zw, lst("LB", c)))
@@ -421,54 +431,47 @@ def rank_program(g, core, T, topo):
             tt(ch("D2", c), ind(Yw, lst("LAp", c)), ch("Bp", c), A.subtract)
             if c == 0:
                 ts(b("R1"), b("D1"), 0.0, None, A.max)
-                act(ch("RR", 2), b("k1"))
             if c == 1:
-                act(ch("RR", 3), b("k3"))
-                gall("R1", "bim")
-            if c == 2:
-                act(b("ZQP"), ind(Zw, b("UL", 16, 32)))
+                gall("R1", "bim", True)
             if c in (2, 3):
                 shifted("D2", c - 2, second[c - 2])
-        tt(b("XD"), ind(Xw, b("UL", 0, 16)), b("ZQP"), A.subtract)
+        compare(0)
         ts(b("R2"), b("D2"), 0.0, None, A.max)
         for c in range(4):
             act(ch("R3", c), b("k%d" % (4 + c)), F.Relu)
             if c < 2:
                 shifted("D2", c + 2, second[c + 2])
-            if c == 2:
-                gall("R2", "bip")
         gall("R3", "bip")
-        for gg in (0, 2, 4, 6, 1, 3):
+        for gg in (2, 4, 6, 1, 3):
             compare(gg)
         for c in range(4):
             act(ch("R4", c), b(second[c]), F.Relu)
             gsum("R4", c, "bim")
-        mm(b("k0", 0, 8), half("GF", 1), b("bpen", 0, 8), False, True)
-        act(b("CL"), b("XD"), F.Sign)
-        tt(b("prop8", 0, 8), b("k0", 0, 8), b("thr"), A.is_gt)
-        act(b("pt"), b("prop8", 0, 8), F.Copy, b("wt"))
-        act(half("RW", 3), ind(Mw, b("UL", 0, 8)))
+            if c == 1:
+                gall("R2", "bip")
+        mm(b("k0", 0, 8), b("o128"), b("th8", 0, 8), False, True)
+        for k in (1, 3):
+            act(b("LST", 8 * k, 8 * k + 8), b("k2", 12 + 4 * k, 20 + 4 * k))
+        act(b("ZQP"), ind(Zw, b("UL", 16, 32)))
+        ts(b("prop8", 0, 8), b("k0", 0, 8), 0.0, None, A.is_gt)
+        act(b("pt"), b("prop8", 0, 8), F.Copy, b("wt", rd, rd + 1))
+        act(b("LST", 0, 8), every16("SC", 143))
+        act(b("LST", 16, 24), every16("SC"))
+        act(half("RW", 2), ind(b("idt"), b("UL", 16, 24)))
         compare(5)
         compare(7)
+        tt(b("XD"), ind(Xw, b("UL", 0, 16)), b("ZQP"), A.subtract)
+        act(b("CL"), b("XD"), F.Sign)
         for gg in (0, 2, 4, 6, 1, 3, 5, 7):
             for i in range(4):
                 o = (2 * gg + i // 2) * 256 + i % 2 * 128
                 mm(b("k2", gg, gg + 1), b("EQ", o, o + 128), b("prop8", gg, gg + 1), i == 0, i == 3)
-        if not last:
-            ts(b("own"), b("LST", 16, 24), float(NV), None, A.is_ge)
-            tt(b("ea"), b("LST", 8, 16), b("LST", 0, 8), A.subtract)
         tt(b("nc"), b("k2", 0, 8), b("pt"), A.is_ge)
-        if not last:
-            tt(b("tv"), b("own"), b("nv5"), A.mult)
         tt(b("EC"), ind(b("nc"), b("bc")), b("diag"), A.mult)
-        mm(b("k3", 0, 40), b("EC"), b("RD"))
         if not last:
-            tt(b("ea"), b("ea"), b("tv"), A.add)
+            tt(b("ea"), b("ea"), b("LST", 0, 8), A.subtract)
+        mm(b("k3", 0, 40), b("EC"), b("RD"))
         tt(b("OF"), b("LST"), b("k3", 0, 32), A.max)
-
-        def scat(n, o):
-            return (T[n][:, 0:DUMP].indirect(T["OF"][:, o:o + 16]), [(n, 0, DUMP), ("OF", o, o + 16)])
-
         if last:
             tt(scat("Z", 16), b("CL"), b("ZQP"), A.add)
             dma("Y", "dzo", ext(T.zo[:, :]), b("Z", 0, NV))
@@ -479,17 +482,22 @@ def rank_program(g, core, T, topo):
         tt(scat("Z", 16), b("CL"), b("ZQP"), A.add)
         tt(b("VU"), b("tv"), b("LST", 0, 8), A.add)
         tt(scat("Y", 0), b("CL"), b("ZQP"), A.add)
+        mm(b("k2", 0, 8), b("ones"), b("nc"))
         border(rd + 1, 1)
         own_list()
         border(rd + 1, 0)
         send(rd + 1)
-        mm(b("k2", 0, 8), b("ones"), b("nc"))
         cp(scat("mrep", 0), b("RW", 256, 512))
         op("V", lambda: g.vector.tensor_reduce(T["cn"][:, :], T["k2"][:, 0:8], AxisListType.X, A.add), [("k2", 0, 8)], [("cn", 0, 1)])
-        names([lambda: cp(scat("imrep", 16), b("RW", 0, 256)),
-               lambda: ts(b("tha"), b("cn"), -1.0, None, A.mult),
-               lambda: ts(b("thb"), b("tha"), 31, None, A.bitwise_and)])
-        ts(b("thh"), b("thb"), 0.5, -BIG, A.mult, A.add)
+        tt(b("WPm"), ind(b("mrep", 0, NV), b("VU")), b("diag"), A.mult)
+        ts(b("tha"), b("cn"), -1.0, None, A.mult)
+        cp(scat("imrep", 16), b("RW", 0, 256))
+        scan(b("WPs"), b("segh"), b("WPm"), A.mult, A.add)
+        ts(b("thb"), b("tha"), 31, None, A.bitwise_and)
+        cp(b("MVL"), every16("WPs"))
+        ts(b("thh"), b("thb"), -0.5, None, A.mult)
+        site_list()
+        act(b("th8", 0, 8), b("ones", 0, 8), F.Copy, b("thh"))
     for s in SEMAPHORES:
         if know["G"].get(s, 0) < due[s] and due[s]:
             g.wait_ge(T.sem[s], due[s])

@@ -2,10 +2,21 @@ import math
 from concourse.bass import DstId, RemoteDMATransfer
 from concourse.mybir import AluOpType as A, AxisListType, ActivationFunctionType as F
 
-N, NV, NW, DUMP = 8, 2048, 2432, 2944
+N, NV, NW = 8, 2048, 2432
+DUMP = 256
+BIG = 4096.0
+HEAD = 896
 ROUNDS = 2
 RATIO = 3.5
-FL = {}
+INTS = "p32i p16i p2i pgi tha thb".split()
+FLOATS = "p32 p16 p2 pg ipf od ev pm40 thh".split()
+SUM, THIRD = 0, 144
+DIFF = ("open zqV02 zqS24 zqS46 zqS68 df02 ab02 df24 ab24 df46 ab46 df67 df78 ab67 mi78 sA06 sD78 sA68 close k0 ",
+        "nq open zqV02 and zqS24 zqS46 zqS68 df02 ab02 df24 ab24 df46 ab46 df67 df78 ab67 mi78 sA06 sD78 sA68 close thr im ")
+NAMES = "mx fg nfS zfS k4 fp sc q a lbp rw rp bp0 la fa fq k1 p w bp1 da0 lb bp2 bp3 own th0 xe0 da1 xe1 lap da2 xe2 da3 xe3 "
+GAIN = ("bb0 dw0 ra04 xa0 bb1 dw1 xa1 xw0 bb2 dw2 xa2 sa04 bb3 dw3 xa3 xw1 eq0 rb04 rc0 xw2 rc1 xw3 rc2 rc3 sc_04 "
+        "eq2 eq4 eq6 eq1 rd0 rd1 rd2 sb04 sd03 rd3 sd34 th1")
+ORDER = tuple(d + NAMES + GAIN for d in DIFF)
 
 
 def _buffers():
@@ -13,29 +24,31 @@ def _buffers():
     def add(names, cols, ty):
         for n in names.split():
             s[n] = ("sbuf", [128, cols], ty)
-    add("Z Y", DUMP, "bfloat16"); add("X", NW, "bfloat16")
-    add("mrep", DUMP, "float32"); add("imrep", DUMP, "int32"); add("nbt nzt", NW, "int32"); add("idt", NW, "float32")
-    add("mc", 128, "int32"); add("mcf", 128, "float32"); add("bxi bzi bci nvi", 8, "int32"); add("ip32 pmi pgi odi lbi tha thb", 1, "int32")
-    add("ipf pm pg od ev pm16 pm640 thh cn", 1, "float32"); add("ln wj wt mid", 2, "float32")
-    add("rowI rowT diag MX FG NF ones segm", 128, "float32"); add("FP SC", 256, "float32"); add("rowc dcv ind LST", 32, "float32")
-    add("vl vn nv5 ea zf fa fq s1 pt nc tv", 8, "float32"); add("WS", 16, "float32")
-    add("naf nqf RW2", 256, "float16"); add("WPm WPs segh SH MLh EC", 128, "float16"); add("SL2", 144, "float16"); add("bxl bxh", 8, "int32"); add("MBL", 8, "uint16")
-    add("RD", 40, "float16"); add("dgh", 16, "float16"); add("ind16", 8, "float16"); add("RW", 512, "float16"); add("RR", 2048, "float16")
-    add("Ib nIb cK c512 prop8 bip bim o128 th8", 128, "bfloat16"); add("SL", 144, "bfloat16")
+    add("Z Y X", NW, "bfloat16"); add("Z1 Y1", DUMP + NW, "bfloat16")
+    add("Tm", DUMP + NW, "float32"); add("Ti", DUMP + NW, "int32"); add("nbt nzt", NW, "int32")
+    add("mc", 128, "int32"); add("mcf", 128, "float32"); add("bxi bzi bci nvi", 8, "int32")
+    add("ci", len(INTS), "int32"); add("cf", len(FLOATS), "float32"); add("cn", 1, "float32"); add("ln wj wt mid", 2, "float32")
+    add("pt com", 8, "float32"); add("prop8 bip bim th8", 8, "bfloat16"); add("RD RDB", 40, "bfloat16")
+    add("rowI rowT diag MX FG NF segm ones", 128, "float32"); add("FP SC", 256, "float32"); add("rowc dcv ind LST", 32, "float32")
+    add("nv5 ea zf fa fq tv alt vn", 8, "float32"); add("WS", 16, "float32")
+    add("naf nqf", 256, "float16"); add("VAL", 512, "float16"); add("WPm", 128, "float16"); add("S0 S1", 130, "float16"); add("PK", 288, "float16"); add("pmul", 3, "int32"); add("bxl bxh", 8, "int32"); add("MBL", 8, "uint16")
+    add("dgh", 16, "float16"); add("ind16", 8, "float16")
+    add("RW RW2", 256, "float16"); add("RR", 2048, "float16")
+    add("Ib nIb cK c512 o128 EC diagh", 128, "bfloat16"); add("SL", 144, "bfloat16")
     add("ML nal nql LA LBp LAp LB", 128, "uint16"); add("BXL BZL bc VU MVL", 8, "uint16"); add("UL OF", 32, "uint16")
     add("Bp Bb D1 D2 R1 R2 R3 R4", 2048, "bfloat16"); add("EQ", 4096, "bfloat16")
-    add("XD CL ZQP sb0 sb1", 256, "bfloat16")
-    s["md"] = ("dram", [8, NV], "float32")
+    add("XG CL ZQP sb0 sb1", 256, "bfloat16")
     s["Lm"] = ("sbuf", [128, 8, 32], "float16")
-    for n in ("st0", "st1"):
-        s[n] = ("sbuf", [128, 3, 256], "bfloat16")
-    for n in range(8):
-        s["k%d" % n] = ("psum", [128, 512], "float32")
+    for n in ("kA", "kB", "kC", "kD"):
+        s[n] = ("psum", [128, 1024], "float32")
     return s
 
 
+BANKS = {"k0": ("kD", 0), "k2": ("kD", 512), "k1": ("kC", 0), "k3": ("kC", 512), "k4": ("kA", 0), "k5": ("kA", 512), "k6": ("kB", 0), "k7": ("kB", 512)}
+
+
 SCRATCH = _buffers()
-SEMAPHORES = ["qV", "qS", "qP", "qG", "sent0", "sent1", "arr0", "arr1", "dz", "dmc", "dim", "dmd", "dmr", "dbx", "dbz", "dnz", "dnb", "dx", "dzo", "dmo"]
+SEMAPHORES = ["qV", "qS", "qP", "qG", "sentA", "sent0", "sentZ", "sentY", "arrA", "arr0", "arrZ", "arrY", "dz1", "dy1", "dr0", "dr1", "dz", "dmc", "dim", "dmr", "dbx", "dbz", "dnz", "dnb", "dx", "dzo", "dzp", "dmo"]
 
 
 def rank_program(g, core, T, topo):
@@ -51,7 +64,7 @@ def rank_program(g, core, T, topo):
         toks = {}
         for w, specs in ((False, reads), (True, writes)):
             for (n, lo, hi) in specs:
-                ps = SCRATCH[n][0] == "psum"
+                ps = n in BANKS
                 for (l2, h2, w2, q2, sem, val, kn) in acc.get(n, []):
                     if ps:
                         if q2 == q and (q == "P" or not (w or w2)): continue
@@ -68,7 +81,7 @@ def rank_program(g, core, T, topo):
         for w, specs in ((False, reads), (True, writes)):
             for (n, lo, hi) in specs:
                 a = acc.setdefault(n, [])
-                if SCRATCH[n][0] == "psum":
+                if n in BANKS:
                     a[:] = [e for e in a if not (e[3] == q and e[2] <= w)]
                 else:
                     a[:] = [e for e in a if not (lo <= e[0] and e[1] <= hi and (w or (e[3] == q and e[4] == sem and not e[2])))]
@@ -80,24 +93,36 @@ def rank_program(g, core, T, topo):
         due["q" + q] += 1
         note(q, reads, writes, "q" + q, due["q" + q], dict(know[q]))
 
-    def dma(q, sem, out, in_, total=16):
+    def dma(q, sem, out, in_, *more):
         order(q, in_[1], out[1])
-        eng[q].dma_start(out[0], in_[0]).then_inc(T.sem[sem], 16)
-        due[sem] += 16
-        note(q, in_[1], out[1], sem, total, dict(know[q]))
+        for o in (out,) + more:
+            eng[q].dma_start(o[0], in_[0]).then_inc(T.sem[sem], 16)
+            due[sem] += 16
+        note(q, in_[1], out[1], sem, due[sem], dict(know[q]))
 
     def b(n, lo=0, hi=None, step=1):
-        hi = SCRATCH[n][1][1] if hi is None else hi
-        return (T[n][:, lo:hi:step] if step != 1 else T[n][:, lo:hi], [(n, lo, hi)])
+        for buf, names in (("ci", INTS), ("cf", FLOATS)):
+            if n in names:
+                return b(buf, names.index(n), names.index(n) + 1)
+        if hi is None:
+            hi = 512 if n in BANKS else SCRATCH[n][1][1]
+        return part(n, 0, 128, lo, hi, step)
 
     def part(n, p0, p1, lo, hi, step=1):
-        return (T[n][p0:p1, lo:hi:step] if step != 1 else T[n][p0:p1, lo:hi], [(n, lo, hi)])
+        t, o = BANKS.get(n, (n, 0))
+        return (T[t][p0:p1, o + lo:o + hi:step] if step != 1 else T[t][p0:p1, o + lo:o + hi], [(n, lo, hi)])
+
+    def banks(n, m):
+        return (T[BANKS[n][0]][:, :], [(n, 0, 512), (m, 0, 512)])
 
     def half(n, k):
         return b(n, 128 * k, 128 * k + 128)
 
     def ch(n, c, m=1):
         return b(n, 512 * c, 512 * (c + m))
+
+    def names(s, lo=0, hi=128, step=1):
+        return b("RW", 128 * s + lo, 128 * s + hi, step)
 
     def lst(n, c, m=1):
         return b(n, 32 * c, 32 * (c + m))
@@ -111,8 +136,15 @@ def rank_program(g, core, T, topo):
     def ind(win, off):
         return (win[0].indirect(off[0]), win[1] + off[1])
 
-    def scat(n, o):
-        return (T[n][:, 0:DUMP].indirect(T["OF"][:, o:o + 16]), [(n, 0, DUMP), ("OF", o, o + 16)])
+    def scat(n, o, k=16):
+        return (T[n][:, 0:DUMP + NV].indirect(T["OF"][:, o:o + k]), [(n, 0, DUMP + NV), ("OF", o, o + k)])
+
+    def tab(n, lo=0, hi=NW):
+        o = SCRATCH[n][1][1] - NW
+        return b(n, o + lo, o + hi)
+
+    def rows(n, k):
+        return (T[n][k:128:16, DUMP:DUMP + NV], [(n, DUMP, DUMP + NV)])
 
     def num(s):
         return (s[0], s[1]) if isinstance(s, tuple) else (s, [])
@@ -154,69 +186,59 @@ def rank_program(g, core, T, topo):
         else:
             op("G", lambda: g.iota(out[0], pat, base, cm), [], out[1])
 
-    dma("S", "dmc", b("mc"), ext(T.m[:, :]))
-    dma("Y", "dbx", b("bxi"), ext(T.bx[:, :]))
-    dma("S", "dbz", b("bzi"), ext(T.bz[:, :]))
+    dma("S", "dbx", b("bxi"), ext(T.bx[:, :]))
+    dma("Y", "dmc", b("mc"), ext(T.m[:, :]))
     dma("Y", "dz", b("Z", 0, NV), ext(T.z[:, :]))
+    dma("S", "dbz", b("bzi"), ext(T.bz[:, :]))
     dma("Y", "dnz", b("nzt", 0, NV), ext(T.nz[:, :]))
     dma("Y", "dnb", b("nbt", 0, NV), ext(T.nb[:, :]))
 
-    iota(b("ip32"), [[0, 1]], 0, 1, False)
-    iota(b("rowT"), [[0, 8], [1, 16]], 0, 0)
-    iota(b("rowI"), [[1, 128]], 0, 0)
-    iota(b("rowc"), [[0, 4], [1, 8]], 0, 0)
-    iota(b("vl"), [[256, 8]], 0, 0)
-    iota(b("vn"), [[80, 8]], 1, 0)
-    iota(b("ones"), [[0, 128]], 1, 0)
-    iota(b("bci"), [[1, 8]], 0, 0, False)
-    iota(b("dcv"), [[0, 2], [256, 2], [0, 8]], NW, 2)
+    def numbers(n, lo, hi):
+        iota(tab(n, lo, hi), [[1, hi - lo]], lo, 0, n == "Tm")
 
     def no_ghosts(n):
-        iota(b(n, NV, NW), [[0, NW - NV]], 0, 0, n in ("mrep", "X"))
+        iota(tab(n, NV, NW), [[0, NW - NV]], 0, 0, n in ("Tm", "X"))
 
-    no_ghosts("nzt")
-    no_ghosts("nbt")
-    ts(b("pmi"), b("ip32"), 15, None, A.bitwise_and)
-    ts(b("lbi"), b("ip32"), 1, None, A.bitwise_and)
-    ts(b("pgi"), b("ip32"), 4, None, A.arith_shift_right)
-    cp(b("ipf"), b("ip32"))
-    ts(b("pm16"), b("pmi"), 16.0, None, A.mult)
-    ts(b("odi"), b("ip32"), 4, 1, A.arith_shift_right, A.bitwise_and)
-    ts(b("ln", 1, 2), b("lbi"), 127.0, b("ipf"), A.mult, A.add)
-    ts(b("ln", 0, 1), b("pgi"), 2.0, b("pm16"), A.mult, A.add)
+    def as_list(row, pick, out):
+        for r in range(16):
+            mm(out, b("PK", pick + 15 - r, pick + 143 - r), row(r), r == 0, r == 15)
+
+    for k, c in enumerate((64, 128, 1024)):
+        iota(b("pmul", k, k + 1), [[0, 1]], 0, c, False)
+    iota(b("ipf"), [[0, 1]], 0, 1)
+    iota(b("rowc"), [[0, 4], [1, 8]], 0, 0)
+    iota(b("rowI"), [[1, 128]], 0, 0)
+    iota(b("rowT"), [[0, 8], [1, 16]], 0, 0)
+    numbers("Ti", 0, HEAD)
+    fill(b("PK"), 0.0)
+    fill(b("SL"), 0.0)
+    ts(b("ci", 0, 3), b("pmul"), 2047, None, A.bitwise_and)
+    ts(b("ci", 3, 4), b("pmul", 1, 2), 11, None, A.arith_shift_right)
+    fill(b("c512"), 512.0)
+    cp(b("cf", 0, 4), b("ci", 0, 4))
+    ts(b("ln", 0, 1), b("p2"), 127.0 / 1024, b("ipf"), A.mult, A.add)
+    ts(b("ln", 1, 2), b("p32"), 1.0 / 8, b("pg"), A.mult, A.add)
     act(b("wj"), b("ln"), F.Exp, -0.5 * math.log(RATIO), 63.5 * math.log(RATIO))
-    cp(b("pm"), b("pmi"))
-    cp(b("od"), b("odi"))
-    cp(b("pg"), b("pgi"))
-    ts(b("dgh"), b("rowT", 0, 16), b("pm"), None, A.is_equal)
-    ts(b("ev"), b("od"), -1.0, 1.0, A.mult, A.add)
     ts(b("ind"), b("rowc"), b("pg"), None, A.is_equal)
-    fill(b("SL2"), 0.0)
+    ts(b("od"), b("p32"), 1024.0, None, A.is_ge)
+    ts(b("ev"), b("p32"), 1024.0, None, A.is_lt)
+    ts(b("dgh"), b("rowI", 0, 16), 128.0, b("p16"), A.mult, A.is_equal)
+    cp(every16("PK"), b("ind", 0, 8))
+    fill(b("nzt", NV, NW), 0)
+    ts(b("bxh"), b("bxi"), 7, None, A.arith_shift_right)
+    ts(b("bxl"), b("bxi"), 127, None, A.bitwise_and)
+    cp(b("VU"), b("bxh"))
+    cp(b("MVL"), b("bxl"))
+    cp(b("BZL"), b("bzi"))
+    ts(b("FG"), ind(b("rowI"), b("VU")), 128.0, b("p16"), A.mult, A.is_equal)
+    tt(b("WPm"), ind(b("mc"), b("MVL")), b("FG"), A.mult)
+    as_list(lambda r: b("WPm", r, 128, 16), SUM, b("k2", 0, 8))
     for e, k in enumerate(("ev", "od")):
         ts((T["Lm"][:, :, 16 * e:16 * e + 16], [("Lm", e, e + 1)]), b("mc"), b(k), None, A.mult)
     for a in range(4):
         for u in range(8):
             mm(part("k0", 32 * a, 32 * a + 32, u, 128, 8), (T["Lm"][32 * a:32 * a + 32, u, :], [("Lm", 0, 2)]), part("dgh", 32 * a, 32 * a + 32, 0, 16))
-    act(every16("SL2"), b("ind", 0, 8), F.Copy, 0.0625)
-
-    def as_list(row, o, pick, out):
-        for r in range(16):
-            mm(out, b(pick, 15 - r, 143 - r), b(row, o + r, o + 128, 16), r == 0, r == 15)
-
-    ts(b("bxl"), b("bxi"), 15, None, A.bitwise_and)
-    ts(b("bxh"), b("bxi"), 4, None, A.arith_shift_right)
-    cp(b("VU"), b("bxl"))
-    cp(b("MVL"), b("bxh"))
-    act(b("MX"), b("k0", 0, 128))
-    ts(b("FG"), ind(b("rowI"), b("VU")), b("pm"), None, A.is_equal)
-    cp(b("BZL"), b("bzi"))
-    tt(b("WPm"), ind(b("MX"), b("MVL")), b("FG"), A.mult)
-    as_list("WPm", 0, "SL2", b("k2", 0, 8))
-    cp(b("ML"), b("MX"))
-    cp(b("mcf"), b("mc"))
-    dma("Y", "dmd", (T["md"][:, :], [("md", 0, NV)]), b("mcf"))
-    ts(b("MBL"), b("k2", 0, 8), 16.0, None, A.mult)
-    ts(b("vl"), b("vl"), b("pm16"), None, A.add)
+    cp(b("MBL"), b("k2", 0, 8))
 
     def engines_to(src, dst):
         e = topo.engines(src, dst)
@@ -226,44 +248,43 @@ def rank_program(g, core, T, topo):
         used = topo.engines(src, far[0])
         return [k for k in e if k not in used]
 
-    def border(rd, k):
-        if k:
-            act(half("sb%d" % rd, 1), ind(b("Z", 0, NV), b("BZL")))
-        else:
-            cp(half("sb%d" % rd, 0), ind(b("Y", 0, NV), b("BXL")) if rd else ind(b("Z", 0, NV), b("MBL")))
-
-    def send(rd):
+    def send(tag, pieces):
         groups = {}
         for d in (1, 2, 3):
             dst = T.cores[(rank - d) % N]
             groups.setdefault(tuple(engines_to(core, dst)), []).append((d, dst))
-        order("G", b("sb%d" % rd)[1], [])
         tr = []
-        for e, ds in groups.items():
-            ids = []
-            for d, dst in ds:
-                rid, pid, _ = topo.addr(dst)
-                ids.append(DstId(rid=rid, pnc=pid))
-            tr.append(RemoteDMATransfer(dst_ids=ids, dma_engine_mask=sum(1 << k for k in e), remote_sem=T.sem["arr%d" % rd],
-                                        srcs=[T["sb%d" % rd][:, :]], dsts=[T["st%d" % rd][:, d - 1, :] for d, _ in ds]))
-            due["sent%d" % rd] += len(e)
-        g.remote_dma_fused(tr, local_sem=T.sem["sent%d" % rd])
-        due["arr%d" % rd] = sum(len(engines_to(T.cores[(rank + d) % N], core)) for d in (1, 2, 3))
-        note("G", [], [("st%d" % rd, 0, 768)], "arr%d" % rd, due["arr%d" % rd], {})
+        for i, (src, n) in enumerate(pieces):
+            order("G", src[1], [])
+            for e, ds in groups.items():
+                ids = []
+                for d, dst in ds:
+                    rid, pid, _ = topo.addr(dst)
+                    ids.append(DstId(rid=rid, pnc=pid))
+                mine = e[i::len(pieces)]
+                tr.append(RemoteDMATransfer(dst_ids=ids, dma_engine_mask=sum(1 << k for k in mine), remote_sem=T.sem["arr" + tag],
+                                            srcs=[src[0]], dsts=[tab(n, NV + 128 * (d - 1), NV + 128 * d)[0] for d, _ in ds]))
+                due["sent" + tag] += len(mine)
+        g.remote_dma_fused(tr, local_sem=T.sem["sent" + tag])
+        due["arr" + tag] = sum(len(engines_to(T.cores[(rank + d) % N], core)) for d in (1, 2, 3))
+        note("G", [], [tab(n, NV, NW)[1][0] for _, n in pieces], "arr" + tag, due["arr" + tag], {})
 
-    border(0, 0)
-    border(0, 1)
-    send(0)
-    no_ghosts("mrep")
-    no_ghosts("imrep")
-    iota(b("idt"), [[1, NW]], 0, 0)
+    act(half("sb0", 1), ind(b("Z", 0, NV), b("BZL")))
+    send("A", [(half("sb0", 1), "Z")])
+    act(tab("Tm", 0, HEAD), tab("Ti", 0, HEAD))
+    cp(half("sb0", 0), ind(b("Z", 0, NV), b("MBL")))
+    send("0", [(half("sb0", 0), "Y")])
+    ts(b("Ib"), b("rowI"), b("ipf"), None, A.is_equal)
+    for k, m in enumerate(("ev", "od")):
+        act(b("mid", k, k + 1), b(m), F.Copy, -1024.0)
+    act(every16("SL"), b("ind", 0, 8), F.Copy, 16.0)
+    numbers("Tm", HEAD, NV)
+    numbers("Ti", HEAD, NV)
+    no_ghosts("Ti")
+    iota(b("dcv"), [[0, 2], [128, 2], [0, 8]], 0, 1)
+    no_ghosts("Tm")
+    iota(b("ones"), [[0, 128]], 1, 0)
     no_ghosts("X")
-    g.sync.wait_ge(T.sem["sent0"], due["sent0"])
-    for t in range(16):
-        dma("Y", "dim", (T["imrep"][t:128:16, 0:NV], [("imrep", 0, NV)] if t == 15 else []), ext(T.im[:, :]), 256)
-    for t in range(16):
-        dma("Y", "dmr", (T["mrep"][t:128:16, 0:NV], [("mrep", 0, NV)] if t == 15 else []), (T["md"][:, :], [("md", 0, NV)]), 256)
-    dma("Y", "dx", b("X", 0, NV), ext(T.x[:, :]))
 
     def turned(n, table, off, e):
         for k, m in enumerate(("ev", "od")):
@@ -275,229 +296,260 @@ def rank_program(g, core, T, topo):
                 mm(part("k1", 32 * a, 32 * a + 32, o, o + 16), part(n, 32 * a, 32 * a + 32, c, 256, 8), part("dgh", 32 * a, 32 * a + 32, 0, 16), False, False)
         mm(half("k1", e), b("Ib"), b("c512"), False, True)
 
-    def own_list():
-        cp(b("nal"), ind(b("nbt", 0, NV), b("VU")))
-        turned("naf", "nbt", "VU", 1)
-
-    def site_list():
-        cp(b("nql"), ind(b("nzt", 0, NV), b("MVL")))
-        turned("nqf", "nzt", "MVL", 0)
-
-    ts(b("diag"), b("rowT"), b("pm"), None, A.is_equal)
-    act(b("Y", 896, 2048), ind(b("Z", 0, NV), b("ML", 56, 128)))
-    cp(b("Y", 0, 896), ind(b("Z", 0, NV), b("ML", 0, 56)))
-    act(b("MLh"), b("MX"), F.Copy, b("diag", 0, 1))
-    as_list("MLh", 0, "SL2", b("k2", 0, 8))
-    cp(b("VU"), b("vl"))
-    ts(b("Ib"), b("rowI"), b("ipf"), None, A.is_equal)
-    fill(b("SL"), 0.0)
-    fill(b("c512"), 512.0)
-    ts(b("pm640"), b("pm"), 640.0, None, A.mult)
-    cp(b("BXL"), b("bxi"))
-    for k, m in enumerate(("ev", "od")):
-        act(b("mid", k, k + 1), b(m), F.Copy, -1024.0)
-    act(b("segh"), b("rowT"), F.Sign)
+    cp(b("ML"), b("k0", 0, 128))
+    cp(b("MVL"), b("mc", 0, 128, 16))
+    act(b("Y", 1056, 2048), ind(b("Z", 0, NV), b("ML", 66, 128)))
+    cp(b("Y", 0, 1056), ind(b("Z", 0, NV), b("ML", 0, 66)))
+    ts(b("VU"), b("rowc", 0, 8), 16.0, b("p16"), A.mult, A.add)
+    cp(b("mcf"), b("mc"))
+    fill(b("nbt", NV, NW), 0)
     act(b("cK"), b("rowT"), F.Copy, -0.5)
-    act(every16("SL"), b("ind", 0, 8), F.Copy, 16.0)
-    ts(b("MVL"), b("k2", 0, 8), 16.0, None, A.mult)
-    ts(b("nvi"), b("vn"), b("pm640"), None, A.add)
-    own_list()
-    site_list()
-    cp(b("bc"), b("bci"))
-    ts(b("nvi"), b("nvi"), 2047, None, A.bitwise_and)
-    tt(b("RD", 0, 32), b("ind"), b("dcv"), A.mult)
-    ts(b("SH"), b("rowI"), 16.0, b("ipf"), A.add, A.is_equal)
-    ts(b("nv5"), b("nvi"), 1.0 / NV, None, A.mult)
+    g.sync.wait_ge(T.sem["sent0"], due["sent0"])
+    dma("Y", "dmr", rows("Tm", 1), b("mcf"), rows("Tm", 2))
+    dma("Y", "dim", rows("Ti", 0), ext(T.im[:, :]), rows("Ti", 2))
+    dma("Y", "dx", b("X", 0, NV), ext(T.x[:, :]))
+    dma("Y", "dz1", tab("Z1", 0, NV), b("Z", 0, NV))
+    dma("Y", "dy1", tab("Y1", 0, NV), b("Y", 0, NV))
+    cp(b("nql"), ind(b("nzt", 0, NV), b("MVL")))
+    turned("nqf", "nzt", "MVL", 0)
     act(b("segm"), b("rowT"), F.Sign)
-    act(b("nIb"), b("Ib"), F.Copy, -1.0)
-    for n, c in (("ind16", 0.0625), ("bip", 1.0), ("bim", -1.0), ("th8", 0.0)):
-        act(b(n, 0, 8), b("ind", 0, 8), F.Copy, c)
-    act(b("o128"), b("ones"), F.Copy, 1.0 / 128)
-    act(b("RD", 32, 40), b("ind", 0, 8))
-    act(b("wt"), b("wj"), F.Copy, 0.9 * RATIO)
+    ts(b("diag"), b("rowT"), 128.0, b("p16"), A.mult, A.is_equal)
+    cp(b("nal"), ind(b("nbt", 0, NV), b("VU")))
+    turned("naf", "nbt", "VU", 1)
 
-    Yw, Zw, Xw = b("Y", 0, NW), b("Z", 0, NW), b("X", 0, NW)
-    Mw, Iw, NBw, NZw = b("mrep", 0, NW), b("imrep", 0, NW), b("nbt"), b("nzt")
+    def constants(k):
+        if k == 0:
+            act(every16("PK", THIRD + 15), b("ind", 0, 8), F.Copy, b("diag", 2, 3))
+            for e in (0, 1):
+                act(b("S%d" % e, 0, 2), b("ind", 0, 2), F.Copy, 0.0)
+            act(b("ind16"), b("ind", 0, 8), F.Copy, b("diag", 0, 1))
+            act(b("nIb"), b("Ib"), F.Copy, -1.0)
+            for n, c in (("th8", 0.0), ("bip", 1.0), ("bim", -1.0)):
+                act(b(n), b("ind", 0, 8), F.Copy, c)
+            ts(b("pm40"), b("p16"), 40.0 / 128, 1.0, A.mult, A.add)
+            cp(b("bc"), b("rowc", 0, 8))
+            ts(b("pm40"), b("p2"), 5080.0 / 1024, b("pm40"), A.mult, A.add)
+            cp(b("BXL"), b("bxi"))
+            ts(b("nvi"), b("rowc", 0, 8), 640.0, b("pm40"), A.mult, A.add)
+        if k == 1:
+            ts(b("nvi"), b("nvi"), 2047, None, A.bitwise_and)
+            tt(b("RD", 0, 32), b("ind"), b("dcv"), A.mult)
+            ts(b("nv5"), b("nvi"), 1.0 / NV, None, A.mult)
+        if k == 4:
+            act(b("o128"), b("rowI"), F.Identity, 0.0, 1.0 / 128)
+            act(b("wt"), b("wj"), F.Copy, 0.9 * RATIO)
+        if k == 3:
+            act(b("diagh"), b("diag"))
+            act(b("RD", 32, 40), b("ind", 0, 8), F.Copy, 0.0)
+            act(b("RDB", 0, 32), b("ind"), F.Copy, BIG)
+            act(b("RDB", 32, 40), b("ind", 0, 8))
+        if k == 2:
+            for e in (0, 1):
+                act(b("S%d" % e, 2, 130), b("Ib"), F.Copy, b("diag", e, e + 1))
+
+    Xw, Mw, Iw, NBw, NZw = tab("X"), tab("Tm"), tab("Ti"), b("nbt"), b("nzt")
 
     for rd in range(ROUNDS):
         last = rd == ROUNDS - 1
-        st = "st%d" % rd
-        cp((T["Z"][:, NV:NW], [("Z", NV, NW)]), (T[st][:, :, 128:256], [(st, 0, 768)]))
-        cp((T["Y"][:, NV:NW], [("Y", NV, NW)]), (T[st][:, :, 0:128], [(st, 0, 768)]))
-        mm(b("k0", 0, 128), b("Ib"), b("cK"), True, False)
+        Yw, Zw = (tab("Y1"), tab("Z1")) if rd else (tab("Y"), tab("Z"))
+        ZQ, DF, AD = "R3", "R4", "R2"
+        KEY = ("k0", "k3")
 
-        def dsum(n, c):
-            for r in range(4 * c, 4 * c + 4):
+        def part256(n, k):
+            return b(n, 256 * k, 256 * k + 256)
+
+        def zq(f, lo, hi):
+            f(b(ZQ, 256 * lo, 256 * hi), ind(Zw, b("nql", 16 * lo, 16 * hi)))
+
+        def df(lo, hi):
+            tt(b(DF, 256 * lo, 256 * hi), ind(Yw, b("nal", 16 * lo, 16 * hi)), b(ZQ, 256 * lo, 256 * hi), A.subtract)
+
+        def edge(start):
+            mm(b("k0", 0, 128), b("Ib"), b("cK"), start, not start)
+
+        def dsum(n, lo, hi):
+            for r in range(2 * lo, 2 * hi):
                 mm(b("k0", 0, 128), b("SL", 15 - r, 143 - r), half(n, r), False, False)
 
-        ZQ, DF, AD = "R3", "R4", "R2"
-        act(b(ZQ, 0, 256), ind(Zw, b("nql", 0, 16)))
-        cp(b(ZQ, 256, 512), ind(Zw, b("nql", 16, 32)))
-        for c in range(4):
-            if c < 3:
-                act(ch(ZQ, c + 1), ind(Zw, lst("nql", c + 1)))
-            tt(ch(DF, c), ind(Yw, lst("nal", c)), ch(ZQ, c), A.subtract)
-        for c in (0, 1, 2):
-            act(ch(AD, c), ch(DF, c), F.Abs)
-        ts(ch(AD, 3), ch(DF, 3), 0.0, -2.0, A.min, A.mult)
-        for n, c in ((AD, 0), (AD, 1), (DF, 3), (AD, 3), (AD, 2)):
-            dsum(n, c)
-        mm(b("k0", 0, 128), b("Ib"), b("cK"), False, True)
+        def ab(lo, hi):
+            act(b(AD, 256 * lo, 256 * hi), b(DF, 256 * lo, 256 * hi), F.Abs)
 
-        def ghost_if(out, tmp, val, scale, bias):
-            act(b(tmp), val, F.Sign, scale, bias)
-            act(b(out), b(tmp), F.Relu, float(NV))
+        def minus(lo, hi):
+            ts(b(AD, 256 * lo, 256 * hi), b(DF, 256 * lo, 256 * hi), 0.0, -2.0, A.min, A.mult)
 
-        scan(b("MX"), b("segm"), b("k0", 0, 128), A.mult, A.max)
-        tt(b("FG"), b("k0", 0, 128), b("MX"), A.is_equal)
-        act(b("NF"), b("FG"), F.Identity, -1.0, 1.0)
-        ghost_if("zf", "s1", every16("MX"), -1.0, 0.5)
-        for e in (0, 1):
-            tt(half("FP", e), b("FG"), half("k1", e), A.mult)
-        for e in (0, 1):
-            scan(half("SC", e), b("NF"), half("FP", e), A.mult, A.add)
-        ghost_if("fq", "pt", every16("SC"), 1.0, 0.5 - NV)
-        cp(b("UL", 16, 24), every16("SC"))
-        tt(b("UL", 0, 8), every16("SC", 143), b("zf"), A.max)
-        cp(b("LBp"), ind(NZw, b("UL", 16, 24)))
-        act(half("RW", 1), ind(Iw, b("UL", 16, 24)))
-        as_list("RW", 128, "SL2", b("k2", 16, 24))
-        act(ch("Bp", 0), ind(Zw, lst("LBp", 0)))
-        cp(b("LA"), ind(NBw, b("UL", 0, 8)))
-        ts(b("fa"), b("UL", 0, 8), float(NV), float(NV), A.is_ge, A.mult)
-        if not last:
-            tt(b("tv"), b("fq"), b("nv5"), A.mult)
-        tt(b("UL", 8, 16), b("k2", 16, 24), b("fa"), A.max)
-        if not last:
-            tt(b("ea"), b("k2", 16, 24), b("tv"), A.add)
-        cp(b("LAp"), ind(NBw, b("UL", 8, 16)))
-        act(half("RW", 3), ind(Mw, b("UL", 0, 8)))
-        as_list("RW", 384, "SL2", b("k2", 24, 32))
+        def find(h, m):
+            lo, hi = 64 * h, 64 * (h + m)
 
-        def gsum(n, c, sgn):
+            def w64(n, e=0):
+                return b(n, 128 * e + lo, 128 * e + hi)
+
+            def ends(n, e=0):
+                return every16(n, 128 * e + lo + 15, 4 * m)
+
+            def ul(k, n="UL"):
+                return b(n, 8 * k + 4 * h, 8 * k + 4 * (h + m))
+
+            def row(s, win, k):
+                act(names(s, lo, hi), ind(win, ul(k)))
+
+            def lists():
+                as_list(lambda r: b("RW", r, 256, 16), THIRD, b("k2", 16, 32))
+
+            def move():
+                dma("Y", "dr%d" % rd, (T["RW2"][0:128:32, :], [("RW2", 0, 256)]), (T["RW"][16:128:32, :], [("RW", 0, 256)]))
+
+            key = b("k0", lo, hi)
+            return {
+                "mx": lambda: scan(w64("MX"), w64("segm"), key, A.mult, A.max),
+                "fg": lambda: tt(w64("FG"), key, w64("MX"), A.is_equal),
+                "nf": lambda: tt(w64("NF"), key, w64("MX"), A.not_equal),
+                "fp": lambda: [tt(w64("FP", e), w64("FG"), w64("k1", e), A.mult) for e in (0, 1)],
+                "sc": lambda: [scan(w64("SC", e), w64("NF"), w64("FP", e), A.mult, A.add) for e in (0, 1)],
+                "zf": lambda: ts(ul(0, "zf"), ends("MX"), 0.5, float(NV), A.is_lt, A.mult),
+                "q": lambda: cp(ul(2), ends("SC")),
+                "a": lambda: tt(ul(0), ends("SC", 1), ul(0, "zf"), A.max),
+                "fa": lambda: ts(ul(0, "fa"), ul(0), float(NV), float(NV), A.is_ge, A.mult),
+                "fq": lambda: ts(ul(0, "fq"), ul(2), float(NV), float(NV), A.is_ge, A.mult),
+                "rw": lambda: row(1, Iw, 2),
+                "rp": lambda: (row(0, Mw, 0), lists(), move(), repeat()),
+                "nfS": lambda: act(w64("NF"), w64("FG"), F.Identity, -1.0, 1.0),
+                "zfS": lambda: (act(b("ea"), ends("MX"), F.Sign, -1.0, 0.5), act(b("zf"), b("ea"), F.Relu, float(NV))),
+                "w": lambda: tt(ul(1), ul(3, "k2"), ul(0, "fa"), A.max),
+                "p": lambda: tt(ul(3), ul(2, "k2"), ul(0, "fq"), A.max),
+                "lbp": lambda: cp(w64("LBp"), ind(NZw, ul(2))),
+                "la": lambda: cp(w64("LA"), ind(NBw, ul(0))),
+                "lap": lambda: cp(w64("LAp"), ind(NBw, ul(1))),
+                "lb": lambda: cp(w64("LB"), ind(NZw, ul(3))),
+            }
+
+        def gsum(n, lo, hi, sgn, start=False):
             for k in range(16):
-                mm(part("k0", 32 * c, 32 * c + 32, 0, 8), b(n, 512 * c + k, 512 * c + 512, 16), b(sgn, 0, 8), False, False)
-
-        def gall(n, sgn, start=False):
-            for k in range(16):
-                mm(b("k0", 0, 8), b(n, k, 2048, 16), b(sgn, 0, 8), start and k == 0, False)
+                mm(part("k0", 32 * lo, 32 * hi, 0, 8), b(n, 512 * lo + k, 512 * hi, 16), b(sgn), start and k == 0, False)
 
         def shifted(n, c, kb):
             mm(b(kb), b("Ib"), ch("Bp", c), True, False)
             mm(b(kb), b("nIb"), ch("Bb", c), False, False)
             mm(b(kb), b("Ib"), ch(n, c), False, True)
 
-        def place(gg):
-            return 256 * (gg // 2 + 4 * (gg % 2))
-
         def compare(gg):
             for s in (0, 1):
                 col = b("WS", 8 * s + gg, 8 * s + gg + 1)
-                ts(b("EQ", (2 * gg + s) * 256, (2 * gg + s) * 256 + 256), b("RR", place(gg), place(gg) + 256), col, b("wj", rd, rd + 1), A.is_equal, A.mult)
+                ts(b("EQ", (2 * gg + s) * 256, (2 * gg + s) * 256 + 256), part256("RR", gg), col, b("wj", rd, rd + 1), A.is_equal, A.mult)
 
-        def first(c):
-            if c:
-                tt(ch("D1", c), ind(Yw, lst("LA", c)), ch("Bp", c), A.subtract)
-            mm(b("k%d" % (4 + c)), b("Ib"), ch("Bp", c), True, False)
-            mm(b("k%d" % (4 + c)), b("Ib"), ch("D1", c), False, False)
-
-        def repeat(n, e):
-            for h in range(4):
-                o, i = b("RR", place(2 * h + e), place(2 * h + e) + 256), part(n, 32 * h, 32 * h + 1, 0, 256)
+        def repeat():
+            for gg in (0, 2, 4, 6, 1, 3, 5, 7):
+                o, i = part256("RR", gg), part("RW2" if gg % 2 else "RW", 32 * (gg // 2), 32 * (gg // 2) + 1, 0, 256)
                 op("G", lambda: g.partition_broadcast(o[0], i[0], 128), i[1], o[1])
 
-        act(ch("Bp", 1), ind(Zw, lst("LBp", 1)))
-        act(half("RW", 0), ind(b("idt"), b("UL", 0, 8)))
-        repeat("RW", 0)
-        tt(ch("D1", 0), ind(Yw, lst("LA", 0)), ch("Bp", 0), A.subtract)
-        tt(b("UL", 24, 32), b("k2", 24, 32), b("fq"), A.max)
-        mm(b("k1", 0, 256), b("SH"), b("RW", 0, 256))
-        for s in (0, 1):
-            mm(b("k2", 8 * s, 8 * s + 8), half("RW", s), b("ind16"))
-        act(ch("Bp", 2), ind(Zw, lst("LBp", 2)))
-        act(ch("Bp", 3), ind(Zw, lst("LBp", 3)))
-        act(b("RW2"), b("k1", 0, 256))
-        act(b("WS"), b("k2", 0, 16))
-        repeat("RW2", 1)
-        first(0)
-        first(1)
-        cp(b("LB"), ind(NZw, b("UL", 24, 32)))
-        first(2)
-        first(3)
-        second = ("k1", "k3", "k4", "k5")
-        for c in range(4):
-            act(ch("Bb", c), ind(Zw, lst("LB", c)))
-            mm(b("k%d" % (4 + c)), b("nIb"), ch("Bb", c), False, True)
-            tt(ch("D2", c), ind(Yw, lst("LAp", c)), ch("Bp", c), A.subtract)
-            if c == 0:
-                ts(b("R1"), b("D1"), 0.0, None, A.max)
-            if c == 1:
-                gall("R1", "bim", True)
-            if c in (2, 3):
-                shifted("D2", c - 2, second[c - 2])
-        compare(0)
-        ts(b("R2"), b("D2"), 0.0, None, A.max)
-        for c in range(4):
-            act(ch("R3", c), b("k%d" % (4 + c)), F.Relu)
-            if c < 2:
-                shifted("D2", c + 2, second[c + 2])
-        gall("R3", "bip")
-        for gg in (2, 4, 6, 1, 3):
-            compare(gg)
-        for c in range(4):
-            act(ch("R4", c), b(second[c]), F.Relu)
-            gsum("R4", c, "bim")
-            if c == 1:
-                gall("R2", "bip")
-        mm(b("k0", 0, 8), b("o128"), b("th8", 0, 8), False, True)
-        for k in (1, 3):
-            act(b("LST", 8 * k, 8 * k + 8), b("k2", 12 + 4 * k, 20 + 4 * k))
+        def own(f=act):
+            for s in (0, 1):
+                mm(b("k2", 8 * s, 8 * s + 8), names(s), b("ind16"))
+            f(b("WS"), b("k2", 0, 16))
+
+        def threshold():
+            if rd:
+                ts(b("thh"), b("thb"), -0.25, None, A.mult)
+                act(b("th8"), b("ones", 0, 8), F.Copy, b("thh"))
+
+        def early(c):
+            mm(b(X1[c]), b("Ib"), ch("Bp", c), True, False)
+            mm(b(X1[c]), b("Ib"), ch("D1", c), False, False)
+
+        X1, X2 = ("k4", "k5", "k6", "k7"), ("k1", "k3", "k4", "k5")
+        steps = {
+            "zqS": lambda lo, hi: zq(act, lo, hi), "zqV": lambda lo, hi: zq(cp, lo, hi), "df": df, "ab": ab, "mi": minus,
+            "open": lambda: edge(True), "close": lambda: edge(False),
+            "sA": lambda lo, hi: dsum(AD, lo, hi), "sD": lambda lo, hi: dsum(DF, lo, hi),
+            "k": lambda k: rd == 0 and constants(k),
+            "bp": lambda c, m=1: act(ch("Bp", c, m), ind(Zw, lst("LBp", c, m))),
+            "bb": lambda c, m=1: act(ch("Bb", c, m), ind(Zw, lst("LB", c, m))),
+            "rC": lambda c: act(ch("R3", c, 2), banks(X1[c], X1[c + 1]), F.Relu),
+            "rD": lambda c: act(ch("R4", c, 2), banks(X2[c], X2[c + 1]), F.Relu),
+            "nq": lambda: turned("nqf", "nzt", "MVL", 0),
+            "da": lambda c: tt(ch("D1", c), ind(Yw, lst("LA", c)), ch("Bp", c), A.subtract),
+            "dw": lambda c: tt(ch("D2", c), ind(Yw, lst("LAp", c)), ch("Bp", c), A.subtract),
+            "xe": early, "xa": lambda c: mm(b(X1[c]), b("nIb"), ch("Bb", c), False, True), "xw": lambda c: shifted("D2", c, X2[c]),
+            "ra": lambda lo, hi: ts(ch("R1", lo, hi - lo), ch("D1", lo, hi - lo), 0.0, None, A.max),
+            "rb": lambda lo, hi: ts(ch("R2", lo, hi - lo), ch("D2", lo, hi - lo), 0.0, None, A.max),
+            "rc": lambda c: act(ch("R3", c), b(X1[c]), F.Relu), "rd": lambda c: act(ch("R4", c), b(X2[c]), F.Relu),
+            "sa": lambda lo, hi: gsum("R1", lo, hi, "bim"), "sb": lambda lo, hi: gsum("R2", lo, hi, "bip"),
+            "sc_": lambda lo, hi: gsum("R3", lo, hi, "bip"), "sd": lambda lo, hi: gsum("R4", lo, hi, "bim"),
+            "th": lambda k: mm(b("k0", 0, 8), b("o128"), b("th8"), k == 0, k == 1),
+            "eq": compare, "own": own, "thr": threshold,
+            "im": lambda: rd and cp(scat("Ti", 24, 8), half("VAL", 3)),
+            "and": lambda: ts(b("thb"), b("tha"), 31, None, A.bitwise_and),
+        }
+        steps["rS"] = lambda c: act(ch("R2", c), ch("D2", c), F.Relu)
+        steps.update(find(0, 2))
+        for word in ORDER[rd].split():
+            name = word.rstrip("0123456789")
+            steps[name](*[int(x) for x in word[len(name):]])
+        ia, iw = (8, 0) if last else (0, 8)
+        for out, val in ((iw, b("k2", 24, 32)), (24, b("k2", 16, 24))):
+            act(b("LST", out, out + 8), val, F.Identity, 1.0, float(DUMP))
         act(b("ZQP"), ind(Zw, b("UL", 16, 32)))
-        ts(b("prop8", 0, 8), b("k0", 0, 8), 0.0, None, A.is_gt)
-        act(b("pt"), b("prop8", 0, 8), F.Copy, b("wt", rd, rd + 1))
-        act(b("LST", 0, 8), every16("SC", 143))
-        act(b("LST", 16, 24), every16("SC"))
-        act(half("RW", 2), ind(b("idt"), b("UL", 16, 24)))
-        compare(5)
-        compare(7)
-        tt(b("XD"), ind(Xw, b("UL", 0, 16)), b("ZQP"), A.subtract)
-        act(b("CL"), b("XD"), F.Sign)
+        ts(b("prop8"), b("k0", 0, 8), 0.0, None, A.is_gt)
+        act(b("pt"), b("prop8"), F.Copy, b("wt", rd, rd + 1))
+        act(b("XG"), ind(Xw, b("UL", 0, 16)))
+        for out, val in ((ia, every16("SC", 143)), (16, every16("SC"))):
+            act(b("LST", out, out + 8), val, F.Identity, 1.0, float(DUMP))
+        for gg in (3, 5, 7):
+            compare(gg)
         for gg in (0, 2, 4, 6, 1, 3, 5, 7):
             for i in range(4):
                 o = (2 * gg + i // 2) * 256 + i % 2 * 128
                 mm(b("k2", gg, gg + 1), b("EQ", o, o + 128), b("prop8", gg, gg + 1), i == 0, i == 3)
-        tt(b("nc"), b("k2", 0, 8), b("pt"), A.is_ge)
-        tt(b("EC"), ind(b("nc"), b("bc")), b("diag"), A.mult)
+        mm(b("k4", 0, 256), b("Ib"), b("XG"), True, False)
+        mm(b("k4", 0, 256), b("nIb"), b("ZQP"), False, True)
         if not last:
-            tt(b("ea"), b("ea"), b("LST", 0, 8), A.subtract)
-        mm(b("k3", 0, 40), b("EC"), b("RD"))
-        tt(b("OF"), b("LST"), b("k3", 0, 32), A.max)
+            constants(3)
+        mm(b("k3", 0, 40), b("diagh"), b("RD"), True, False)
+        act(b("CL"), b("k4", 0, 256), F.Sign)
+        if not last:
+            tt(b("tv"), b("fq"), b("nv5"), A.mult)
+            ts(b("alt"), b("LST", 8, 16), float(DUMP), None, A.subtract)
+        tt(b("com"), b("k2", 0, 8), b("pt"), A.is_lt)
+        if not last:
+            tt(b("alt"), b("alt"), b("tv"), A.add)
+        tt(b("EC"), ind(b("com"), b("bc")), b("diag"), A.mult)
+        if not last:
+            tt(b("ea"), every16("SC", 143), b("alt"), A.subtract)
+        mm(b("k3", 0, 40), b("EC"), b("RDB"), False, True)
+        tt(b("OF"), b("LST"), b("k3", 0, 32), A.min)
         if last:
-            tt(scat("Z", 16), b("CL"), b("ZQP"), A.add)
-            dma("Y", "dzo", ext(T.zo[:, :]), b("Z", 0, NV))
-            cp(scat("mrep", 0), b("RW", 256, 512))
-            dma("S", "dmo", ext(T.mo[:, :]), (T["mrep"][0:128:16, 0:NV], [("mrep", 0, NV)]))
+            tt(scat("Z1", 16), b("CL"), b("ZQP"), A.add)
+            for q, sem, p in (("Y", "dzo", 0), ("S", "dzp", 64)):
+                dma(q, sem, ext(T.zo[p:p + 64, :]), part("Z1", p, p + 64, DUMP, DUMP + NV))
+            cp(scat("Tm", 0), b("RW"))
+            dma("Y", "dmo", ext(T.mo[:, :]), rows("Tm", 1))
             break
+        constants(2)
+        for t in (0, 1):
+            for k in (0, 1):
+                out = half("k1", 2 * t + k)
+                mm(out, b("S0", 2, 130), names(k), True, False)
+                mm(out, b("S1", 2, 130), names(1 - k), False, False)
+                mm(out, b("S0", 0, 128) if t else b("S1", 1, 129), names(k if t else 1 - k), False, True)
         tt(b("tv"), b("k3", 32, 40), b("ea"), A.mult)
-        tt(scat("Z", 16), b("CL"), b("ZQP"), A.add)
-        tt(b("VU"), b("tv"), b("LST", 0, 8), A.add)
-        tt(scat("Y", 0), b("CL"), b("ZQP"), A.add)
-        mm(b("k2", 0, 8), b("ones"), b("nc"))
-        border(rd + 1, 1)
-        own_list()
-        border(rd + 1, 0)
-        send(rd + 1)
-        cp(scat("mrep", 0), b("RW", 256, 512))
-        op("V", lambda: g.vector.tensor_reduce(T["cn"][:, :], T["k2"][:, 0:8], AxisListType.X, A.add), [("k2", 0, 8)], [("cn", 0, 1)])
-        tt(b("WPm"), ind(b("mrep", 0, NV), b("VU")), b("diag"), A.mult)
-        ts(b("tha"), b("cn"), -1.0, None, A.mult)
-        cp(scat("imrep", 16), b("RW", 0, 256))
-        scan(b("WPs"), b("segh"), b("WPm"), A.mult, A.add)
-        ts(b("thb"), b("tha"), 31, None, A.bitwise_and)
-        cp(b("MVL"), every16("WPs"))
-        ts(b("thh"), b("thb"), -0.5, None, A.mult)
-        site_list()
-        act(b("th8", 0, 8), b("ones", 0, 8), F.Copy, b("thh"))
+        tt(scat("Z1", 16), b("CL"), b("ZQP"), A.add)
+        tt(scat("Y1", 0), b("CL"), b("ZQP"), A.add)
+        tt(b("VU"), b("tv"), b("alt"), A.add)
+        mm(b("k2", 0, 8), b("ones"), b("com"))
+        for tag, n, k, off in (("Z", "Z1", 1, "BZL"), ("Y", "Y1", 0, "BXL")):
+            act(half("sb1", k), ind(tab(n, 0, NV), b(off)))
+            send(tag, [(half("sb1", k), n)])
+            if k:
+                act(b("VAL"), b("k1"))
+        cp(scat("Tm", 0), part256("VAL", 0))
+        turned("naf", "nbt", "VU", 1)
+        act(b("WPm"), ind(tab("Tm", 0, NV), b("VU")))
+        cp(b("nal"), ind(b("nbt", 0, NV), b("VU")))
+        as_list(lambda r: b("WPm", r, 128, 16), THIRD, b("k3", 0, 8))
+        cp(scat("Ti", 16, 8), half("VAL", 2))
+        op("V", lambda: g.vector.tensor_reduce(T["cn"][:, :], b("k2", 0, 8)[0], AxisListType.X, A.add), [("k2", 0, 8)], [("cn", 0, 1)])
+        cp(b("MVL"), b("k3", 0, 8))
+        cp(b("tha"), b("cn"))
+        cp(b("nql"), ind(b("nzt", 0, NV), b("MVL")))
     for s in SEMAPHORES:
         if know["G"].get(s, 0) < due[s] and due[s]:
             g.wait_ge(T.sem[s], due[s])

import math
from concourse.bass import DstId, RemoteDMATransfer
from concourse.mybir import AluOpType as A, AxisListType, ActivationFunctionType as F

N, NV, NW = 8, 2048, 2432
DUMP = 256
BIG = 4096.0
HEAD = 896
ROUNDS = 2
RATIO = 3.5
INTS = "p32i p16i p2i pgi tha thb".split()
FLOATS = "p32 p16 p2 pg ipf od ev pm40 thh".split()
SUM, THIRD = 0, 144
DIFF = ("open zqV02 zqS24 zqS46 zqS68 df02 ab02 df24 ab24 df46 ab46 df67 df78 ab67 mi78 sA06 sD78 sA68 close k0 ",
        "nq open zqV02 and zqS24 zqS46 zqS68 df02 ab02 df24 ab24 df46 ab46 df67 df78 ab67 mi78 sA06 sD78 sA68 close thr im ")
NAMES = "mx fg nfS zfS k4 fp sc q a lbp rw rp bp0 la fa fq k1 p w bp1 da0 lb bp2 bp3 own th0 xe0 da1 xe1 lap da2 xe2 da3 xe3 "
GAIN = ("bb0 dw0 ra04 xa0 bb1 dw1 xa1 xw0 bb2 dw2 xa2 sa04 bb3 dw3 xa3 xw1 eq0 rb04 rc0 xw2 rc1 xw3 rc2 rc3 sc_04 "
        "eq2 eq4 eq6 eq1 rd0 rd1 rd2 sb04 sd03 rd3 sd34 th1")
ORDER = tuple(d + NAMES + GAIN for d in DIFF)


def _buffers():
    s = {}
    def add(names, cols, ty):
        for n in names.split():
            s[n] = ("sbuf", [128, cols], ty)
    add("Z Y X", NW, "bfloat16"); add("Z1 Y1", DUMP + NW, "bfloat16")
    add("Tm", DUMP + NW, "float32"); add("Ti", DUMP + NW, "int32"); add("nbt nzt", NW, "int32")
    add("mc", 128, "int32"); add("mcf", 128, "float32"); add("bxi bzi bci nvi", 8, "int32")
    add("ci", len(INTS), "int32"); add("cf", len(FLOATS), "float32"); add("cn", 1, "float32"); add("ln wj wt mid", 2, "float32")
    add("pt com", 8, "float32"); add("prop8 bip bim th8", 8, "bfloat16"); add("RD RDB", 40, "bfloat16")
    add("rowI rowT diag MX FG NF segm ones", 128, "float32"); add("FP SC", 256, "float32"); add("rowc dcv ind LST", 32, "float32")
    add("nv5 ea zf fa fq tv alt vn", 8, "float32"); add("WS", 16, "float32")
    add("naf nqf", 256, "float16"); add("VAL", 512, "float16"); add("WPm", 128, "float16"); add("S0 S1", 130, "float16"); add("PK", 288, "float16"); add("pmul", 3, "int32"); add("bxl bxh", 8, "int32"); add("MBL", 8, "uint16")
    add("dgh", 16, "float16"); add("ind16", 8, "float16")
    add("RW RW2", 256, "float16"); add("RR", 2048, "float16")
    add("Ib nIb cK c512 o128 EC diagh", 128, "bfloat16"); add("SL", 144, "bfloat16")
    add("ML nal nql LA LBp LAp LB", 128, "uint16"); add("BXL BZL bc VU MVL", 8, "uint16"); add("UL OF", 32, "uint16")
    add("Bp Bb D1 D2 R1 R2 R3 R4", 2048, "bfloat16"); add("EQ", 4096, "bfloat16")
    add("XG CL ZQP sb0 sb1", 256, "bfloat16")
    s["Lm"] = ("sbuf", [128, 8, 32], "float16")
    for n in ("kA", "kB", "kC", "kD"):
        s[n] = ("psum", [128, 1024], "float32")
    return s


BANKS = {"k0": ("kD", 0), "k2": ("kD", 512), "k1": ("kC", 0), "k3": ("kC", 512), "k4": ("kA", 0), "k5": ("kA", 512), "k6": ("kB", 0), "k7": ("kB", 512)}


SCRATCH = _buffers()
SEMAPHORES = ["qV", "qS", "qP", "qG", "sentA", "sent0", "sentZ", "sentY", "arrA", "arr0", "arrZ", "arrY", "dz1", "dy1", "dr0", "dr1", "dz", "dmc", "dim", "dmr", "dbx", "dbz", "dnz", "dnb", "dx", "dzo", "dzp", "dmo"]


def rank_program(g, core, T, topo):
    rank = T.rank_of(core)
    if rank is None:
        return
    eng = {"V": g.vector, "S": g.scalar, "P": g.tensor, "G": g, "Y": g.sync}
    due = {n: 0 for n in SEMAPHORES}
    know = {q: {} for q in eng}
    acc = {}

    def order(q, reads, writes):
        toks = {}
        for w, specs in ((False, reads), (True, writes)):
            for (n, lo, hi) in specs:
                ps = n in BANKS
                for (l2, h2, w2, q2, sem, val, kn) in acc.get(n, []):
                    if ps:
                        if q2 == q and (q == "P" or not (w or w2)): continue
                    elif not (w or w2) or lo >= h2 or l2 >= hi:
                        continue
                    if toks.get(sem, (0,))[0] < val: toks[sem] = (val, kn)
        for sem, (val, kn) in sorted(toks.items(), key=lambda t: -sum(t[1][1].values())):
            if know[q].get(sem, 0) < val:
                eng[q].wait_ge(T.sem[sem], val)
                for s2, v2 in list(kn.items()) + [(sem, val)]:
                    if know[q].get(s2, 0) < v2: know[q][s2] = v2

    def note(q, reads, writes, sem, val, kn):
        for w, specs in ((False, reads), (True, writes)):
            for (n, lo, hi) in specs:
                a = acc.setdefault(n, [])
                if n in BANKS:
                    a[:] = [e for e in a if not (e[3] == q and e[2] <= w)]
                else:
                    a[:] = [e for e in a if not (lo <= e[0] and e[1] <= hi and (w or (e[3] == q and e[4] == sem and not e[2])))]
                a.append((lo, hi, w, q, sem, val, kn))

    def op(q, fn, reads, writes):
        order(q, reads, writes)
        fn().then_inc(T.sem["q" + q], 1)
        due["q" + q] += 1
        note(q, reads, writes, "q" + q, due["q" + q], dict(know[q]))

    def dma(q, sem, out, in_, *more):
        order(q, in_[1], out[1])
        for o in (out,) + more:
            eng[q].dma_start(o[0], in_[0]).then_inc(T.sem[sem], 16)
            due[sem] += 16
        note(q, in_[1], out[1], sem, due[sem], dict(know[q]))

    def b(n, lo=0, hi=None, step=1):
        for buf, names in (("ci", INTS), ("cf", FLOATS)):
            if n in names:
                return b(buf, names.index(n), names.index(n) + 1)
        if hi is None:
            hi = 512 if n in BANKS else SCRATCH[n][1][1]
        return part(n, 0, 128, lo, hi, step)

    def part(n, p0, p1, lo, hi, step=1):
        t, o = BANKS.get(n, (n, 0))
        return (T[t][p0:p1, o + lo:o + hi:step] if step != 1 else T[t][p0:p1, o + lo:o + hi], [(n, lo, hi)])

    def banks(n, m):
        return (T[BANKS[n][0]][:, :], [(n, 0, 512), (m, 0, 512)])

    def half(n, k):
        return b(n, 128 * k, 128 * k + 128)

    def ch(n, c, m=1):
        return b(n, 512 * c, 512 * (c + m))

    def names(s, lo=0, hi=128, step=1):
        return b("RW", 128 * s + lo, 128 * s + hi, step)

    def lst(n, c, m=1):
        return b(n, 32 * c, 32 * (c + m))

    def every16(n, base=15, cnt=8):
        return b(n, base, base + 16 * cnt - 15, 16)

    def ext(ap):
        return (ap, [])

    def ind(win, off):
        return (win[0].indirect(off[0]), win[1] + off[1])

    def scat(n, o, k=16):
        return (T[n][:, 0:DUMP + NV].indirect(T["OF"][:, o:o + k]), [(n, 0, DUMP + NV), ("OF", o, o + k)])

    def tab(n, lo=0, hi=NW):
        o = SCRATCH[n][1][1] - NW
        return b(n, o + lo, o + hi)

    def rows(n, k):
        return (T[n][k:128:16, DUMP:DUMP + NV], [(n, DUMP, DUMP + NV)])

    def num(s):
        return (s[0], s[1]) if isinstance(s, tuple) else (s, [])

    def tt(out, in0, in1, o):
        op("V", lambda: g.vector.tensor_tensor(out[0], in0[0], in1[0], o), in0[1] + in1[1] + out[1][1:], out[1][:1])

    def ts(out, in0, s1, s2, o0, o1=None):
        a1, r1 = num(s1)
        a2, r2 = num(s2)
        if o1 is None:
            op("V", lambda: g.vector.tensor_scalar(out[0], in0[0], a1, None, o0), in0[1] + r1, out[1])
        else:
            op("V", lambda: g.vector.tensor_scalar(out[0], in0[0], a1, a2, o0, o1), in0[1] + r1 + r2, out[1])

    def cp(out, in_):
        op("V", lambda: g.vector.tensor_copy(out[0], in_[0]), in_[1] + out[1][1:], out[1][:1])

    def fill(out, c):
        op("V", lambda: g.vector.memset(out[0], c), [], out[1])

    def scan(out, d0, d1, o0, o1):
        op("V", lambda: g.vector.tensor_tensor_scan(out[0], d0[0], d1[0], 0.0, o0, o1), d0[1] + d1[1], out[1])

    def act(out, in_, f=F.Copy, scale=1.0, bias=None):
        sc, r = num(scale)
        if bias is None:
            op("S", lambda: g.scalar.activation(out[0], in_[0], f, scale=sc), in_[1] + r, out[1])
        else:
            bi, r2 = num(bias)
            op("S", lambda: g.scalar.activation(out[0], in_[0], f, bias=bi, scale=sc), in_[1] + r + r2, out[1])

    def mm(out, l, r, start=True, stop=True):
        op("P", lambda: g.tensor.matmul(out[0], l[0], r[0], start, stop), l[1] + r[1], out[1])

    def iota(out, pat, base, cm, f=True):
        if f:
            op("G", lambda: g.iota(out[0], pat, base, cm, allow_small_or_imprecise_dtypes=True), [], out[1])
        else:
            op("G", lambda: g.iota(out[0], pat, base, cm), [], out[1])

    dma("S", "dbx", b("bxi"), ext(T.bx[:, :]))
    dma("Y", "dmc", b("mc"), ext(T.m[:, :]))
    dma("Y", "dz", b("Z", 0, NV), ext(T.z[:, :]))
    dma("S", "dbz", b("bzi"), ext(T.bz[:, :]))
    dma("Y", "dnz", b("nzt", 0, NV), ext(T.nz[:, :]))
    dma("Y", "dnb", b("nbt", 0, NV), ext(T.nb[:, :]))

    def numbers(n, lo, hi):
        iota(tab(n, lo, hi), [[1, hi - lo]], lo, 0, n == "Tm")

    def no_ghosts(n):
        iota(tab(n, NV, NW), [[0, NW - NV]], 0, 0, n in ("Tm", "X"))

    def as_list(row, pick, out):
        for r in range(16):
            mm(out, b("PK", pick + 15 - r, pick + 143 - r), row(r), r == 0, r == 15)

    for k, c in enumerate((64, 128, 1024)):
        iota(b("pmul", k, k + 1), [[0, 1]], 0, c, False)
    iota(b("ipf"), [[0, 1]], 0, 1)
    iota(b("rowc"), [[0, 4], [1, 8]], 0, 0)
    iota(b("rowI"), [[1, 128]], 0, 0)
    iota(b("rowT"), [[0, 8], [1, 16]], 0, 0)
    numbers("Ti", 0, HEAD)
    fill(b("PK"), 0.0)
    fill(b("SL"), 0.0)
    ts(b("ci", 0, 3), b("pmul"), 2047, None, A.bitwise_and)
    ts(b("ci", 3, 4), b("pmul", 1, 2), 11, None, A.arith_shift_right)
    fill(b("c512"), 512.0)
    cp(b("cf", 0, 4), b("ci", 0, 4))
    ts(b("ln", 0, 1), b("p2"), 127.0 / 1024, b("ipf"), A.mult, A.add)
    ts(b("ln", 1, 2), b("p32"), 1.0 / 8, b("pg"), A.mult, A.add)
    act(b("wj"), b("ln"), F.Exp, -0.5 * math.log(RATIO), 63.5 * math.log(RATIO))
    ts(b("ind"), b("rowc"), b("pg"), None, A.is_equal)
    ts(b("od"), b("p32"), 1024.0, None, A.is_ge)
    ts(b("ev"), b("p32"), 1024.0, None, A.is_lt)
    ts(b("dgh"), b("rowI", 0, 16), 128.0, b("p16"), A.mult, A.is_equal)
    cp(every16("PK"), b("ind", 0, 8))
    fill(b("nzt", NV, NW), 0)
    ts(b("bxh"), b("bxi"), 7, None, A.arith_shift_right)
    ts(b("bxl"), b("bxi"), 127, None, A.bitwise_and)
    cp(b("VU"), b("bxh"))
    cp(b("MVL"), b("bxl"))
    cp(b("BZL"), b("bzi"))
    ts(b("FG"), ind(b("rowI"), b("VU")), 128.0, b("p16"), A.mult, A.is_equal)
    tt(b("WPm"), ind(b("mc"), b("MVL")), b("FG"), A.mult)
    as_list(lambda r: b("WPm", r, 128, 16), SUM, b("k2", 0, 8))
    for e, k in enumerate(("ev", "od")):
        ts((T["Lm"][:, :, 16 * e:16 * e + 16], [("Lm", e, e + 1)]), b("mc"), b(k), None, A.mult)
    for a in range(4):
        for u in range(8):
            mm(part("k0", 32 * a, 32 * a + 32, u, 128, 8), (T["Lm"][32 * a:32 * a + 32, u, :], [("Lm", 0, 2)]), part("dgh", 32 * a, 32 * a + 32, 0, 16))
    cp(b("MBL"), b("k2", 0, 8))

    def engines_to(src, dst):
        e = topo.engines(src, dst)
        if topo.chip(src) != topo.chip(dst):
            return e
        far = [c for c in T.cores if topo.chip(c) != topo.chip(src) and topo.may_write(src, c)]
        used = topo.engines(src, far[0])
        return [k for k in e if k not in used]

    def send(tag, pieces):
        groups = {}
        for d in (1, 2, 3):
            dst = T.cores[(rank - d) % N]
            groups.setdefault(tuple(engines_to(core, dst)), []).append((d, dst))
        tr = []
        for i, (src, n) in enumerate(pieces):
            order("G", src[1], [])
            for e, ds in groups.items():
                ids = []
                for d, dst in ds:
                    rid, pid, _ = topo.addr(dst)
                    ids.append(DstId(rid=rid, pnc=pid))
                mine = e[i::len(pieces)]
                tr.append(RemoteDMATransfer(dst_ids=ids, dma_engine_mask=sum(1 << k for k in mine), remote_sem=T.sem["arr" + tag],
                                            srcs=[src[0]], dsts=[tab(n, NV + 128 * (d - 1), NV + 128 * d)[0] for d, _ in ds]))
                due["sent" + tag] += len(mine)
        g.remote_dma_fused(tr, local_sem=T.sem["sent" + tag])
        due["arr" + tag] = sum(len(engines_to(T.cores[(rank + d) % N], core)) for d in (1, 2, 3))
        note("G", [], [tab(n, NV, NW)[1][0] for _, n in pieces], "arr" + tag, due["arr" + tag], {})

    act(half("sb0", 1), ind(b("Z", 0, NV), b("BZL")))
    send("A", [(half("sb0", 1), "Z")])
    act(tab("Tm", 0, HEAD), tab("Ti", 0, HEAD))
    cp(half("sb0", 0), ind(b("Z", 0, NV), b("MBL")))
    send("0", [(half("sb0", 0), "Y")])
    ts(b("Ib"), b("rowI"), b("ipf"), None, A.is_equal)
    for k, m in enumerate(("ev", "od")):
        act(b("mid", k, k + 1), b(m), F.Copy, -1024.0)
    act(every16("SL"), b("ind", 0, 8), F.Copy, 16.0)
    numbers("Tm", HEAD, NV)
    numbers("Ti", HEAD, NV)
    no_ghosts("Ti")
    iota(b("dcv"), [[0, 2], [128, 2], [0, 8]], 0, 1)
    no_ghosts("Tm")
    iota(b("ones"), [[0, 128]], 1, 0)
    no_ghosts("X")

    def turned(n, table, off, e):
        for k, m in enumerate(("ev", "od")):
            act(half(n, k), ind(b(table, 0, NV), b(off)), F.Identity, b(m), b("mid", k, k + 1))
        mm(half("k1", e), b("Ib"), b("c512"), True, False)
        for a in range(4):
            for c in range(8):
                o = 128 * e + 16 * c
                mm(part("k1", 32 * a, 32 * a + 32, o, o + 16), part(n, 32 * a, 32 * a + 32, c, 256, 8), part("dgh", 32 * a, 32 * a + 32, 0, 16), False, False)
        mm(half("k1", e), b("Ib"), b("c512"), False, True)

    cp(b("ML"), b("k0", 0, 128))
    cp(b("MVL"), b("mc", 0, 128, 16))
    act(b("Y", 1056, 2048), ind(b("Z", 0, NV), b("ML", 66, 128)))
    cp(b("Y", 0, 1056), ind(b("Z", 0, NV), b("ML", 0, 66)))
    ts(b("VU"), b("rowc", 0, 8), 16.0, b("p16"), A.mult, A.add)
    cp(b("mcf"), b("mc"))
    fill(b("nbt", NV, NW), 0)
    act(b("cK"), b("rowT"), F.Copy, -0.5)
    g.sync.wait_ge(T.sem["sent0"], due["sent0"])
    dma("Y", "dmr", rows("Tm", 1), b("mcf"), rows("Tm", 2))
    dma("Y", "dim", rows("Ti", 0), ext(T.im[:, :]), rows("Ti", 2))
    dma("Y", "dx", b("X", 0, NV), ext(T.x[:, :]))
    dma("Y", "dz1", tab("Z1", 0, NV), b("Z", 0, NV))
    dma("Y", "dy1", tab("Y1", 0, NV), b("Y", 0, NV))
    cp(b("nql"), ind(b("nzt", 0, NV), b("MVL")))
    turned("nqf", "nzt", "MVL", 0)
    act(b("segm"), b("rowT"), F.Sign)
    ts(b("diag"), b("rowT"), 128.0, b("p16"), A.mult, A.is_equal)
    cp(b("nal"), ind(b("nbt", 0, NV), b("VU")))
    turned("naf", "nbt", "VU", 1)

    def constants(k):
        if k == 0:
            act(every16("PK", THIRD + 15), b("ind", 0, 8), F.Copy, b("diag", 2, 3))
            for e in (0, 1):
                act(b("S%d" % e, 0, 2), b("ind", 0, 2), F.Copy, 0.0)
            act(b("ind16"), b("ind", 0, 8), F.Copy, b("diag", 0, 1))
            act(b("nIb"), b("Ib"), F.Copy, -1.0)
            for n, c in (("th8", 0.0), ("bip", 1.0), ("bim", -1.0)):
                act(b(n), b("ind", 0, 8), F.Copy, c)
            ts(b("pm40"), b("p16"), 40.0 / 128, 1.0, A.mult, A.add)
            cp(b("bc"), b("rowc", 0, 8))
            ts(b("pm40"), b("p2"), 5080.0 / 1024, b("pm40"), A.mult, A.add)
            cp(b("BXL"), b("bxi"))
            ts(b("nvi"), b("rowc", 0, 8), 640.0, b("pm40"), A.mult, A.add)
        if k == 1:
            ts(b("nvi"), b("nvi"), 2047, None, A.bitwise_and)
            tt(b("RD", 0, 32), b("ind"), b("dcv"), A.mult)
            ts(b("nv5"), b("nvi"), 1.0 / NV, None, A.mult)
        if k == 4:
            act(b("o128"), b("rowI"), F.Identity, 0.0, 1.0 / 128)
            act(b("wt"), b("wj"), F.Copy, 0.9 * RATIO)
        if k == 3:
            act(b("diagh"), b("diag"))
            act(b("RD", 32, 40), b("ind", 0, 8), F.Copy, 0.0)
            act(b("RDB", 0, 32), b("ind"), F.Copy, BIG)
            act(b("RDB", 32, 40), b("ind", 0, 8))
        if k == 2:
            for e in (0, 1):
                act(b("S%d" % e, 2, 130), b("Ib"), F.Copy, b("diag", e, e + 1))

    Xw, Mw, Iw, NBw, NZw = tab("X"), tab("Tm"), tab("Ti"), b("nbt"), b("nzt")

    for rd in range(ROUNDS):
        last = rd == ROUNDS - 1
        Yw, Zw = (tab("Y1"), tab("Z1")) if rd else (tab("Y"), tab("Z"))
        ZQ, DF, AD = "R3", "R4", "R2"
        KEY = ("k0", "k3")

        def part256(n, k):
            return b(n, 256 * k, 256 * k + 256)

        def zq(f, lo, hi):
            f(b(ZQ, 256 * lo, 256 * hi), ind(Zw, b("nql", 16 * lo, 16 * hi)))

        def df(lo, hi):
            tt(b(DF, 256 * lo, 256 * hi), ind(Yw, b("nal", 16 * lo, 16 * hi)), b(ZQ, 256 * lo, 256 * hi), A.subtract)

        def edge(start):
            mm(b("k0", 0, 128), b("Ib"), b("cK"), start, not start)

        def dsum(n, lo, hi):
            for r in range(2 * lo, 2 * hi):
                mm(b("k0", 0, 128), b("SL", 15 - r, 143 - r), half(n, r), False, False)

        def ab(lo, hi):
            act(b(AD, 256 * lo, 256 * hi), b(DF, 256 * lo, 256 * hi), F.Abs)

        def minus(lo, hi):
            ts(b(AD, 256 * lo, 256 * hi), b(DF, 256 * lo, 256 * hi), 0.0, -2.0, A.min, A.mult)

        def find(h, m):
            lo, hi = 64 * h, 64 * (h + m)

            def w64(n, e=0):
                return b(n, 128 * e + lo, 128 * e + hi)

            def ends(n, e=0):
                return every16(n, 128 * e + lo + 15, 4 * m)

            def ul(k, n="UL"):
                return b(n, 8 * k + 4 * h, 8 * k + 4 * (h + m))

            def row(s, win, k):
                act(names(s, lo, hi), ind(win, ul(k)))

            def lists():
                as_list(lambda r: b("RW", r, 256, 16), THIRD, b("k2", 16, 32))

            def move():
                dma("Y", "dr%d" % rd, (T["RW2"][0:128:32, :], [("RW2", 0, 256)]), (T["RW"][16:128:32, :], [("RW", 0, 256)]))

            key = b("k0", lo, hi)
            return {
                "mx": lambda: scan(w64("MX"), w64("segm"), key, A.mult, A.max),
                "fg": lambda: tt(w64("FG"), key, w64("MX"), A.is_equal),
                "nf": lambda: tt(w64("NF"), key, w64("MX"), A.not_equal),
                "fp": lambda: [tt(w64("FP", e), w64("FG"), w64("k1", e), A.mult) for e in (0, 1)],
                "sc": lambda: [scan(w64("SC", e), w64("NF"), w64("FP", e), A.mult, A.add) for e in (0, 1)],
                "zf": lambda: ts(ul(0, "zf"), ends("MX"), 0.5, float(NV), A.is_lt, A.mult),
                "q": lambda: cp(ul(2), ends("SC")),
                "a": lambda: tt(ul(0), ends("SC", 1), ul(0, "zf"), A.max),
                "fa": lambda: ts(ul(0, "fa"), ul(0), float(NV), float(NV), A.is_ge, A.mult),
                "fq": lambda: ts(ul(0, "fq"), ul(2), float(NV), float(NV), A.is_ge, A.mult),
                "rw": lambda: row(1, Iw, 2),
                "rp": lambda: (row(0, Mw, 0), lists(), move(), repeat()),
                "nfS": lambda: act(w64("NF"), w64("FG"), F.Identity, -1.0, 1.0),
                "zfS": lambda: (act(b("ea"), ends("MX"), F.Sign, -1.0, 0.5), act(b("zf"), b("ea"), F.Relu, float(NV))),
                "w": lambda: tt(ul(1), ul(3, "k2"), ul(0, "fa"), A.max),
                "p": lambda: tt(ul(3), ul(2, "k2"), ul(0, "fq"), A.max),
                "lbp": lambda: cp(w64("LBp"), ind(NZw, ul(2))),
                "la": lambda: cp(w64("LA"), ind(NBw, ul(0))),
                "lap": lambda: cp(w64("LAp"), ind(NBw, ul(1))),
                "lb": lambda: cp(w64("LB"), ind(NZw, ul(3))),
            }

        def gsum(n, lo, hi, sgn, start=False):
            for k in range(16):
                mm(part("k0", 32 * lo, 32 * hi, 0, 8), b(n, 512 * lo + k, 512 * hi, 16), b(sgn), start and k == 0, False)

        def shifted(n, c, kb):
            mm(b(kb), b("Ib"), ch("Bp", c), True, False)
            mm(b(kb), b("nIb"), ch("Bb", c), False, False)
            mm(b(kb), b("Ib"), ch(n, c), False, True)

        def compare(gg):
            for s in (0, 1):
                col = b("WS", 8 * s + gg, 8 * s + gg + 1)
                ts(b("EQ", (2 * gg + s) * 256, (2 * gg + s) * 256 + 256), part256("RR", gg), col, b("wj", rd, rd + 1), A.is_equal, A.mult)

        def repeat():
            for gg in (0, 2, 4, 6, 1, 3, 5, 7):
                o, i = part256("RR", gg), part("RW2" if gg % 2 else "RW", 32 * (gg // 2), 32 * (gg // 2) + 1, 0, 256)
                op("G", lambda: g.partition_broadcast(o[0], i[0], 128), i[1], o[1])

        def own(f=act):
            for s in (0, 1):
                mm(b("k2", 8 * s, 8 * s + 8), names(s), b("ind16"))
            f(b("WS"), b("k2", 0, 16))

        def threshold():
            if rd:
                ts(b("thh"), b("thb"), -0.25, None, A.mult)
                act(b("th8"), b("ones", 0, 8), F.Copy, b("thh"))

        def early(c):
            mm(b(X1[c]), b("Ib"), ch("Bp", c), True, False)
            mm(b(X1[c]), b("Ib"), ch("D1", c), False, False)

        X1, X2 = ("k4", "k5", "k6", "k7"), ("k1", "k3", "k4", "k5")
        steps = {
            "zqS": lambda lo, hi: zq(act, lo, hi), "zqV": lambda lo, hi: zq(cp, lo, hi), "df": df, "ab": ab, "mi": minus,
            "open": lambda: edge(True), "close": lambda: edge(False),
            "sA": lambda lo, hi: dsum(AD, lo, hi), "sD": lambda lo, hi: dsum(DF, lo, hi),
            "k": lambda k: rd == 0 and constants(k),
            "bp": lambda c, m=1: act(ch("Bp", c, m), ind(Zw, lst("LBp", c, m))),
            "bb": lambda c, m=1: act(ch("Bb", c, m), ind(Zw, lst("LB", c, m))),
            "rC": lambda c: act(ch("R3", c, 2), banks(X1[c], X1[c + 1]), F.Relu),
            "rD": lambda c: act(ch("R4", c, 2), banks(X2[c], X2[c + 1]), F.Relu),
            "nq": lambda: turned("nqf", "nzt", "MVL", 0),
            "da": lambda c: tt(ch("D1", c), ind(Yw, lst("LA", c)), ch("Bp", c), A.subtract),
            "dw": lambda c: tt(ch("D2", c), ind(Yw, lst("LAp", c)), ch("Bp", c), A.subtract),
            "xe": early, "xa": lambda c: mm(b(X1[c]), b("nIb"), ch("Bb", c), False, True), "xw": lambda c: shifted("D2", c, X2[c]),
            "ra": lambda lo, hi: ts(ch("R1", lo, hi - lo), ch("D1", lo, hi - lo), 0.0, None, A.max),
            "rb": lambda lo, hi: ts(ch("R2", lo, hi - lo), ch("D2", lo, hi - lo), 0.0, None, A.max),
            "rc": lambda c: act(ch("R3", c), b(X1[c]), F.Relu), "rd": lambda c: act(ch("R4", c), b(X2[c]), F.Relu),
            "sa": lambda lo, hi: gsum("R1", lo, hi, "bim"), "sb": lambda lo, hi: gsum("R2", lo, hi, "bip"),
            "sc_": lambda lo, hi: gsum("R3", lo, hi, "bip"), "sd": lambda lo, hi: gsum("R4", lo, hi, "bim"),
            "th": lambda k: mm(b("k0", 0, 8), b("o128"), b("th8"), k == 0, k == 1),
            "eq": compare, "own": own, "thr": threshold,
            "im": lambda: rd and cp(scat("Ti", 24, 8), half("VAL", 3)),
            "and": lambda: ts(b("thb"), b("tha"), 31, None, A.bitwise_and),
        }
        steps["rS"] = lambda c: act(ch("R2", c), ch("D2", c), F.Relu)
        steps.update(find(0, 2))
        for word in ORDER[rd].split():
            name = word.rstrip("0123456789")
            steps[name](*[int(x) for x in word[len(name):]])
        ia, iw = (8, 0) if last else (0, 8)
        for out, val in ((iw, b("k2", 24, 32)), (24, b("k2", 16, 24))):
            act(b("LST", out, out + 8), val, F.Identity, 1.0, float(DUMP))
        act(b("ZQP"), ind(Zw, b("UL", 16, 32)))
        ts(b("prop8"), b("k0", 0, 8), 0.0, None, A.is_gt)
        act(b("pt"), b("prop8"), F.Copy, b("wt", rd, rd + 1))
        act(b("XG"), ind(Xw, b("UL", 0, 16)))
        for out, val in ((ia, every16("SC", 143)), (16, every16("SC"))):
            act(b("LST", out, out + 8), val, F.Identity, 1.0, float(DUMP))
        for gg in (3, 5, 7):
            compare(gg)
        for gg in (0, 2, 4, 6, 1, 3, 5, 7):
            for i in range(4):
                o = (2 * gg + i // 2) * 256 + i % 2 * 128
                mm(b("k2", gg, gg + 1), b("EQ", o, o + 128), b("prop8", gg, gg + 1), i == 0, i == 3)
        mm(b("k4", 0, 256), b("Ib"), b("XG"), True, False)
        mm(b("k4", 0, 256), b("nIb"), b("ZQP"), False, True)
        if not last:
            constants(3)
        mm(b("k3", 0, 40), b("diagh"), b("RD"), True, False)
        act(b("CL"), b("k4", 0, 256), F.Sign)
        if not last:
            tt(b("tv"), b("fq"), b("nv5"), A.mult)
            ts(b("alt"), b("LST", 8, 16), float(DUMP), None, A.subtract)
        tt(b("com"), b("k2", 0, 8), b("pt"), A.is_lt)
        if not last:
            tt(b("alt"), b("alt"), b("tv"), A.add)
        tt(b("EC"), ind(b("com"), b("bc")), b("diag"), A.mult)
        if not last:
            tt(b("ea"), every16("SC", 143), b("alt"), A.subtract)
        mm(b("k3", 0, 40), b("EC"), b("RDB"), False, True)
        tt(b("OF"), b("LST"), b("k3", 0, 32), A.min)
        if last:
            tt(scat("Z1", 16), b("CL"), b("ZQP"), A.add)
            for q, sem, p in (("Y", "dzo", 0), ("S", "dzp", 64)):
                dma(q, sem, ext(T.zo[p:p + 64, :]), part("Z1", p, p + 64, DUMP, DUMP + NV))
            cp(scat("Tm", 0), b("RW"))
            dma("Y", "dmo", ext(T.mo[:, :]), rows("Tm", 1))
            break
        constants(2)
        for t in (0, 1):
            for k in (0, 1):
                out = half("k1", 2 * t + k)
                mm(out, b("S0", 2, 130), names(k), True, False)
                mm(out, b("S1", 2, 130), names(1 - k), False, False)
                mm(out, b("S0", 0, 128) if t else b("S1", 1, 129), names(k if t else 1 - k), False, True)
        tt(b("tv"), b("k3", 32, 40), b("ea"), A.mult)
        tt(scat("Z1", 16), b("CL"), b("ZQP"), A.add)
        tt(scat("Y1", 0), b("CL"), b("ZQP"), A.add)
        tt(b("VU"), b("tv"), b("alt"), A.add)
        mm(b("k2", 0, 8), b("ones"), b("com"))
        for tag, n, k, off in (("Z", "Z1", 1, "BZL"), ("Y", "Y1", 0, "BXL")):
            act(half("sb1", k), ind(tab(n, 0, NV), b(off)))
            send(tag, [(half("sb1", k), n)])
            if k:
                act(b("VAL"), b("k1"))
        cp(scat("Tm", 0), part256("VAL", 0))
        turned("naf", "nbt", "VU", 1)
        act(b("WPm"), ind(tab("Tm", 0, NV), b("VU")))
        cp(b("nal"), ind(b("nbt", 0, NV), b("VU")))
        as_list(lambda r: b("WPm", r, 128, 16), THIRD, b("k3", 0, 8))
        cp(scat("Ti", 16, 8), half("VAL", 2))
        op("V", lambda: g.vector.tensor_reduce(T["cn"][:, :], b("k2", 0, 8)[0], AxisListType.X, A.add), [("k2", 0, 8)], [("cn", 0, 1)])
        cp(b("MVL"), b("k3", 0, 8))
        cp(b("tha"), b("cn"))
        cp(b("nql"), ind(b("nzt", 0, NV), b("MVL")))
    for s in SEMAPHORES:
        if know["G"].get(s, 0) < due[s] and due[s]:
            g.wait_ge(T.sem[s], due[s])
